import numpy as np, ml_dtypes
CORES = [9,25,41,57]
N = 4
BF = ml_dtypes.bfloat16
def gentries(a):
    return np.ascontiguousarray(a.reshape(8, 16, -1).transpose(0, 2, 1)).reshape(8, -1)
def gtable(e):
    e = np.asarray(e); return np.ascontiguousarray(e.reshape(8, -1, 16).transpose(0, 2, 1)).reshape(128, -1).astype(np.int32)
W, K, NM, SM, RO = 12288, 1024, 2047, 63, 8
def walks(rng):
    pace = rng.choice(np.array([0.02, 0.1, 0.4, 1.0]), (N, 8, 16, 1))
    x = rng.integers(-3, 4, (N, 8, 16, W)) * (rng.random((N, 8, 16, W), dtype=np.float32) < pace)
    x[..., 0] = rng.integers(-SM, SM + 1, (N, 8, 16))
    return np.abs((np.add.accumulate(x, axis=-1) + SM) % (4 * SM) - 2 * SM) - SM
def spans(rng):
    u = np.exp2(6 + rng.random((8, K)) * (np.log2(NM + 1) - 6)).astype(np.int64)
    return np.clip(np.where(rng.random((8, K)) < 0.5, u, rng.integers(64, NM + 1, (8, K))), 64, NM)
def starts(rng, n, power=1):
    return np.minimum((rng.random((N, 8, K)) ** power * (W - n)).astype(np.int64), W - 1 - n)
def pack(s, lo, n):
    return {"walk": np.ascontiguousarray(s.reshape(N, 128, W)).astype(np.float32).astype(BF), "lo": np.stack([gtable(a) for a in lo]), "span": np.stack([gtable(n)] * N)}
def setup_inputs(rng):
    s = walks(rng); n = spans(rng)
    return pack(s, starts(rng, n), n)
def setup_inputs_ends(rng):
    s = walks(rng); n = rng.choice(np.array([64, 65, 127, 128, NM - 1, NM]), (8, K)); lo = starts(rng, n)
    k = rng.integers(0, 3, (N, 8, K)); lo = np.where(k == 0, 0, np.where(k == 1, W - 1 - n, lo))
    s[:, 0] = SM; s[:, 0, :, 0] = -SM; s[:, 0, :, NM] = -SM; s[:, 0, ::2] = -s[:, 0, ::2]
    n[0, ::2] = NM; lo[:, 0, ::2] = 0; n[0, 1::2] = 64; lo[:, 0, 1::2] = np.minimum(lo[:, 0, 1::2], W - 65)
    s[:, 1] = SM * (2 * rng.integers(0, 2, (N, 16, W)) - 1)
    n[3] = NM; lo[:, 3] = rng.integers(0, W - NM, (N, 1))
    s[:, 2] = SM - rng.integers(0, 2, (N, 16, W))
    s[:, 2, :, :32] *= -1; s[:, 2, :, NM - 31:NM + 1] *= -1
    s[:, 2] *= 2 * rng.integers(0, 2, (N, 16, 1)) - 1
    n[2] = NM - rng.integers(0, 32, K); lo[:, 2] = np.minimum((rng.random((N, K)) * (NM - n[2] + 1)).astype(np.int64), NM - n[2])
    h = NM >> 2; q = int(rng.integers(0, N)); j = int(rng.integers(0, 16)); i = rng.integers(0, 16, N)
    s[:, 4] = SM
    s[q, 4, j] = SM - 1; s[q, 4, j, h - 15:h + 5] = SM - 2; s[q, 4, j, 3 * h - 45:3 * h + 6] = SM
    s[:, 4, :, :4] = -SM; s[:, 4, :, 4 * h - 60:NM + 1] = -SM
    for a in range(N): s[a, 4, int(i[a]), 4 * h - 60:NM + 1] = 1 - SM
    s[:, 4] *= 2 * rng.integers(0, 2, (N, 16, 1)) - 1
    n[4] = 4 * (h - rng.integers(0, 16, K)) + rng.choice(np.array([0, 1, 3]), K); n[4, :3] = 4 * h + np.array([1, 0, 3])
    lo[:, 4] = np.minimum(rng.integers(0, 4, (N, K)), NM - n[4])
    c = rng.integers(-SM, SM + 1, (N, 2, 16)); e = rng.integers(1, SM + 1, (N, 2, 16)); e = np.where(c > 0, c - e, c + e)
    last = rng.integers(NM, W, N); begin = rng.integers(0, W - NM, N); more = spans(rng)
    for a in range(N):
        s[a, 5] = c[a, 0][:, None]; s[a, 5, :, int(last[a])] = e[a, 0]
        s[a, 6] = c[a, 1][:, None]; s[a, 6, :, int(begin[a])] = e[a, 1]
    n[5] = np.where(rng.random(K) < 0.5, NM - rng.integers(0, 63, K), more[5]); n[5, 0] = NM - 30; lo[:, 5] = last[:, None] - n[5]
    n[6] = np.where(rng.random(K) < 0.5, 1024 + 2 * rng.integers(0, 100, K), more[6]); n[6, 0] = 1024; lo[:, 6] = begin[:, None]
    return pack(s, lo, n)
def setup_inputs_ties(rng):
    amp = rng.integers(1, SM + 1, (N, 8, 16, 1)) * (2 * rng.integers(0, 2, (N, 8, 16, 1)) - 1)
    pat = np.repeat(rng.integers(0, 2, (N, 8, 1, W // 64)), 64, axis=-1); n = spans(rng); lo = starts(rng, n)
    pat[:, 1::2] = pat[:1, 1::2].copy(); lo[:, 1::2] = lo[:1, 1::2].copy(); pat[:, 6] = 1
    return pack(amp * pat, lo, n)
def setup_inputs_short(rng):
    s = walks(rng); n = rng.integers(64, 97, (8, K)); lo = starts(rng, n)
    u = np.arange(W) % 64; saw = np.where(u == 0, -SM, SM - (u * SM >> 5)); v = (64 - u) % 64; was = np.where(v == 0, -SM, SM - (v * SM >> 5))
    sg = 2 * rng.integers(0, 2, (N, 16, 1)) - 1
    s[:, 0] = sg * saw; s[:, 4] = sg * was; s[:, 2, ::2] = saw; s[:, 6, 1::2] = was
    n[::2] = 64; lo[:, ::2] = 64 * rng.integers(0, W // 64 - 1, (N, 4, K))
    tail = np.maximum(-SM, SM - 64 + np.arange(66)); tail[0] = -SM; tail[65] = -SM
    s[:, 1, :, W - 66:] = sg * tail; n[1, ::4] = 65; lo[:, 1, ::4] = W - 66
    return pack(s, lo, n)
def setup_inputs_uneven(rng):
    s = walks(rng); n = spans(rng); lo = starts(rng, n); big = rng.integers(0, N, 8); big[0] = 0; big[1] = N - 1
    keep = np.arange(N)[:, None] == big[None, :]
    s = np.where(keep[:, :, None, None], s, np.sign(s))
    one = s[big[5], 5, 3].copy(); s[:, 5] = 0; s[big[5], 5, 3] = one
    k = rng.integers(0, 5, K); n[7] = n[7][k]; lo[:, 7] = lo[:, 7][:, k]
    return pack(s, lo, n)
def setup_inputs_spread(rng):
    z = np.exp2(-rng.integers(0, 6, (N, 8, 1, W)).astype(np.float64)) * (rng.random((N, 8, 1, W)) > 0.0625)
    s = np.rint(SM * z * (2 * rng.random((N, 8, 16, W)) - 1)).astype(np.int64); n = spans(rng)
    return pack(s, starts(rng, n, 4), n)
def check_inputs(d):
    bad = []; s = d["walk"].astype(np.float32); lo = d["lo"].astype(np.int64); n = d["span"].astype(np.int64)
    if not np.all((np.abs(s) <= SM) & (s == np.rint(s))): bad.append("whole numbers of walk")
    if np.min(n) < 64 or np.max(n) > NM: bad.append("range of span")
    if not np.all(n == n[:1]): bad.append("span alike on all ranks")
    if np.min(lo) < 0 or np.max(lo + n) > W - 1: bad.append("range of lo")
    return bad
def reference(walk, lo, span):
    s = walk.astype(np.float32).astype(np.int64).reshape(N, 8, 16, W)
    at = np.stack([gentries(a) for a in lo]).astype(np.int64)
    n = gentries(span[0]).astype(np.int64)
    def pick(q, t):
        return np.take_along_axis(s[q], (at[q] + t)[:, None, :], 2)
    first = [pick(q, 0 * n) for q in range(N)]; rise = [pick(q, n) - first[q] for q in range(N)]
    def gain(t):
        g = np.zeros((8, K), np.int64)
        for q in range(N):
            g = g + np.add.reduce(np.abs(n[:, None, :] * (pick(q, t) - first[q]) - t[:, None, :] * rise[q]), axis=1)
        return g
    l = np.zeros((8, K), np.int64); r = n.copy(); m = n >> 1; gm = gain(m)
    for rnd in range(RO):
        a = r - m; b = m - l; right = a > b
        w = np.where(right, m + (a >> 1), m - (b >> 1))
        gw = gain(w); up = gw > gm
        end = np.where(up, m, w); low = right == up
        l = np.where(low, end, l); r = np.where(low, r, end)
        m = np.where(up, w, m); gm = np.where(up, gw, gm)
    return {"ym": np.stack([gtable(m)] * N).astype(np.float32), "yg": np.stack([gtable(gm)] * N).astype(np.float32)}

@@ -1,0 +1,446 @@
+from concourse.bass import DstId, RemoteDMATransfer
+from concourse.mybir import AluOpType as ALU, ActivationFunctionType as ACT
+
+WC = 12288
+V = 32
+NE = 4
+CYC = 0.001
+PEC = 0.0005
+GAM = 1.56
+LINK = 6.0
+HOP = 0.15
+SAME = 0.12
+SLACK = 0.05
+LOAD = 12.5
+NI, NF = 48, 10
+
+SCRATCH = {
+    "win": ("sbuf", [128, WC], "bfloat16"),
+    "lo_s": ("sbuf", [128, 64], "int32"),
+    "n_s": ("sbuf", [128, 64], "int32"),
+    "ones": ("sbuf", [128, 128], "bfloat16"),
+    "mones": ("sbuf", [128, 128], "bfloat16"),
+    "ident": ("sbuf", [128, 128], "bfloat16"),
+    "nident": ("sbuf", [128, 128], "bfloat16"),
+    "bo1": ("sbuf", [128, 128], "bfloat16"),
+    "bo": ("sbuf", [128, 128], "bfloat16"),
+    "pc": ("sbuf", [128, 16], "int32"),
+    "pc2": ("sbuf", [128, 16], "int32"),
+    "m16": ("sbuf", [128, 16], "float32"),
+    "zsum": ("sbuf", [128, 144], "float32"),
+    "fexp": ("sbuf", [128, 2048], "float16"),
+    "qbuf": ("sbuf", [128, 16, 128], "float32"),
+    "absd": ("sbuf", [128, 16, 128], "float32"),
+    "land": ("sbuf", [128, 2 * NE * 3 * 128], "float32"),
+    "sendb": ("sbuf", [128, 2 * NE * 128], "float32"),
+    "om": ("sbuf", [128, 64], "float32"),
+    "og": ("sbuf", [128, 64], "float32"),
+}
+for _x in range(2):
+    SCRATCH["n4l%d" % _x] = ("sbuf", [128, 128], "float16")
+    SCRATCH["n4_%d" % _x] = ("sbuf", [128, 16, 128], "float32")
+    SCRATCH["b4_%d" % _x] = ("sbuf", [128, 16, 128], "bfloat16")
+    SCRATCH["st%d" % _x] = ("sbuf", [128, 2048], "bfloat16")
+    SCRATCH["s0_%d" % _x] = ("sbuf", [128, 512], "bfloat16")
+    SCRATCH["sn_%d" % _x] = ("sbuf", [128, 512], "bfloat16")
+    SCRATCH["s0c%d" % _x] = ("sbuf", [128, 16, V], "bfloat16")
+    SCRATCH["eo%d" % _x] = ("sbuf", [128, 64], "uint16")
+    SCRATCH["wl%d" % _x] = ("sbuf", [128, NE * 128], "float16")
+    SCRATCH["off%d" % _x] = ("sbuf", [128, NE * 128], "uint16")
+    SCRATCH["si%d" % _x] = ("sbuf", [128, NE * NI * V], "int32")
+    SCRATCH["sf%d" % _x] = ("sbuf", [128, NE * NF * V], "float32")
+    SCRATCH["ps%d" % _x] = ("psum", [128, 512], "float32")
+    SCRATCH["pt%d" % _x] = ("psum", [128, 4, 128], "float32")
+for _k in range(4):
+    SCRATCH["pa%d" % _k] = ("psum", [128, 4, 128], "float32")
+
+SEMAPHORES = ["cv", "ca", "ct", "cg", "ld_lo", "ld_n", "ld_w", "sent", "st_s", "st_a"] + \
+    ["arr%d" % _k for _k in range(2 * NE)]
+
+
+def rank_program(g, core, T, topo):
+    rank = T.rank_of(core)
+    if rank is None:
+        return
+    cores = list(T.cores)
+    nr = len(cores)
+    peers = [q for q in range(nr) if q != rank]
+    emask = topo.mask(core, cores[peers[0]])
+    for q in peers[1:]:
+        emask = emask & topo.mask(core, cores[q])
+    neng = bin(emask).count("1")
+
+    steps = []
+    lastw = {}
+    readers = {}
+    phase = [-1]
+
+    def add(e, fns, cost, reads, writes, lat=0.0, event=None, after=None):
+        deps = {}
+        for k in reads:
+            if k in lastw:
+                deps[lastw[k]] = True
+            if k.startswith("P"):
+                for j in readers.get(k, []):
+                    if steps[j]["e"] != e:
+                        deps.setdefault(j, False)
+        for k in writes:
+            if k in lastw:
+                deps.setdefault(lastw[k], False)
+            for j in readers.get(k, []):
+                deps.setdefault(j, False)
+        if after is not None:
+            deps.setdefault(after, None)
+        i = len(steps)
+        steps.append({"e": e, "fns": fns, "cost": cost, "lat": lat, "event": event, "deps": deps, "w": phase[0]})
+        for k in reads:
+            readers.setdefault(k, []).append(i)
+        for k in writes:
+            lastw[k] = i
+            readers[k] = []
+
+    def tt(out, a, b, alu, reads, writes, n=V):
+        k = 1 if [r for r in reads if r.startswith("P")] else 2
+        add("v", [lambda: g.vector.tensor_tensor(out, a, b, alu)], max(64, n * k) * CYC, reads, writes)
+
+    def ts(out, a, s1, s2, o0, o1, reads, writes, n=V):
+        if o1 is None:
+            add("v", [lambda: g.vector.tensor_scalar(out, a, s1, None, o0)], max(64, n) * CYC, reads, writes)
+        else:
+            add("v", [lambda: g.vector.tensor_scalar(out, a, s1, s2, o0, o1)], max(64, n) * CYC, reads, writes)
+
+    def cp(out, a, reads, writes, n=V):
+        add("v", [lambda: g.vector.tensor_copy(out, a)], max(64, n) * CYC, reads, writes)
+
+    def act(out, a, f, reads, writes, n, after=None):
+        add("a", [lambda: g.scalar.activation(out, a, f)], max(64, n) * CYC, reads, writes, after=after)
+
+    def mms(calls, cyc, reads, writes):
+        fns = [(lambda c=c: g.tensor.matmul(c[0], c[1], c[2], c[3], c[4])) for c in calls]
+        add("t", fns, len(calls) * max(64, cyc) * PEC, reads, writes)
+
+    def dma(e, q, out, src, sem, val, lat, reads, writes, after=None):
+        add(e, [lambda: q.dma_start(out, src).then_inc(T.sem[sem], 16)], 0.1, reads, writes, lat, (sem, val), after)
+
+    def pool(fn, reads, writes):
+        add("g", [fn], 0.4, reads, writes)
+
+    dma("a", g.scalar, T.n_s[:], T.span[:], "ld_n", 16, 2.0, [], ["n"])
+    dma("s", g.sync, T.lo_s[:], T.lo[:], "ld_lo", 16, 2.0, [], ["lo"])
+    dma("s", g.sync, T.win[:], T.walk[:], "ld_w", 16, LOAD, [], ["win"], len(steps) - 1)
+
+    add("v", [lambda: g.vector.memset(T.ones[:], 1.0)], 64 * CYC, [], ["ones"])
+    add("v", [lambda: g.vector.memset(T.mones[:], -1.0)], 64 * CYC, [], ["mones"])
+    add("v", [lambda: g.vector.memset(T.zsum[:], 0.0)], 144 * CYC, [], ["z"])
+    pool(lambda: g.iota(T.pc[:], [[-1, 16]], 16, 1), [], ["pc"])
+    pool(lambda: g.affine_select(T.bo1[:], T.ones[:], [[-16, 8], [0, 16]], ALU.is_ge, 0.0, 0, 1), ["ones"], ["bo1"])
+    pool(lambda: g.affine_select(T.bo[:], T.bo1[:], [[16, 8], [0, 16]], ALU.is_ge, 0.0, 15, -1), ["bo1"], ["bo"])
+    pool(lambda: g.affine_select(T.ident[:], T.ones[:], [[-1, 128]], ALU.is_equal, 0.0, 0, 1), ["ones"], ["id"])
+    pool(lambda: g.affine_select(T.nident[:], T.mones[:], [[-1, 128]], ALU.is_equal, 0.0, 0, 1), ["mones"], ["nid"])
+    ts(T.pc2[:], T.pc[:], 15, None, ALU.bitwise_and, None, ["pc"], ["pc2"])
+    ts(T.m16[:], T.pc2[:], 0.0, None, ALU.is_equal, None, ["pc2"], ["m16"])
+    for c in range(16):
+        ts(T.fexp[:, c * 128:(c + 1) * 128], T.bo[:], T.m16[:, c:c + 1], None, ALU.mult, None, ["bo", "m16"], ["f%d" % c])
+    cp(T.zsum[:, 15:143:16], T.bo[:, 0:128:16], ["bo"], ["z"])
+
+    slots = {}
+
+    def blk(kind, x, e, name, w=1, sub=None):
+        key = (kind, name)
+        if key not in slots:
+            used = slots.get(("used", kind), 0)
+            slots[key] = used
+            slots[("used", kind)] = used + w
+        base = (e * (NI if kind == "si" else NF) + slots[key]) * V
+        if sub is not None:
+            return T["%s%d" % (kind, x)][:, base + sub * V: base + (sub + 1) * V]
+        return T["%s%d" % (kind, x)][:, base: base + w * V]
+
+    for nm in ("MS", "lm2", "R2", "h2", "d2", "o2"):
+        blk("si", 0, 0, nm, 2)
+    blk("sf", 0, 0, "G", 4)
+
+    def pblk(x, name, a=0, b=2):
+        base = {"COL": 4, "LOW": 6, "sg2": 8}[name]
+        return T["ps%d" % x][:, (base + a) * V:(base + b) * V]
+
+    def node(x, e):
+        I = lambda n, w=1, sub=None: blk("si", x, e, n, w, sub)
+        K = lambda n: "%s.%d.%d" % (n, x, e)
+        W = lambda a, b: T["wl%d" % x][:, e * 128 + a * V: e * 128 + b * V]
+        O = lambda a, b: T["off%d" % x][:, e * 128 + a * V: e * 128 + b * V]
+        B, kR, knR, kc0, kc1 = "Ps%d" % x, "R.%d" % x, "nR.%d" % x, "c0.%d" % x, "c1.%d" % x
+        ts(I("h"), I("M"), 1, None, ALU.arith_shift_right, None, [K("M")], [K("h")])
+        ts(I("sg"), pblk(x, "LOW", 1, 2), 2.0, -1.0, ALU.mult, ALU.add, [kR, B], [K("sg")])
+        tt(I("d"), I("sg"), I("h"), ALU.mult, [K("sg"), K("h")], [K("d")])
+        tt(W(1, 2), W(0, 1), I("d"), ALU.add, [K("m"), K("d")], [K("w1")])
+        tt(pblk(x, "COL", 0, 1), W(0, 1), T.lo_s[:, x * V:(x + 1) * V], ALU.add, [K("m"), "lo", B], [kc0])
+        tt(pblk(x, "COL", 1, 2), pblk(x, "COL", 0, 1), I("d"), ALU.add, [kc0, K("d"), B], [kc1])
+        cp(O(1, 2), pblk(x, "COL", 1, 2), [kc1, B], [K("off1")])
+        if e == 0:
+            cp(O(0, 1), pblk(x, "COL", 0, 1), [kc0, B], [K("off0")])
+        tt(I("MS", 2, 1), I("M"), I("h"), ALU.subtract, [K("M"), K("h")], [K("X")])
+        ts(I("h2", 2), I("MS", 2), 1, None, ALU.arith_shift_right, None, [K("s"), K("X")], [K("h2")], 2 * V)
+        ts(pblk(x, "LOW", 0, 1), pblk(x, "LOW", 1, 2), -1.0, 1.0, ALU.mult, ALU.add, [kR, B], [knR])
+        tt(I("lm2", 2), pblk(x, "LOW"), I("MS", 2), ALU.mult, [kR, knR, K("s"), K("X"), B], [K("lm2")], 2 * V)
+        tt(I("R2", 2, 0), I("lm2", 2, 0), I("h"), ALU.is_gt, [K("lm2"), K("h")], [K("R2a")])
+        tt(I("R2", 2, 1), I("lm2", 2, 1), I("h"), ALU.is_gt, [K("lm2"), K("h")], [K("R2b")])
+        ts(pblk(x, "sg2"), I("R2", 2), 2.0, -1.0, ALU.mult, ALU.add, [K("R2a"), K("R2b"), B], ["sg2.%d" % x], 2 * V)
+        tt(I("d2", 2), pblk(x, "sg2"), I("h2", 2), ALU.mult, ["sg2.%d" % x, K("h2"), B], [K("d2")], 2 * V)
+        tt(W(2, 4), W(0, 2), I("d2", 2), ALU.add, [K("m"), K("w1"), K("d2")], [K("w2")], 2 * V)
+        tt(I("o2", 2), pblk(x, "COL"), I("d2", 2), ALU.add, [K("d2"), kc0, kc1, B], [K("o2")], 2 * V)
+        cp(O(2, 4), I("o2", 2), [K("o2")], [K("off2")], 2 * V)
+        tt(I("dd"), I("d2", 2, 1), I("d2", 2, 0), ALU.subtract, [K("d2")], [K("dd")])
+        if e < NE - 1:
+            tt(I("dM"), I("MS", 2, 1), I("MS", 2, 0), ALU.subtract, [K("s"), K("X")], [K("dM")])
+            tt(I("dh"), I("h2", 2, 1), I("h2", 2, 0), ALU.subtract, [K("h2")], [K("dh")])
+            tt(I("dY"), I("dM"), I("dh"), ALU.subtract, [K("dM"), K("dh")], [K("dY")])
+            tt(I("XN"), I("MS", 2, 0), I("h2", 2, 0), ALU.subtract, [K("s"), K("h2")], [K("XN")])
+            tt(I("YN"), I("XN"), I("h"), ALU.subtract, [K("XN"), K("h")], [K("YN")])
+
+    def start(x):
+        I = lambda n, w=1, sub=None: blk("si", x, 0, n, w, sub)
+        K = lambda n: "%s.%d.0" % (n, x)
+        n = T.n_s[:, x * V:(x + 1) * V]
+        lo = T.lo_s[:, x * V:(x + 1) * V]
+        ts(I("MS", 2, 0), n, 1, None, ALU.arith_shift_right, None, ["n"], [K("s")])
+        tt(I("M"), n, I("MS", 2, 0), ALU.subtract, ["n", K("s")], [K("M")])
+        cp(T["wl%d" % x][:, 0:V], I("MS", 2, 0), [K("s")], [K("m")])
+        tt(pblk(x, "LOW", 1, 2), I("M"), I("MS", 2, 0), ALU.is_gt, [K("M"), K("s"), "Ps%d" % x], ["R.%d" % x])
+        tt(I("oe"), n, lo, ALU.add, ["n", "lo"], [K("oe")])
+        cp(T["eo%d" % x][:, 0:V], lo, ["lo"], ["e0.%d" % x])
+        cp(T["eo%d" % x][:, V:2 * V], I("oe"), [K("oe")], ["en.%d" % x])
+        node(x, 0)
+
+    def spread_n(x):
+        n = T.n_s[:, x * V:(x + 1) * V]
+        for p in range(4):
+            cp(T["n4l%d" % x][:, p * V:(p + 1) * V], n, ["n"], ["n4l.%d.%d" % (x, p)])
+        for k in range(4):
+            mms([(T["pa%d" % k][:, c - 4 * k, :], T.fexp[:, c * 128:(c + 1) * 128], T["n4l%d" % x][:], True, True)
+                 for c in range(4 * k, 4 * k + 4)], 128,
+                ["f%d" % c for c in range(4 * k, 4 * k + 4)] + ["n4l.%d.%d" % (x, p) for p in range(4)], ["Pa%d" % k])
+            act(T["n4_%d" % x][:, 4 * k:4 * k + 4, :], T["pa%d" % k][:], ACT.Copy, ["Pa%d" % k], ["n4.%d.%d" % (x, k)], 512)
+
+    def advance(x, e):
+        p0 = 0 if e == 0 else 1
+        n = (4 - p0) * V
+        last = e == NE - 1
+        I = lambda n, w=1, sub=None: blk("si", x, e, n, w, sub)
+        F = lambda n, w=1, sub=None: blk("sf", x, e, n, w, sub)
+        K = lambda n: "%s.%d.%d" % (n, x, e)
+        J = lambda n, w=1, sub=None: blk("si", x, e + 1, n, w, sub)
+        L = lambda n: "%s.%d.%d" % (n, x, e + 1)
+        i = 2 * e + x
+        B, kR, kg = "Ps%d" % x, "R.%d" % x, K("G")
+        ps = T["ps%d" % x][:, 0:n]
+        slot = lambda k: T.land[:, (3 * i + k) * 128:(3 * i + k) * 128 + n]
+        m = T["wl%d" % x][:, e * 128:e * 128 + V]
+        G = lambda p: F("G", 4, p)
+        base = (e * NF + p0) * V
+        tt(ps, ps, slot(0), ALU.add, [B, "arr%d" % i], [B], n)
+        tt(ps, ps, slot(1), ALU.add, [B], [B], n)
+        tt(T["sf%d" % x][:, base:base + n], ps, slot(2), ALU.add, [B], [kg], n)
+        if e > 0:
+            gm, kgm = blk("sf", x, e - 1, "gm2"), "gm2.%d.%d" % (x, e - 1)
+        else:
+            gm, kgm = G(0), kg
+        gout, kgout = (T.og[:, x * V:(x + 1) * V], "og%d" % x) if last else (F("gm2"), K("gm2"))
+        mout, kmout = (T.om[:, x * V:(x + 1) * V], "om%d" % x) if last else \
+            (T["wl%d" % x][:, (e + 1) * 128:(e + 1) * 128 + V], L("m"))
+        tt(I("up1"), G(1), gm, ALU.is_gt, [kg, kgm], [K("up1")])
+        tt(I("t4"), I("up1"), I("d"), ALU.mult, [K("up1"), K("d")], [K("t4")])
+        tt(F("gm1"), G(1), gm, ALU.max, [kg, kgm], [K("gm1")])
+        tt(F("dg"), G(3), G(2), ALU.subtract, [kg], [K("dg")])
+        tt(F("t1"), I("up1"), F("dg"), ALU.mult, [K("up1"), K("dg")], [K("t1")])
+        tt(F("g2"), G(2), F("t1"), ALU.add, [kg, K("t1")], [K("g2")])
+        tt(I("t3"), I("up1"), I("dd"), ALU.mult, [K("up1"), K("dd")], [K("t3")])
+        tt(I("d1"), I("d2", 2, 0), I("t3"), ALU.add, [K("d2"), K("t3")], [K("d1")])
+        tt(I("up2"), F("g2"), F("gm1"), ALU.is_gt, [K("g2"), K("gm1")], [K("up2")])
+        tt(I("m1"), m, I("t4"), ALU.add, [K("m"), K("t4")], [K("m1")])
+        tt(I("t6"), I("up2"), I("d1"), ALU.mult, [K("up2"), K("d1")], [K("t6")])
+        tt(gout, F("g2"), F("gm1"), ALU.max, [K("g2"), K("gm1")], [kgout])
+        tt(mout, I("m1"), I("t6"), ALU.add, [K("m1"), K("t6")], [kmout])
+        if last:
+            return
+        tt(I("t2"), I("up1"), I("dh"), ALU.mult, [K("up1"), K("dh")], [K("t2")])
+        tt(J("MS", 2, 0), I("h2", 2, 0), I("t2"), ALU.add, [K("h2"), K("t2")], [L("s")])
+        ts(I("R1"), I("d1"), 0.0, None, ALU.is_gt, None, [K("d1")], [K("R1")])
+        tt(I("t7"), I("up1"), I("dY"), ALU.mult, [K("up1"), K("dY")], [K("t7")])
+        tt(I("Y"), I("YN"), I("t7"), ALU.add, [K("t7"), K("YN")], [K("Y")])
+        tt(I("low"), I("up2"), I("R1"), ALU.is_equal, [K("up2"), K("R1")], [K("low")])
+        tt(I("t5"), I("up2"), I("Y"), ALU.mult, [K("up2"), K("Y")], [K("t5")])
+        tt(J("M"), I("h"), I("t5"), ALU.add, [K("h"), K("t5")], [L("M")])
+        tt(I("lm"), I("low"), J("M"), ALU.mult, [K("low"), L("M")], [K("lm")])
+        tt(pblk(x, "LOW", 1, 2), I("lm"), J("MS", 2, 0), ALU.is_gt, [K("lm"), L("s"), B], [kR])
+        node(x, e + 1)
+
+    def rise(x, turn, bank):
+        ends = lambda a: T.win[:, 0:WC].indirect(T["eo%d" % x][:, a * V:(a + 1) * V])
+        at = lambda b, c: T[b][:, c // 4, c % 4 * V:(c % 4 + 1) * V]
+        s0, sn, b4 = T["s0_%d" % x], T["sn_%d" % x], T["b4_%d" % x]
+        act(s0[:], ends(0), ACT.Copy, ["win", "e0.%d" % x], ["s0.%d" % x], 512 * GAM)
+        mms([(at(turn, c), T.ident[:], s0[:, c:512:16], True, True) for c in range(16)], 64,
+            ["s0.%d" % x, "id"], ["P" + turn[1:]])
+        act(T["s0c%d" % x][:], T[turn][:], ACT.Copy, ["P" + turn[1:]], ["s0c.%d" % x], 512)
+        if bank is None:
+            cp(sn[:], ends(1), ["win", "en.%d" % x], ["sn.%d" % x], 512 * GAM)
+            keys = ["b4a.%d.%d" % (x, c) for c in range(16)]
+            for c in range(16):
+                tt(b4[:, c, 0:V], sn[:, c:512:16], s0[:, c:512:16], ALU.subtract, ["sn.%d" % x, "s0.%d" % x], [keys[c]])
+        else:
+            act(sn[:], ends(1), ACT.Copy, ["win", "en.%d" % x], ["sn.%d" % x], 512 * GAM)
+            calls = []
+            for c in range(16):
+                calls.append((at(bank, c), T.ident[:], sn[:, c:512:16], True, False))
+                calls.append((at(bank, c), T.nident[:], s0[:, c:512:16], False, True))
+            mms(calls, 64, ["sn.%d" % x, "s0.%d" % x, "id", "nid"], ["P" + bank[1:]])
+            keys = ["b4a.%d" % x]
+            cp(b4[:, :, 0:V], T[bank][:], ["P" + bank[1:]], keys, 512)
+        cp(b4[:, :, V:2 * V], b4[:, :, 0:V], keys, ["b4b.%d" % x], 256)
+        cp(b4[:, :, 2 * V:4 * V], b4[:, :, 0:2 * V], keys + ["b4b.%d" % x], ["b4.%d" % x], 512)
+
+    def gains(x, e):
+        p0 = 0 if e == 0 else 1
+        P = 4 - p0
+        n = P * V
+        K = lambda nm: "%s.%d.%d" % (nm, x, e)
+        for p in range(p0, 4):
+            act(T["st%d" % x][:, (p - p0) * 512:(p - p0 + 1) * 512],
+                T.win[:, 0:WC].indirect(T["off%d" % x][:, e * 128 + p * V:e * 128 + (p + 1) * V]), ACT.Copy,
+                ["win", K("off%d" % min(p, 2))], ["st.%d.%d" % (x, p - p0)], 512 * GAM,
+                len(steps) - 1 if p > p0 else None)
+        rhs = T["wl%d" % x][:, e * 128 + p0 * V:(e + 1) * 128]
+        for k in range(4):
+            cs = range(4 * k, 4 * k + 4)
+            pt = T["pt%d" % (k % 2)]
+            mms([(pt[:, c - 4 * k, 0:n], T.fexp[:, c * 128:(c + 1) * 128], rhs, True, True) for c in cs], n,
+                [K("m"), K("w1"), K("w2")] + ["f%d" % c for c in cs], ["Pt%d" % (k % 2)])
+            tt(T.qbuf[:, 4 * k:4 * k + 4, 0:n], pt[:, :, 0:n], T["b4_%d" % x][:, 4 * k:4 * k + 4, 0:n], ALU.mult,
+               ["Pt%d" % (k % 2), "b4.%d" % x], ["q%d" % k], 4 * n)
+        for k in range(4):
+            cs = range(4 * k, 4 * k + 4)
+            kb = "Pa%d" % k
+            bank = T["pa%d" % k]
+            pa = bank[:, :, 0:n]
+            mms([(bank[:, :, p * V:(p + 1) * V], T.nident[:], T["s0c%d" % x][:, 4 * k:4 * k + 4, :], p == 0, False)
+                 for p in range(P)], 128, ["s0c.%d" % x, "nid"], [kb])
+            mms([(bank[:, c - 4 * k, 0:n], T.ident[:], T["st%d" % x][:, c:16 * n:16], False, c == 4 * k + 3) for c in cs], n,
+                ["st.%d.%d" % (x, p) for p in range(P)] + ["id"], [kb])
+            tt(pa, pa, T["n4_%d" % x][:, 4 * k:4 * k + 4, 0:n], ALU.mult, [kb, "n4.%d.%d" % (x, k)], [kb], 4 * n)
+            tt(pa, pa, T.qbuf[:, 4 * k:4 * k + 4, 0:n], ALU.subtract, [kb, "q%d" % k], [kb], 4 * n)
+            for a, b in ([(0, 2), (2, 4)] if k == 3 else [(0, 4)]):
+                ca = range(4 * k + a, 4 * k + b)
+                act(T.absd[:, 4 * k + a:4 * k + b, 0:n], bank[:, a:b, 0:n], ACT.Abs, [kb], ["ab%d" % c for c in ca], (b - a) * n)
+                mms([(T["ps%d" % x][:, 0:n], T.zsum[:, 15 - c:143 - c], T.absd[:, c, 0:n], c == 0, c == 15) for c in ca],
+                    4 * n, ["ab%d" % c for c in ca] + ["z"], ["Ps%d" % x])
+        i = 2 * e + x
+        src = T.sendb[:, i * 128:i * 128 + n]
+        act(src, T["ps%d" % x][:, 0:n], ACT.Copy, ["Ps%d" % x], ["snd%d" % i], n)
+        ids, dsts = [], []
+        for q in peers:
+            rid, pid, _se = topo.addr(cores[q])
+            k = (rank - q - 1) % nr
+            ids.append(DstId(rid=rid, pnc=pid))
+            dsts.append(T.land[:, (3 * i + k) * 128:(3 * i + k) * 128 + n])
+        add("g", [lambda: g.remote_dma_fused(
+            [RemoteDMATransfer(dst_ids=ids, dma_engine_mask=emask, remote_sem=T.sem["arr%d" % i], src=src, dsts=dsts)],
+            local_sem=T.sem.sent)], 0.5, ["snd%d" % i], ["arr%d" % i], LINK, ("arr%d" % i, neng * len(peers)))
+
+    spread_n(0)
+    start(0)
+    spread_n(1)
+    start(1)
+    phase[0] = 0
+    rise(0, "pa3", None)
+    gains(0, 0)
+    phase[0] = 0.5
+    rise(1, "pt1", "pt0")
+    phase[0] = 1
+    gains(1, 0)
+    for e in range(1, NE):
+        for x in range(2):
+            phase[0] = 2 * e + x
+            advance(x, e - 1)
+            gains(x, e)
+    for x in range(2):
+        phase[0] = 2 * NE + x
+        advance(x, NE - 1)
+        dma("a", g.scalar, T.yg[:, x * V:(x + 1) * V], T.og[:, x * V:(x + 1) * V], "st_a", 32, 2.0, ["og%d" % x], [])
+        dma("s", g.sync, T.ym[:, x * V:(x + 1) * V], T.om[:, x * V:(x + 1) * V], "st_s", 32, 2.0, ["om%d" % x], [])
+
+    ns = len(steps)
+    succ = [[] for _ in range(ns)]
+    for i, s in enumerate(steps):
+        for j in s["deps"]:
+            succ[j].append(i)
+
+    def waits(j, i):
+        raw = steps[i]["deps"][j]
+        return not (raw is None or (steps[j]["e"] == "t" and steps[i]["e"] == "t" and not raw))
+
+    def gap(j, i):
+        if not waits(j, i):
+            return 0.0
+        return steps[j]["lat"] + (SAME if steps[j]["e"] == steps[i]["e"] else HOP)
+
+    way = [0.0] * ns
+    for i in range(ns - 1, -1, -1):
+        way[i] = steps[i]["cost"] + max([steps[i]["lat"]] + [gap(i, j) + way[j] for j in succ[i]])
+    left = [len(s["deps"]) for s in steps]
+    can = [0.0] * ns
+    ready = {e: [] for e in "vatgs"}
+    free = {e: 0.0 for e in "vatgs"}
+    for i in range(ns):
+        if left[i] == 0:
+            ready[steps[i]["e"]].append(i)
+    order = []
+    while len(order) < ns:
+        best = None
+        for e in "vatgs":
+            if ready[e]:
+                t0 = max(free[e], min(can[i] for i in ready[e]))
+                if best is None or t0 < best[0]:
+                    best = (t0, e)
+        t0, e = best
+        i = max([j for j in ready[e] if can[j] <= t0 + SLACK], key=lambda j: (-steps[j]["w"], way[j], -j))
+        ready[e].remove(i)
+        free[e] = max(t0, can[i]) + steps[i]["cost"]
+        order.append(i)
+        for j in succ[i]:
+            can[j] = max(can[j], free[e] + gap(i, j))
+            left[j] -= 1
+            if left[j] == 0:
+                ready[steps[j]["e"]].append(j)
+
+    queue = {"v": g.vector, "a": g.scalar, "t": g.tensor, "g": g, "s": g.sync}
+    semof = {"v": "cv", "a": "ca", "t": "ct", "g": "cg"}
+    count = {"v": 0, "a": 0, "t": 0, "g": 0}
+    known = {}
+    done = {}
+    for i in order:
+        s = steps[i]
+        e = s["e"]
+        want = {}
+        for j in s["deps"]:
+            if waits(j, i):
+                sem, val = done[j]
+                want[sem] = max(want.get(sem, 0), val)
+        for sem, val in want.items():
+            if val > known.get((e, sem), 0):
+                queue[e].wait_ge(T.sem[sem], val)
+                known[(e, sem)] = val
+        if s["event"] is not None:
+            s["fns"][0]()
+            done[i] = s["event"]
+        else:
+            for fn in s["fns"]:
+                count[e] += 1
+                fn().then_inc(T.sem[semof[e]], 1)
+            done[i] = (semof[e], count[e])
+
+    for e in "vatg":
+        g.wait_ge(T.sem[semof[e]], count[e])
+    g.wait_ge(T.sem.sent, neng * 2 * NE)
+    g.wait_ge(T.sem.st_a, 32)
+    g.wait_ge(T.sem.st_s, 32)

@@ -3,59 +3,74 @@ from concourse.mybir import AluOpType as ALU, ActivationFunctionType as ACT
 
 WC = 12288
 V = 32
+NP = 2
 NE = 4
-CYC = 0.001
-PEC = 0.0005
+NPA = 3
+VGATHER = [(0, 0, 0)]
+CYC = 0.00085
+PEC = 0.00043
 GAM = 1.56
-LINK = 6.0
-HOP = 0.15
-SAME = 0.12
+LINK = 5.0
+HOP = 0.17
+SAME = 0.17
 SLACK = 0.05
 LOAD = 12.5
-NI, NF = 48, 10
+ROUNDS = 0
+ORDER = []
+MG = 12582912.0
+REC = {"ur": 60, "gr": 4, "mr": 20, "so": 4, "ao": 5, "mo": 4, "dr": 3, "do": 3, "xa": 5, "xb": 5, "xo": 5}
 
 SCRATCH = {
     "win": ("sbuf", [128, WC], "bfloat16"),
     "lo_s": ("sbuf", [128, 64], "int32"),
     "n_s": ("sbuf", [128, 64], "int32"),
-    "ones": ("sbuf", [128, 128], "bfloat16"),
-    "mones": ("sbuf", [128, 128], "bfloat16"),
+    "lnf": ("sbuf", [128, 128], "float32"),
+    "loq": ("sbuf", [128, 64], "int32"),
+    "nq": ("sbuf", [128, 64], "int32"),
+    "nh": ("sbuf", [128, 64], "float16"),
+    "im": ("sbuf", [128, 128], "int32"),
+    "ig": ("sbuf", [128, 128], "int32"),
+    "pi": ("sbuf", [128, 8], "int32"),
+    "pf": ("sbuf", [128, 8], "float32"),
     "ident": ("sbuf", [128, 128], "bfloat16"),
     "nident": ("sbuf", [128, 128], "bfloat16"),
-    "bo1": ("sbuf", [128, 128], "bfloat16"),
-    "bo": ("sbuf", [128, 128], "bfloat16"),
-    "pc": ("sbuf", [128, 16], "int32"),
-    "pc2": ("sbuf", [128, 16], "int32"),
-    "m16": ("sbuf", [128, 16], "float32"),
-    "zsum": ("sbuf", [128, 144], "float32"),
+    "permq": ("sbuf", [128, 128], "float32"),
+    "permt": ("sbuf", [128, 128], "float32"),
+    "bsel": ("sbuf", [128, 8], "float32"),
+    "boq": ("sbuf", [128, 128], "float16"),
+    "mq": ("sbuf", [128, 16], "float32"),
     "fexp": ("sbuf", [128, 2048], "float16"),
-    "qbuf": ("sbuf", [128, 16, 128], "float32"),
-    "absd": ("sbuf", [128, 16, 128], "float32"),
-    "land": ("sbuf", [128, 2 * NE * 3 * 128], "float32"),
-    "sendb": ("sbuf", [128, 2 * NE * 128], "float32"),
-    "om": ("sbuf", [128, 64], "float32"),
-    "og": ("sbuf", [128, 64], "float32"),
+    "land": ("sbuf", [128, NP * NE * 3 * 128], "float32"),
+    "sendb": ("sbuf", [128, NP * NE * 128], "float32"),
+    "oq": ("sbuf", [128, 128], "float32"),
+    "ol": ("sbuf", [128, 128], "float32"),
+    "wr": ("sbuf", [128, 256], "float32"),
+    "wt": ("sbuf", [128, 256], "float16"),
+    "gt": ("sbuf", [128, 128], "float32"),
+    "d2": ("sbuf", [128, 64, 2], "int32"),
+    "ti": ("sbuf", [128, 4, 64], "int32"),
+    "tf": ("sbuf", [128, 6, 64], "float32"),
+    "ps": ("psum", [128, 512], "float32"),
+    "pp": ("psum", [128, 512], "float32"),
+    "pv": ("psum", [128, 512], "float32"),
 }
-for _x in range(2):
-    SCRATCH["n4l%d" % _x] = ("sbuf", [128, 128], "float16")
-    SCRATCH["n4_%d" % _x] = ("sbuf", [128, 16, 128], "float32")
-    SCRATCH["b4_%d" % _x] = ("sbuf", [128, 16, 128], "bfloat16")
+for _n in REC:
+    SCRATCH[_n] = ("sbuf", [128, 65 * REC[_n]], "float32")
+for _k in range(NPA):
+    SCRATCH["pa%d" % _k] = ("psum", [128, V, 16], "float32")
+    SCRATCH["ab%d" % _k] = ("sbuf", [128, 512], "float32")
+for _x in range(NP):
+    SCRATCH["nw%d" % _x] = ("sbuf", [128, 512], "float32")
+    SCRATCH["qb%d" % _x] = ("sbuf", [128, 2048], "float32")
     SCRATCH["st%d" % _x] = ("sbuf", [128, 2048], "bfloat16")
     SCRATCH["s0_%d" % _x] = ("sbuf", [128, 512], "bfloat16")
-    SCRATCH["sn_%d" % _x] = ("sbuf", [128, 512], "bfloat16")
-    SCRATCH["s0c%d" % _x] = ("sbuf", [128, 16, V], "bfloat16")
+    SCRATCH["ri%d" % _x] = ("sbuf", [128, 512], "bfloat16")
     SCRATCH["eo%d" % _x] = ("sbuf", [128, 64], "uint16")
-    SCRATCH["wl%d" % _x] = ("sbuf", [128, NE * 128], "float16")
-    SCRATCH["off%d" % _x] = ("sbuf", [128, NE * 128], "uint16")
-    SCRATCH["si%d" % _x] = ("sbuf", [128, NE * NI * V], "int32")
-    SCRATCH["sf%d" % _x] = ("sbuf", [128, NE * NF * V], "float32")
-    SCRATCH["ps%d" % _x] = ("psum", [128, 512], "float32")
-    SCRATCH["pt%d" % _x] = ("psum", [128, 4, 128], "float32")
-for _k in range(4):
-    SCRATCH["pa%d" % _k] = ("psum", [128, 4, 128], "float32")
+    SCRATCH["off%d" % _x] = ("sbuf", [128, 128], "uint16")
+    SCRATCH["pt%d" % _x] = ("psum", [128, 128, 4], "float32")
 
 SEMAPHORES = ["cv", "ca", "ct", "cg", "ld_lo", "ld_n", "ld_w", "sent", "st_s", "st_a"] + \
-    ["arr%d" % _k for _k in range(2 * NE)]
+    ["arr%d_%d" % (_k, _r) for _k in range(NP * NE) for _r in range(4)]
 
 
 def rank_program(g, core, T, topo):
@@ -64,7 +79,7 @@ def rank_program(g, core, T, topo):
         return
     cores = list(T.cores)
     nr = len(cores)
-    peers = [q for q in range(nr) if q != rank]
+    peers = [(rank + k) % nr for k in range(1, nr)]
     emask = topo.mask(core, cores[peers[0]])
     for q in peers[1:]:
         emask = emask & topo.mask(core, cores[q])
@@ -98,22 +113,28 @@ def rank_program(g, core, T, topo):
         for k in writes:
             lastw[k] = i
             readers[k] = []
+        return i
 
-    def tt(out, a, b, alu, reads, writes, n=V):
-        k = 1 if [r for r in reads if r.startswith("P")] else 2
-        add("v", [lambda: g.vector.tensor_tensor(out, a, b, alu)], max(64, n * k) * CYC, reads, writes)
+    def tt(out, a, b, alu, reads, writes, n=64):
+        add("v", [lambda: g.vector.tensor_tensor(out, a, b, alu)], max(64, n) * CYC, reads, writes)
 
-    def ts(out, a, s1, s2, o0, o1, reads, writes, n=V):
+    def ts(out, a, s1, s2, o0, o1, reads, writes, n=64):
         if o1 is None:
             add("v", [lambda: g.vector.tensor_scalar(out, a, s1, None, o0)], max(64, n) * CYC, reads, writes)
         else:
             add("v", [lambda: g.vector.tensor_scalar(out, a, s1, s2, o0, o1)], max(64, n) * CYC, reads, writes)
 
-    def cp(out, a, reads, writes, n=V):
+    def cp(out, a, reads, writes, n=64):
         add("v", [lambda: g.vector.tensor_copy(out, a)], max(64, n) * CYC, reads, writes)
 
+    def scan(out, d0, d1, o1, reads, writes, n):
+        add("v", [lambda: g.vector.tensor_tensor_scan(out, d0, d1, 0.0, ALU.mult, o1)], max(64, n) * CYC, reads, writes)
+
+    def fill(ap, val, key, n=64):
+        add("v", [lambda: g.vector.memset(ap, val)], max(64, n) * CYC, [], [key])
+
     def act(out, a, f, reads, writes, n, after=None):
-        add("a", [lambda: g.scalar.activation(out, a, f)], max(64, n) * CYC, reads, writes, after=after)
+        return add("a", [lambda: g.scalar.activation(out, a, f)], max(64, n) * CYC, reads, writes, after=after)
 
     def mms(calls, cyc, reads, writes):
         fns = [(lambda c=c: g.tensor.matmul(c[0], c[1], c[2], c[3], c[4])) for c in calls]
@@ -129,245 +150,229 @@ def rank_program(g, core, T, topo):
     dma("s", g.sync, T.lo_s[:], T.lo[:], "ld_lo", 16, 2.0, [], ["lo"])
     dma("s", g.sync, T.win[:], T.walk[:], "ld_w", 16, LOAD, [], ["win"], len(steps) - 1)
 
-    add("v", [lambda: g.vector.memset(T.ones[:], 1.0)], 64 * CYC, [], ["ones"])
-    add("v", [lambda: g.vector.memset(T.mones[:], -1.0)], 64 * CYC, [], ["mones"])
-    add("v", [lambda: g.vector.memset(T.zsum[:], 0.0)], 144 * CYC, [], ["z"])
-    pool(lambda: g.iota(T.pc[:], [[-1, 16]], 16, 1), [], ["pc"])
-    pool(lambda: g.affine_select(T.bo1[:], T.ones[:], [[-16, 8], [0, 16]], ALU.is_ge, 0.0, 0, 1), ["ones"], ["bo1"])
-    pool(lambda: g.affine_select(T.bo[:], T.bo1[:], [[16, 8], [0, 16]], ALU.is_ge, 0.0, 15, -1), ["bo1"], ["bo"])
-    pool(lambda: g.affine_select(T.ident[:], T.ones[:], [[-1, 128]], ALU.is_equal, 0.0, 0, 1), ["ones"], ["id"])
-    pool(lambda: g.affine_select(T.nident[:], T.mones[:], [[-1, 128]], ALU.is_equal, 0.0, 0, 1), ["mones"], ["nid"])
-    ts(T.pc2[:], T.pc[:], 15, None, ALU.bitwise_and, None, ["pc"], ["pc2"])
-    ts(T.m16[:], T.pc2[:], 0.0, None, ALU.is_equal, None, ["pc2"], ["m16"])
-    for c in range(16):
-        ts(T.fexp[:, c * 128:(c + 1) * 128], T.bo[:], T.m16[:, c:c + 1], None, ALU.mult, None, ["bo", "m16"], ["f%d" % c])
-    cp(T.zsum[:, 15:143:16], T.bo[:, 0:128:16], ["bo"], ["z"])
+    pool(lambda: g.iota(T.pi[:, 0:1], [[1, 1]], 0, 1), [], ["p"])
+    pool(lambda: g.iota(T.im[:], [[1, 128]], 0, 0), [], ["im"])
+    pool(lambda: g.iota(T.ig[:], [[1, 8], [0, 16]], 0, 0), [], ["ig"])
+    for k, (val, alu) in enumerate([(7, ALU.bitwise_and), (3, ALU.arith_shift_right), (15, ALU.bitwise_and), (4, ALU.arith_shift_right)]):
+        ts(T.pi[:, k + 1:k + 2], T.pi[:, 0:1], val, None, alu, None, ["p"], ["p%d" % k])
+    cp(T.pf[:, 0:5], T.pi[:, 0:5], ["p", "p0", "p1", "p2", "p3"], ["pf"])
+    col = lambda k: T.pf[:, k:k + 1]
+    ts(col(5), col(1), 16.0, col(2), ALU.mult, ALU.add, ["pf"], ["lq"])
+    ts(col(6), col(3), 8.0, col(4), ALU.mult, ALU.add, ["pf"], ["ql"])
+    ts(T.permt[:], T.im[:], col(6), None, ALU.is_equal, None, ["im", "ql"], ["permt"], 128)
+    ts(T.permq[:], T.im[:], col(5), None, ALU.is_equal, None, ["im", "lq"], ["perm"], 128)
+    ts(T.ident[:], T.im[:], col(0), None, ALU.is_equal, None, ["im", "pf"], ["id"], 128)
+    ts(T.nident[:], T.im[:], col(0), -1.0, ALU.is_equal, ALU.mult, ["im", "pf"], ["nid"], 128)
+    ts(T.bsel[:], T.im[:, 0:8], col(4), None, ALU.is_equal, None, ["im", "pf"], ["bsel"])
+    ts(T.mq[:], T.im[:, 0:16], col(2), None, ALU.is_equal, None, ["im", "pf"], ["mq"])
+    ts(T.boq[:], T.ig[:], col(1), None, ALU.is_equal, None, ["ig", "pf"], ["boq"], 128)
+    for a in range(16):
+        ts(T.fexp[:, a * 128:(a + 1) * 128], T.boq[:], T.mq[:, a:a + 1], None, ALU.mult, None, ["boq", "mq"], ["f%d" % a])
+    fx = lambda a: T.fexp[:, a * 128:(a + 1) * 128]
+    consts = []
+    for name, slots in [("ur", {0: 0.0, 5: 0.0, 35: -1.0, 50: 1.0, 8: 0.0, 32: 0.5, 44: 1.0, 56: 1.0, 25: 0.0, 55: 0.5, 70: 1.0}),
+                        ("gr", {2: 0.0}), ("mr", {8: MG, 12: -MG, 21: MG, 26: -MG}),
+                        ("xa", {0: 0.0, 2: -1.0, 3: -1.0, 4: -1.0}), ("xb", {0: 1.0, 2: -0.5, 3: -0.5, 4: -0.5})]:
+        for a, val in slots.items():
+            consts.append("k%s%d" % (name, a))
+            fill(T[name][:, a:a + 63 * REC[name] + 1:REC[name]], val, consts[-1])
+    cp(T.lnf[:, 0:64], T.lo_s[:], ["lo"], ["lof"])
+    cp(T.lnf[:, 64:128], T.n_s[:], ["n"], ["nf"])
+    mms([(T.pp[:, 0:128], T.permt[:], T.lnf[:], True, True)], 512, ["permt", "lof", "nf"], ["Pp"])
+    cp(T.loq[:], T.pp[:, 0:64], ["Pp"], ["loq"])
+    cp(T.nq[:], T.pp[:, 64:128], ["Pp"], ["nq"])
+    cp(T.nh[:], T.pp[:, 64:128], ["Pp"], ["nh"])
 
-    slots = {}
+    def rec(name, x, a, n=1):
+        q = REC[name] // n
+        b = x * V * REC[name] + a
+        return T[name][:, b:b + (V * n - 1) * q + 1:q]
 
-    def blk(kind, x, e, name, w=1, sub=None):
-        key = (kind, name)
-        if key not in slots:
-            used = slots.get(("used", kind), 0)
-            slots[key] = used
-            slots[("used", kind)] = used + w
-        base = (e * (NI if kind == "si" else NF) + slots[key]) * V
-        if sub is not None:
-            return T["%s%d" % (kind, x)][:, base + sub * V: base + (sub + 1) * V]
-        return T["%s%d" % (kind, x)][:, base: base + w * V]
+    def cols(name, x):
+        return T[name][:, x * V:(x + 1) * V]
 
-    for nm in ("MS", "lm2", "R2", "h2", "d2", "o2"):
-        blk("si", 0, 0, nm, 2)
-    blk("sf", 0, 0, "G", 4)
+    def tmp(name, k, x):
+        return T[name][:, k, x * V:(x + 1) * V]
 
-    def pblk(x, name, a=0, b=2):
-        base = {"COL": 4, "LOW": 6, "sg2": 8}[name]
-        return T["ps%d" % x][:, (base + a) * V:(base + b) * V]
+    def blk(name, x, a, b, base=0, wide=128):
+        return T[name][:, x * wide + base + a * V:x * wide + base + b * V]
 
     def node(x, e):
-        I = lambda n, w=1, sub=None: blk("si", x, e, n, w, sub)
-        K = lambda n: "%s.%d.%d" % (n, x, e)
-        W = lambda a, b: T["wl%d" % x][:, e * 128 + a * V: e * 128 + b * V]
-        O = lambda a, b: T["off%d" % x][:, e * 128 + a * V: e * 128 + b * V]
-        B, kR, knR, kc0, kc1 = "Ps%d" % x, "R.%d" % x, "nR.%d" % x, "c0.%d" % x, "c1.%d" % x
-        ts(I("h"), I("M"), 1, None, ALU.arith_shift_right, None, [K("M")], [K("h")])
-        ts(I("sg"), pblk(x, "LOW", 1, 2), 2.0, -1.0, ALU.mult, ALU.add, [kR, B], [K("sg")])
-        tt(I("d"), I("sg"), I("h"), ALU.mult, [K("sg"), K("h")], [K("d")])
-        tt(W(1, 2), W(0, 1), I("d"), ALU.add, [K("m"), K("d")], [K("w1")])
-        tt(pblk(x, "COL", 0, 1), W(0, 1), T.lo_s[:, x * V:(x + 1) * V], ALU.add, [K("m"), "lo", B], [kc0])
-        tt(pblk(x, "COL", 1, 2), pblk(x, "COL", 0, 1), I("d"), ALU.add, [kc0, K("d"), B], [kc1])
-        cp(O(1, 2), pblk(x, "COL", 1, 2), [kc1, B], [K("off1")])
-        if e == 0:
-            cp(O(0, 1), pblk(x, "COL", 0, 1), [kc0, B], [K("off0")])
-        tt(I("MS", 2, 1), I("M"), I("h"), ALU.subtract, [K("M"), K("h")], [K("X")])
-        ts(I("h2", 2), I("MS", 2), 1, None, ALU.arith_shift_right, None, [K("s"), K("X")], [K("h2")], 2 * V)
-        ts(pblk(x, "LOW", 0, 1), pblk(x, "LOW", 1, 2), -1.0, 1.0, ALU.mult, ALU.add, [kR, B], [knR])
-        tt(I("lm2", 2), pblk(x, "LOW"), I("MS", 2), ALU.mult, [kR, knR, K("s"), K("X"), B], [K("lm2")], 2 * V)
-        tt(I("R2", 2, 0), I("lm2", 2, 0), I("h"), ALU.is_gt, [K("lm2"), K("h")], [K("R2a")])
-        tt(I("R2", 2, 1), I("lm2", 2, 1), I("h"), ALU.is_gt, [K("lm2"), K("h")], [K("R2b")])
-        ts(pblk(x, "sg2"), I("R2", 2), 2.0, -1.0, ALU.mult, ALU.add, [K("R2a"), K("R2b"), B], ["sg2.%d" % x], 2 * V)
-        tt(I("d2", 2), pblk(x, "sg2"), I("h2", 2), ALU.mult, ["sg2.%d" % x, K("h2"), B], [K("d2")], 2 * V)
-        tt(W(2, 4), W(0, 2), I("d2", 2), ALU.add, [K("m"), K("w1"), K("d2")], [K("w2")], 2 * V)
-        tt(I("o2", 2), pblk(x, "COL"), I("d2", 2), ALU.add, [K("d2"), kc0, kc1, B], [K("o2")], 2 * V)
-        cp(O(2, 4), I("o2", 2), [K("o2")], [K("off2")], 2 * V)
-        tt(I("dd"), I("d2", 2, 1), I("d2", 2, 0), ALU.subtract, [K("d2")], [K("dd")])
+        p0 = 0 if e == 0 else 1
+        K = lambda n: "%s.%d" % (n, x)
+        R = lambda name, a, n=1: rec(name, x, a, n)
+        W = lambda a: blk("wr", x, a, a + 1)
+        mb, h, sb, xb, m, d = R("mo", 1), R("mo", 3), R("mr", 4), R("mr", 14), R("do", 2), tmp("ti", 0, x)
+        d2 = lambda a, b: T.d2[:, x * V:(x + 1) * V, a:b]
+        sg = lambda a, q: T.pv[:, x * 256 + a:x * 256 + 2 * V:q]
+        tt(xb, mb, h, ALU.subtract, [K("mh")], [K("xb")])
+        tt(tmp("tf", 0, x), sb, h, ALU.subtract, [K("mh"), K("sb")], [K("t2l")])
+        tt(tmp("tf", 1, x), xb, h, ALU.subtract, [K("mh"), K("xb")], [K("t2w")])
+        tt(d, R("xo", 4), mb, ALU.mult, [K("sg"), K("mh")], [K("d")])
+        tt(sg(0, 2), R("xo", 3), tmp("tf", 0, x), ALU.min, [K("sg"), K("t2l")], [K("sgl"), K("acc")])
+        tt(sg(1, 2), R("xo", 4), tmp("tf", 1, x), ALU.min, [K("sg"), K("t2w")], [K("sgw"), K("acc2")])
+        tt(W(2), m, d, ALU.add, [K("m"), K("d")], [K("w")])
+        tt(d2(0, 2), sg(0, 1), R("mr", 4, 2), ALU.mult, [K("sgl"), K("sgw"), K("sb"), K("xb"), K("acc"), K("acc2")], [K("d2")])
+        tt(W(1), m, d2(0, 1), ALU.add, [K("m"), K("d2")], [K("wl")])
+        tt(W(3), W(2), d2(1, 2), ALU.add, [K("w"), K("d2")], [K("ww")])
+        n = (4 - p0) * V
+        kw = [K("w"), K("wl"), K("ww")] + ([] if e else [K("w0")])
+        mms([(T.pp[:, 0:n], T.permq[:], blk("wr", x, p0, 4), True, True)], 4 * n, kw + ["perm"], ["Pp"])
+        cp(T["off%d" % x][:, p0 * V:4 * V], T.pp[:, 0:n], ["Pp"], [K("off")], n)
+        tt(blk("wt", x, p0, 4), blk("wr", x, p0, 4), blk("pv", x, p0, 4, 128, 256), ALU.subtract, kw + [K("lo4")], [K("wt")], n)
+        tt(R("dr", 0), d2(1, 2), d2(0, 1), ALU.subtract, [K("d2")], [K("dd")])
+        cp(R("dr", 1), d2(0, 1), [K("d2")], [K("dl")])
         if e < NE - 1:
-            tt(I("dM"), I("MS", 2, 1), I("MS", 2, 0), ALU.subtract, [K("s"), K("X")], [K("dM")])
-            tt(I("dh"), I("h2", 2, 1), I("h2", 2, 0), ALU.subtract, [K("h2")], [K("dh")])
-            tt(I("dY"), I("dM"), I("dh"), ALU.subtract, [K("dM"), K("dh")], [K("dY")])
-            tt(I("XN"), I("MS", 2, 0), I("h2", 2, 0), ALU.subtract, [K("s"), K("h2")], [K("XN")])
-            tt(I("YN"), I("XN"), I("h"), ALU.subtract, [K("XN"), K("h")], [K("YN")])
+            tt(R("mr", 0), xb, sb, ALU.subtract, [K("xb"), K("sb")], [K("dm")])
+            ts(R("mr", 16), h, -0.5, None, ALU.add, None, [K("mh")], [K("hb")])
+
+    nbank = [0]
+
+    def bank():
+        k = nbank[0] % NPA
+        nbank[0] += 1
+        return k
 
     def start(x):
-        I = lambda n, w=1, sub=None: blk("si", x, 0, n, w, sub)
-        K = lambda n: "%s.%d.0" % (n, x)
-        n = T.n_s[:, x * V:(x + 1) * V]
-        lo = T.lo_s[:, x * V:(x + 1) * V]
-        ts(I("MS", 2, 0), n, 1, None, ALU.arith_shift_right, None, ["n"], [K("s")])
-        tt(I("M"), n, I("MS", 2, 0), ALU.subtract, ["n", K("s")], [K("M")])
-        cp(T["wl%d" % x][:, 0:V], I("MS", 2, 0), [K("s")], [K("m")])
-        tt(pblk(x, "LOW", 1, 2), I("M"), I("MS", 2, 0), ALU.is_gt, [K("M"), K("s"), "Ps%d" % x], ["R.%d" % x])
-        tt(I("oe"), n, lo, ALU.add, ["n", "lo"], [K("oe")])
-        cp(T["eo%d" % x][:, 0:V], lo, ["lo"], ["e0.%d" % x])
-        cp(T["eo%d" % x][:, V:2 * V], I("oe"), [K("oe")], ["en.%d" % x])
+        K = lambda n: "%s.%d" % (n, x)
+        R = lambda name, a, n=1: rec(name, x, a, n)
+        n, lo = cols("nq", x), cols("loq", x)
+        I = lambda k: tmp("ti", k, x)
+        tt(tmp("tf", 3, x), cols("n_s", x), cols("lo_s", x), ALU.add, ["n", "lo"], [K("f3")])
+        cp(T["eo%d" % x][:, 0:V], cols("lo_s", x), ["lo"], [K("e0")])
+        cp(T["eo%d" % x][:, V:2 * V], tmp("tf", 3, x), [K("f3")], [K("en")])
+        ts(I(1), n, 1, None, ALU.arith_shift_right, None, ["nq"], [K("i1")])
+        tt(I(2), n, I(1), ALU.subtract, ["nq", K("i1")], [K("i2")])
+        ts(I(3), I(2), 1, None, ALU.arith_shift_right, None, [K("i2")], [K("i3")])
+        ts(R("mr", 4), I(1), -0.5, None, ALU.add, None, [K("i1")], [K("sb")])
+        ts(R("mo", 1), I(2), -0.5, None, ALU.add, None, [K("i2")], [K("a0")])
+        cp(R("mo", 3), I(3), [K("i3"), K("a0")], [K("mh")])
+        tt(tmp("tf", 2, x), I(2), I(1), ALU.subtract, [K("i1"), K("i2")], [K("ud")])
+        ts(R("xo", 3), tmp("tf", 2, x), -1.0, 0.5, ALU.mult, ALU.add, [K("ud")], [K("a2")])
+        ts(R("xo", 4), tmp("tf", 2, x), -0.5, None, ALU.add, None, [K("ud"), K("a2")], [K("sg")])
+        tt(R("do", 2), I(1), lo, ALU.add, [K("i1"), "loq"], [K("m")])
+        cp(blk("wr", x, 0, 1), R("do", 2), [K("m")], [K("w0")])
+        for p in range(4):
+            cp(blk("pv", x, p, p + 1, 128, 256), lo, ["loq"] + ([K("lo4")] if p else []), [K("lo4")])
+        k = bank()
+        mms([(T["pa%d" % k][:, :, a], fx(a), cols("nh", x), True, True) for a in range(16)], 64,
+            ["f%d" % a for a in range(16)] + ["nh"], ["Pa%d" % k])
+        act(T["nw%d" % x][:], T["pa%d" % k][:], ACT.Copy, ["Pa%d" % k], [K("nw")], 512)
         node(x, 0)
 
-    def spread_n(x):
-        n = T.n_s[:, x * V:(x + 1) * V]
-        for p in range(4):
-            cp(T["n4l%d" % x][:, p * V:(p + 1) * V], n, ["n"], ["n4l.%d.%d" % (x, p)])
-        for k in range(4):
-            mms([(T["pa%d" % k][:, c - 4 * k, :], T.fexp[:, c * 128:(c + 1) * 128], T["n4l%d" % x][:], True, True)
-                 for c in range(4 * k, 4 * k + 4)], 128,
-                ["f%d" % c for c in range(4 * k, 4 * k + 4)] + ["n4l.%d.%d" % (x, p) for p in range(4)], ["Pa%d" % k])
-            act(T["n4_%d" % x][:, 4 * k:4 * k + 4, :], T["pa%d" % k][:], ACT.Copy, ["Pa%d" % k], ["n4.%d.%d" % (x, k)], 512)
-
     def advance(x, e):
+        K = lambda n: "%s.%d" % (n, x)
+        R = lambda name, a, n=1: rec(name, x, a, n)
+        i = NP * e + x
         p0 = 0 if e == 0 else 1
         n = (4 - p0) * V
-        last = e == NE - 1
-        I = lambda n, w=1, sub=None: blk("si", x, e, n, w, sub)
-        F = lambda n, w=1, sub=None: blk("sf", x, e, n, w, sub)
-        K = lambda n: "%s.%d.%d" % (n, x, e)
-        J = lambda n, w=1, sub=None: blk("si", x, e + 1, n, w, sub)
-        L = lambda n: "%s.%d.%d" % (n, x, e + 1)
-        i = 2 * e + x
-        B, kR, kg = "Ps%d" % x, "R.%d" % x, K("G")
-        ps = T["ps%d" % x][:, 0:n]
-        slot = lambda k: T.land[:, (3 * i + k) * 128:(3 * i + k) * 128 + n]
-        m = T["wl%d" % x][:, e * 128:e * 128 + V]
-        G = lambda p: F("G", 4, p)
-        base = (e * NF + p0) * V
-        tt(ps, ps, slot(0), ALU.add, [B, "arr%d" % i], [B], n)
-        tt(ps, ps, slot(1), ALU.add, [B], [B], n)
-        tt(T["sf%d" % x][:, base:base + n], ps, slot(2), ALU.add, [B], [kg], n)
-        if e > 0:
-            gm, kgm = blk("sf", x, e - 1, "gm2"), "gm2.%d.%d" % (x, e - 1)
-        else:
-            gm, kgm = G(0), kg
-        gout, kgout = (T.og[:, x * V:(x + 1) * V], "og%d" % x) if last else (F("gm2"), K("gm2"))
-        mout, kmout = (T.om[:, x * V:(x + 1) * V], "om%d" % x) if last else \
-            (T["wl%d" % x][:, (e + 1) * 128:(e + 1) * 128 + V], L("m"))
-        tt(I("up1"), G(1), gm, ALU.is_gt, [kg, kgm], [K("up1")])
-        tt(I("t4"), I("up1"), I("d"), ALU.mult, [K("up1"), K("d")], [K("t4")])
-        tt(F("gm1"), G(1), gm, ALU.max, [kg, kgm], [K("gm1")])
-        tt(F("dg"), G(3), G(2), ALU.subtract, [kg], [K("dg")])
-        tt(F("t1"), I("up1"), F("dg"), ALU.mult, [K("up1"), K("dg")], [K("t1")])
-        tt(F("g2"), G(2), F("t1"), ALU.add, [kg, K("t1")], [K("g2")])
-        tt(I("t3"), I("up1"), I("dd"), ALU.mult, [K("up1"), K("dd")], [K("t3")])
-        tt(I("d1"), I("d2", 2, 0), I("t3"), ALU.add, [K("d2"), K("t3")], [K("d1")])
-        tt(I("up2"), F("g2"), F("gm1"), ALU.is_gt, [K("g2"), K("gm1")], [K("up2")])
-        tt(I("m1"), m, I("t4"), ALU.add, [K("m"), K("t4")], [K("m1")])
-        tt(I("t6"), I("up2"), I("d1"), ALU.mult, [K("up2"), K("d1")], [K("t6")])
-        tt(gout, F("g2"), F("gm1"), ALU.max, [K("g2"), K("gm1")], [kgout])
-        tt(mout, I("m1"), I("t6"), ALU.add, [K("m1"), K("t6")], [kmout])
-        if last:
+        slot = lambda k, a, b: T.land[:, (3 * i + k) * 128 + a * V:(3 * i + k) * 128 + b * V]
+        acc = lambda a, b: blk("pv", x, a, b, 0, 256)
+        gm, g1, g3 = tmp("tf", 4, x), blk("gt", x, 0, 1, 0, 64), blk("gt", x, 1, 2, 0, 64)
+        tt(acc(p0, 4), T.sendb[:, i * 128 + p0 * V:(i + 1) * 128], slot(0, p0, 4), ALU.add, ["snd%d" % i, "arr%d.0" % i], [K("acc"), K("acc2")], 2 * n)
+        tt(acc(p0, 4), acc(p0, 4), slot(1, p0, 4), ALU.add, [K("acc"), "arr%d.1" % i], [K("acc")], n)
+        if e == 0:
+            tt(gm, acc(0, 1), slot(2, 0, 1), ALU.add, [K("acc"), "arr%d.2" % i], [K("gm")])
+        tt(blk("gt", x, 0, 2, 0, 64), acc(2, 4), slot(2, 2, 4), ALU.add, [K("acc"), "arr%d.2" % i], [K("G")])
+        tt(R("gr", 1), acc(1, 2), slot(2, 1, 2), ALU.add, [K("acc"), "arr%d.2" % i], [K("G2")])
+        u1, u2, ud = R("ur", 20), R("ur", 40), tmp("tf", 2, x)
+        tt(u1, g1, gm, ALU.is_gt, [K("G"), K("gm")], [K("u1")])
+        tt(R("gr", 3), g1, gm, ALU.max, [K("G"), K("gm")], [K("gm1")])
+        tt(R("gr", 0), g3, R("gr", 1), ALU.subtract, [K("G"), K("G2")], [K("dg")])
+        scan(R("so", 0, 4), R("ur", 5, 4), R("gr", 0, 4), ALU.subtract, [K("u1"), K("gm1"), K("dg"), K("G2")] + consts, [K("so")], 4 * V)
+        tt(ud, u1, tmp("ti", 0, x), ALU.mult, [K("u1"), K("d")], [K("ud")])
+        tt(R("dr", 2), R("do", 2), ud, ALU.add, [K("m"), K("ud")], [K("m1")])
+        ts(u2, R("so", 3), 0.0, None, ALU.is_gt, None, [K("so")], [K("u2")])
+        scan(R("do", 0, 3), R("ur", 0, 3), R("dr", 0, 3), ALU.add,
+             [K("u1"), K("u2"), K("dd"), K("dl"), K("m1")] + consts, [K("m"), K("d1")], 3 * V)
+        if e == NE - 1:
+            tt(blk("oq", x, 0, 1, 0, 64), R("so", 2), R("gr", 3), ALU.max, [K("so"), K("gm1")], [K("og")])
+            tt(blk("oq", x, 1, 2, 0, 64), R("do", 2), cols("loq", x), ALU.subtract, [K("m"), "loq"], [K("om")])
+            mms([(T.pp[:, 0:64], T.permq[:], blk("oq", x, 0, 2, 0, 64), True, True)], 256, [K("og"), K("om"), "perm"], ["Pp"])
+            cp(blk("ol", x, 0, 2, 0, 64), T.pp[:, 0:64], ["Pp"], [K("ol")])
             return
-        tt(I("t2"), I("up1"), I("dh"), ALU.mult, [K("up1"), K("dh")], [K("t2")])
-        tt(J("MS", 2, 0), I("h2", 2, 0), I("t2"), ALU.add, [K("h2"), K("t2")], [L("s")])
-        ts(I("R1"), I("d1"), 0.0, None, ALU.is_gt, None, [K("d1")], [K("R1")])
-        tt(I("t7"), I("up1"), I("dY"), ALU.mult, [K("up1"), K("dY")], [K("t7")])
-        tt(I("Y"), I("YN"), I("t7"), ALU.add, [K("t7"), K("YN")], [K("Y")])
-        tt(I("low"), I("up2"), I("R1"), ALU.is_equal, [K("up2"), K("R1")], [K("low")])
-        tt(I("t5"), I("up2"), I("Y"), ALU.mult, [K("up2"), K("Y")], [K("t5")])
-        tt(J("M"), I("h"), I("t5"), ALU.add, [K("h"), K("t5")], [L("M")])
-        tt(I("lm"), I("low"), J("M"), ALU.mult, [K("low"), L("M")], [K("lm")])
-        tt(pblk(x, "LOW", 1, 2), I("lm"), J("MS", 2, 0), ALU.is_gt, [K("lm"), L("s"), B], [kR])
+        tt(gm, R("so", 2), R("gr", 3), ALU.max, [K("so"), K("gm1")], [K("gm")])
+        scan(R("ao", 0, 5), R("ur", 8, 5), R("mr", 0, 5), ALU.add, [K("u1"), K("dm"), K("sb"), K("hb")] + consts, [K("a1")], 5 * V)
+        ts(tmp("tf", 3, x), R("so", 3), 0.0, 0.5, ALU.is_le, ALU.subtract, [K("so")], [K("nv")])
+        tt(R("mr", 11), R("ao", 1), R("ao", 4), ALU.subtract, [K("a1")], [K("y")])
+        ts(R("mr", 4), R("ao", 3), -0.5, None, ALU.add, None, [K("a1")], [K("sb")])
+        scan(R("mo", 0, 4), R("ur", 25, 4), R("mr", 11, 4), ALU.add, [K("u2"), K("y"), K("hb")] + consts, [K("mh")], 4 * V)
+        tt(R("xb", 1), R("ao", 3), R("mo", 1), ALU.subtract, [K("a1"), K("mh")], [K("nt")])
+        tt(R("xa", 1), R("do", 1), tmp("tf", 3, x), ALU.mult, [K("d1"), K("nv")], [K("q")])
+        scan(R("xo", 0, 5), R("xa", 0, 5), R("xb", 0, 5), ALU.max, [K("q"), K("nt")] + consts, [K("sg")], 5 * V)
         node(x, e + 1)
 
-    def rise(x, turn, bank):
-        ends = lambda a: T.win[:, 0:WC].indirect(T["eo%d" % x][:, a * V:(a + 1) * V])
-        at = lambda b, c: T[b][:, c // 4, c % 4 * V:(c % 4 + 1) * V]
-        s0, sn, b4 = T["s0_%d" % x], T["sn_%d" % x], T["b4_%d" % x]
-        act(s0[:], ends(0), ACT.Copy, ["win", "e0.%d" % x], ["s0.%d" % x], 512 * GAM)
-        mms([(at(turn, c), T.ident[:], s0[:, c:512:16], True, True) for c in range(16)], 64,
-            ["s0.%d" % x, "id"], ["P" + turn[1:]])
-        act(T["s0c%d" % x][:], T[turn][:], ACT.Copy, ["P" + turn[1:]], ["s0c.%d" % x], 512)
-        if bank is None:
-            cp(sn[:], ends(1), ["win", "en.%d" % x], ["sn.%d" % x], 512 * GAM)
-            keys = ["b4a.%d.%d" % (x, c) for c in range(16)]
-            for c in range(16):
-                tt(b4[:, c, 0:V], sn[:, c:512:16], s0[:, c:512:16], ALU.subtract, ["sn.%d" % x, "s0.%d" % x], [keys[c]])
-        else:
-            act(sn[:], ends(1), ACT.Copy, ["win", "en.%d" % x], ["sn.%d" % x], 512 * GAM)
-            calls = []
-            for c in range(16):
-                calls.append((at(bank, c), T.ident[:], sn[:, c:512:16], True, False))
-                calls.append((at(bank, c), T.nident[:], s0[:, c:512:16], False, True))
-            mms(calls, 64, ["sn.%d" % x, "s0.%d" % x, "id", "nid"], ["P" + bank[1:]])
-            keys = ["b4a.%d" % x]
-            cp(b4[:, :, 0:V], T[bank][:], ["P" + bank[1:]], keys, 512)
-        cp(b4[:, :, V:2 * V], b4[:, :, 0:V], keys, ["b4b.%d" % x], 256)
-        cp(b4[:, :, 2 * V:4 * V], b4[:, :, 0:2 * V], keys + ["b4b.%d" % x], ["b4.%d" % x], 512)
+    def gather(off):
+        return T.win[:, 0:WC].indirect(off)
+
+    GC = 512 * GAM + 64
+
+    def rise(x):
+        s0, ri, eo = T["s0_%d" % x], T["ri%d" % x], T["eo%d" % x]
+        act(s0[:], gather(eo[:, 0:V]), ACT.Copy, ["win", "e0.%d" % x], ["s0.%d" % x], GC)
+        tt(ri[:], gather(eo[:, V:2 * V]), s0[:], ALU.subtract, ["win", "en.%d" % x, "s0.%d" % x], ["ri.%d" % x], GC)
 
     def gains(x, e):
         p0 = 0 if e == 0 else 1
-        P = 4 - p0
-        n = P * V
-        K = lambda nm: "%s.%d.%d" % (nm, x, e)
+        n = (4 - p0) * V
+        i = NP * e + x
+        K = lambda nm: "%s.%d" % (nm, x)
+        st, off, qb = T["st%d" % x], T["off%d" % x], T["qb%d" % x]
         for p in range(p0, 4):
-            act(T["st%d" % x][:, (p - p0) * 512:(p - p0 + 1) * 512],
-                T.win[:, 0:WC].indirect(T["off%d" % x][:, e * 128 + p * V:e * 128 + (p + 1) * V]), ACT.Copy,
-                ["win", K("off%d" % min(p, 2))], ["st.%d.%d" % (x, p - p0)], 512 * GAM,
-                len(steps) - 1 if p > p0 else None)
-        rhs = T["wl%d" % x][:, e * 128 + p0 * V:(e + 1) * 128]
+            if (x, e, p) in VGATHER:
+                cp(st[:, 512 * p:512 * p + 512], gather(off[:, p * V:p * V + V]), ["win", K("off")], [K("st%d" % p)], GC)
+            else:
+                act(st[:, 512 * p:512 * p + 512], gather(off[:, p * V:p * V + V]), ACT.Copy, ["win", K("off")], [K("st%d" % p)], GC)
         for k in range(4):
-            cs = range(4 * k, 4 * k + 4)
-            pt = T["pt%d" % (k % 2)]
-            mms([(pt[:, c - 4 * k, 0:n], T.fexp[:, c * 128:(c + 1) * 128], rhs, True, True) for c in cs], n,
-                [K("m"), K("w1"), K("w2")] + ["f%d" % c for c in cs], ["Pt%d" % (k % 2)])
-            tt(T.qbuf[:, 4 * k:4 * k + 4, 0:n], pt[:, :, 0:n], T["b4_%d" % x][:, 4 * k:4 * k + 4, 0:n], ALU.mult,
-               ["Pt%d" % (k % 2), "b4.%d" % x], ["q%d" % k], 4 * n)
-        for k in range(4):
-            cs = range(4 * k, 4 * k + 4)
-            kb = "Pa%d" % k
-            bank = T["pa%d" % k]
-            pa = bank[:, :, 0:n]
-            mms([(bank[:, :, p * V:(p + 1) * V], T.nident[:], T["s0c%d" % x][:, 4 * k:4 * k + 4, :], p == 0, False)
-                 for p in range(P)], 128, ["s0c.%d" % x, "nid"], [kb])
-            mms([(bank[:, c - 4 * k, 0:n], T.ident[:], T["st%d" % x][:, c:16 * n:16], False, c == 4 * k + 3) for c in cs], n,
-                ["st.%d.%d" % (x, p) for p in range(P)] + ["id"], [kb])
-            tt(pa, pa, T["n4_%d" % x][:, 4 * k:4 * k + 4, 0:n], ALU.mult, [kb, "n4.%d.%d" % (x, k)], [kb], 4 * n)
-            tt(pa, pa, T.qbuf[:, 4 * k:4 * k + 4, 0:n], ALU.subtract, [kb, "q%d" % k], [kb], 4 * n)
-            for a, b in ([(0, 2), (2, 4)] if k == 3 else [(0, 4)]):
-                ca = range(4 * k + a, 4 * k + b)
-                act(T.absd[:, 4 * k + a:4 * k + b, 0:n], bank[:, a:b, 0:n], ACT.Abs, [kb], ["ab%d" % c for c in ca], (b - a) * n)
-                mms([(T["ps%d" % x][:, 0:n], T.zsum[:, 15 - c:143 - c], T.absd[:, c, 0:n], c == 0, c == 15) for c in ca],
-                    4 * n, ["ab%d" % c for c in ca] + ["z"], ["Ps%d" % x])
-        i = 2 * e + x
-        src = T.sendb[:, i * 128:i * 128 + n]
-        act(src, T["ps%d" % x][:, 0:n], ACT.Copy, ["Ps%d" % x], ["snd%d" % i], n)
+            pt, kt = T["pt%d" % (k % 2)], "Pt%d" % (k % 2)
+            mms([(pt[:, p0 * V:4 * V, c], fx(4 * c + k), blk("wt", x, p0, 4), True, True) for c in range(4)], n,
+                [K("wt")] + ["f%d" % (4 * c + k) for c in range(4)], [kt])
+            for p in range(p0, 4):
+                tt(qb[:, 512 * p + k:512 * p + 512:4], pt[:, p * V:p * V + V, :], T["ri%d" % x][:, k:512:4], ALU.mult,
+                   [kt, K("ri")], [K("q%d.%d" % (p, k))], 128)
+        for p in range(p0, 4):
+            b = bank()
+            pa, kb, ab = T["pa%d" % b], "Pa%d" % b, T["ab%d" % b]
+            mms([(pa[:], T.nident[:], T["s0_%d" % x][:], True, False)], 512, [K("s0"), "nid"], [kb])
+            mms([(pa[:], T.ident[:], st[:, 512 * p:512 * p + 512], False, True)], 512, [K("st%d" % p), "id"], [kb])
+            tt(pa[:], pa[:], T["nw%d" % x][:], ALU.mult, [kb, K("nw")], [kb], 512)
+            tt(pa[:], pa[:], qb[:, 512 * p:512 * p + 512], ALU.subtract, [kb] + [K("q%d.%d" % (p, k)) for k in range(4)], [kb], 512)
+            for c in range(4):
+                act(ab[:, 128 * c:128 * c + 128], pa[:, :, 4 * c:4 * c + 4], ACT.Abs, [kb], ["ab%d.%d" % (b, c)], 128)
+            mms([(T.ps[:, 32 * p + 8 * k:32 * p + 8 * k + 8], ab[:, k:512:4], T.bsel[:], True, True) for k in range(4)], 256,
+                ["ab%d.%d" % (b, c) for c in range(4)] + ["bsel"], ["Ps"])
+        src = T.sendb[:, i * 128 + p0 * V:(i + 1) * 128]
+        add("v", [lambda: g.vector.transpose(src, T.ps[:, p0 * V:128])], n * CYC, ["Ps"], ["snd%d" % i])
         ids, dsts = [], []
         for q in peers:
             rid, pid, _se = topo.addr(cores[q])
-            k = (rank - q - 1) % nr
+            k = (q - rank - 1) % nr
             ids.append(DstId(rid=rid, pnc=pid))
-            dsts.append(T.land[:, (3 * i + k) * 128:(3 * i + k) * 128 + n])
+            dsts.append(T.land[:, (3 * i + k) * 128 + p0 * V:(3 * i + k + 1) * 128])
         add("g", [lambda: g.remote_dma_fused(
-            [RemoteDMATransfer(dst_ids=ids, dma_engine_mask=emask, remote_sem=T.sem["arr%d" % i], src=src, dsts=dsts)],
-            local_sem=T.sem.sent)], 0.5, ["snd%d" % i], ["arr%d" % i], LINK, ("arr%d" % i, neng * len(peers)))
+            [RemoteDMATransfer(dst_ids=ids, dma_engine_mask=emask, remote_sem=T.sem["arr%d_%d" % (i, rank)], src=src, dsts=dsts)],
+            local_sem=T.sem.sent)], 0.5, ["snd%d" % i], ["out%d" % i], 0.0, ("sent", 0))
+        for k in range(nr - 1):
+            add("x", [lambda: None], 0.0, ["out%d" % i], ["arr%d.%d" % (i, k)], LINK * (k + 4) / 6,
+                ("arr%d_%d" % (i, (rank - k - 1) % nr), neng))
 
-    spread_n(0)
-    start(0)
-    spread_n(1)
-    start(1)
-    phase[0] = 0
-    rise(0, "pa3", None)
-    gains(0, 0)
-    phase[0] = 0.5
-    rise(1, "pt1", "pt0")
-    phase[0] = 1
-    gains(1, 0)
+    for x in range(NP):
+        start(x)
+    for x in range(NP):
+        phase[0] = x - 0.5
+        rise(x)
+        phase[0] = x
+        gains(x, 0)
     for e in range(1, NE):
-        for x in range(2):
-            phase[0] = 2 * e + x
+        for x in range(NP):
+            phase[0] = NP * e + x
             advance(x, e - 1)
             gains(x, e)
-    for x in range(2):
-        phase[0] = 2 * NE + x
+    for x in range(NP):
+        phase[0] = NP * NE + x
         advance(x, NE - 1)
-        dma("a", g.scalar, T.yg[:, x * V:(x + 1) * V], T.og[:, x * V:(x + 1) * V], "st_a", 32, 2.0, ["og%d" % x], [])
-        dma("s", g.sync, T.ym[:, x * V:(x + 1) * V], T.om[:, x * V:(x + 1) * V], "st_s", 32, 2.0, ["om%d" % x], [])
+        dma("a", g.scalar, cols("yg", x), blk("ol", x, 0, 1, 0, 64), "st_a", 16 * NP, 2.0, ["ol.%d" % x], [])
+        dma("s", g.sync, cols("ym", x), blk("ol", x, 1, 2, 0, 64), "st_s", 16 * NP, 2.0, ["ol.%d" % x], [])
 
     ns = len(steps)
     succ = [[] for _ in range(ns)]
@@ -377,41 +382,72 @@ def rank_program(g, core, T, topo):
 
     def waits(j, i):
         raw = steps[i]["deps"][j]
-        return not (raw is None or (steps[j]["e"] == "t" and steps[i]["e"] == "t" and not raw))
+        return not (raw is None or (steps[j]["e"] == steps[i]["e"] and steps[i]["e"] in "t" and not raw))
 
     def gap(j, i):
         if not waits(j, i):
             return 0.0
         return steps[j]["lat"] + (SAME if steps[j]["e"] == steps[i]["e"] else HOP)
 
-    way = [0.0] * ns
-    for i in range(ns - 1, -1, -1):
-        way[i] = steps[i]["cost"] + max([steps[i]["lat"]] + [gap(i, j) + way[j] for j in succ[i]])
-    left = [len(s["deps"]) for s in steps]
-    can = [0.0] * ns
-    ready = {e: [] for e in "vatgs"}
-    free = {e: 0.0 for e in "vatgs"}
-    for i in range(ns):
-        if left[i] == 0:
-            ready[steps[i]["e"]].append(i)
-    order = []
-    while len(order) < ns:
+    cost = [s["cost"] for s in steps]
+    into = [[(j, gap(j, i)) for j in steps[i]["deps"]] for i in range(ns)]
+    outof = [[(j, gap(i, j)) for j in succ[i]] for i in range(ns)]
+
+    def place(seq, back):
+        busy = {e: [] for e in "vatgsx"}
+        at = [0.0] * ns
+        for i in seq:
+            c = cost[i]
+            t = steps[i]["lat"] if back else 0.0
+            for j, d in (outof[i] if back else into[i]):
+                t = max(t, at[j] + cost[j] + d)
+            line = busy[steps[i]["e"]]
+            k = len(line)
+            while k > 0 and line[k - 1][1] > t:
+                k -= 1
+            while k < len(line) and line[k][0] < t + c - 1e-9:
+                t = max(t, line[k][1])
+                k += 1
+            line.insert(k, (t, t + c))
+            at[i] = t
+        return at
+
+    def greedy(way):
+        left = [len(s["deps"]) for s in steps]
+        can = [0.0] * ns
+        at = [0.0] * ns
+        ready = {e: [] for e in "vatgsx"}
+        free = {e: 0.0 for e in "vatgsx"}
+        for i in range(ns):
+            if left[i] == 0:
+                ready[steps[i]["e"]].append(i)
+        for _ in range(ns):
+            t0, e = min((max(free[e], min(can[i] for i in ready[e])), e) for e in ready if ready[e])
+            i = max([j for j in ready[e] if can[j] <= t0 + SLACK], key=lambda j: (-steps[j]["w"], way[j], -j))
+            ready[e].remove(i)
+            at[i] = max(t0, can[i])
+            free[e] = at[i] + cost[i]
+            for j, d in outof[i]:
+                can[j] = max(can[j], free[e] + d)
+                left[j] -= 1
+                if left[j] == 0:
+                    ready[steps[j]["e"]].append(j)
+        return at
+
+    if not ORDER:
+        way = [0.0] * ns
+        for i in range(ns - 1, -1, -1):
+            way[i] = cost[i] + max([steps[i]["lat"]] + [d + way[j] for j, d in outof[i]])
+        at = greedy(way)
         best = None
-        for e in "vatgs":
-            if ready[e]:
-                t0 = max(free[e], min(can[i] for i in ready[e]))
-                if best is None or t0 < best[0]:
-                    best = (t0, e)
-        t0, e = best
-        i = max([j for j in ready[e] if can[j] <= t0 + SLACK], key=lambda j: (-steps[j]["w"], way[j], -j))
-        ready[e].remove(i)
-        free[e] = max(t0, can[i]) + steps[i]["cost"]
-        order.append(i)
-        for j in succ[i]:
-            can[j] = max(can[j], free[e] + gap(i, j))
-            left[j] -= 1
-            if left[j] == 0:
-                ready[steps[j]["e"]].append(j)
+        for _ in range(ROUNDS + 1):
+            end = max(at[i] + cost[i] + steps[i]["lat"] for i in range(ns))
+            if best is None or end < best[0]:
+                best = (end, at)
+            back = place(sorted(range(ns), key=lambda i: (-(at[i] + cost[i]), -i)), True)
+            at = place(sorted(range(ns), key=lambda i: (-(back[i] + cost[i]), i)), False)
+        ORDER.extend(sorted(range(ns), key=lambda i: (best[1][i], i)))
+    order = ORDER
 
     queue = {"v": g.vector, "a": g.scalar, "t": g.tensor, "g": g, "s": g.sync}
     semof = {"v": "cv", "a": "ca", "t": "ct", "g": "cg"}
@@ -421,6 +457,9 @@ def rank_program(g, core, T, topo):
     for i in order:
         s = steps[i]
         e = s["e"]
+        if e == "x":
+            done[i] = s["event"]
+            continue
         want = {}
         for j in s["deps"]:
             if waits(j, i):
@@ -441,6 +480,6 @@ def rank_program(g, core, T, topo):
 
     for e in "vatg":
         g.wait_ge(T.sem[semof[e]], count[e])
-    g.wait_ge(T.sem.sent, neng * 2 * NE)
-    g.wait_ge(T.sem.st_a, 32)
-    g.wait_ge(T.sem.st_s, 32)
+    g.wait_ge(T.sem.sent, neng * NP * NE)
+    g.wait_ge(T.sem.st_a, 16 * NP)
+    g.wait_ge(T.sem.st_s, 16 * NP)

@@ -2,20 +2,28 @@ from concourse.bass import DstId, RemoteDMATransfer
 from concourse.mybir import AluOpType as ALU, ActivationFunctionType as ACT
 
 WC = 12288
-V = 32
-NP = 2
+WID = [32, 32]
+NP = len(WID)
 NE = 4
 NPA = 3
+NPT = 3
+SPLIT = True
+EARLY = True
 VGATHER = [(0, 0, 0)]
-CYC = 0.00085
-PEC = 0.00043
+ASIDE = ["hb", "sb", "nv"]
+CYC = 0.00083
+PEC = 0.00042
 GAM = 1.56
 LINK = 5.0
-HOP = 0.17
-SAME = 0.17
+STEP = 1.16
+HOP = 0.18
+SAME = 0.18
 SLACK = 0.05
 LOAD = 12.5
-ROUNDS = 0
+ROUNDS = 3
+GREEDY = False
+AHEAD = 0
+WG = 32
 ORDER = []
 MG = 12582912.0
 REC = {"ur": 60, "gr": 4, "mr": 20, "so": 4, "ao": 5, "mo": 4, "dr": 3, "do": 3, "xa": 5, "xb": 5, "xo": 5}
@@ -24,40 +32,42 @@ SCRATCH = {
     "win": ("sbuf", [128, WC], "bfloat16"),
     "lo_s": ("sbuf", [128, 64], "int32"),
     "n_s": ("sbuf", [128, 64], "int32"),
-    "lnf": ("sbuf", [128, 128], "float32"),
-    "loq": ("sbuf", [128, 64], "int32"),
+    "nf": ("sbuf", [128, 64], "float32"),
+    "lo4": ("sbuf", [128, NP * 128], "float32"),
     "nq": ("sbuf", [128, 64], "int32"),
     "nh": ("sbuf", [128, 64], "float16"),
     "im": ("sbuf", [128, 128], "int32"),
     "ig": ("sbuf", [128, 128], "int32"),
     "pi": ("sbuf", [128, 8], "int32"),
-    "pf": ("sbuf", [128, 8], "float32"),
+    "pf": ("sbuf", [128, 16], "float32"),
     "ident": ("sbuf", [128, 128], "bfloat16"),
     "nident": ("sbuf", [128, 128], "bfloat16"),
     "permq": ("sbuf", [128, 128], "float32"),
+    "permh": ("sbuf", [128, 128], "float16"),
     "permt": ("sbuf", [128, 128], "float32"),
+    "idf": ("sbuf", [128, 128], "float32"),
     "bsel": ("sbuf", [128, 8], "float32"),
     "boq": ("sbuf", [128, 128], "float16"),
     "mq": ("sbuf", [128, 16], "float32"),
     "fexp": ("sbuf", [128, 2048], "float16"),
     "land": ("sbuf", [128, NP * NE * 3 * 128], "float32"),
     "sendb": ("sbuf", [128, NP * NE * 128], "float32"),
-    "oq": ("sbuf", [128, 128], "float32"),
-    "ol": ("sbuf", [128, 128], "float32"),
-    "wr": ("sbuf", [128, 256], "float32"),
-    "wt": ("sbuf", [128, 256], "float16"),
-    "gt": ("sbuf", [128, 128], "float32"),
+    "ol": ("sbuf", [128, NP * 64], "float32"),
+    "wt": ("sbuf", [128, NP * 128], "float16"),
+    "gt": ("sbuf", [128, NP * 64], "float32"),
     "d2": ("sbuf", [128, 64, 2], "int32"),
+    "sg": ("sbuf", [128, 64, 2], "float32"),
     "ti": ("sbuf", [128, 4, 64], "int32"),
     "tf": ("sbuf", [128, 6, 64], "float32"),
     "ps": ("psum", [128, 512], "float32"),
     "pp": ("psum", [128, 512], "float32"),
-    "pv": ("psum", [128, 512], "float32"),
 }
 for _n in REC:
     SCRATCH[_n] = ("sbuf", [128, 65 * REC[_n]], "float32")
+for _k in range(NPT):
+    SCRATCH["pt%d" % _k] = ("psum", [128, 128, 4], "float32")
 for _k in range(NPA):
-    SCRATCH["pa%d" % _k] = ("psum", [128, V, 16], "float32")
+    SCRATCH["pa%d" % _k] = ("psum", [128, 128, 4], "float32")
     SCRATCH["ab%d" % _k] = ("sbuf", [128, 512], "float32")
 for _x in range(NP):
     SCRATCH["nw%d" % _x] = ("sbuf", [128, 512], "float32")
@@ -67,7 +77,6 @@ for _x in range(NP):
     SCRATCH["ri%d" % _x] = ("sbuf", [128, 512], "bfloat16")
     SCRATCH["eo%d" % _x] = ("sbuf", [128, 64], "uint16")
     SCRATCH["off%d" % _x] = ("sbuf", [128, 128], "uint16")
-    SCRATCH["pt%d" % _x] = ("psum", [128, 128, 4], "float32")
 
 SEMAPHORES = ["cv", "ca", "ct", "cg", "ld_lo", "ld_n", "ld_w", "sent", "st_s", "st_a"] + \
     ["arr%d_%d" % (_k, _r) for _k in range(NP * NE) for _r in range(4)]
@@ -136,9 +145,15 @@ def rank_program(g, core, T, topo):
     def act(out, a, f, reads, writes, n, after=None):
         return add("a", [lambda: g.scalar.activation(out, a, f)], max(64, n) * CYC, reads, writes, after=after)
 
+    def less_half(name, out, a, reads, writes):
+        if name in ASIDE:
+            add("a", [lambda: g.scalar.activation(out, a, ACT.Identity, T.pf[:, 7:8])], 64 * CYC, reads + ["half"], writes)
+        else:
+            ts(out, a, -0.5, None, ALU.add, None, reads, writes)
+
     def mms(calls, cyc, reads, writes):
         fns = [(lambda c=c: g.tensor.matmul(c[0], c[1], c[2], c[3], c[4])) for c in calls]
-        add("t", fns, len(calls) * max(64, cyc) * PEC, reads, writes)
+        add("t", fns, cyc * PEC, reads, writes)
 
     def dma(e, q, out, src, sem, val, lat, reads, writes, after=None):
         add(e, [lambda: q.dma_start(out, src).then_inc(T.sem[sem], 16)], 0.1, reads, writes, lat, (sem, val), after)
@@ -157,12 +172,16 @@ def rank_program(g, core, T, topo):
         ts(T.pi[:, k + 1:k + 2], T.pi[:, 0:1], val, None, alu, None, ["p"], ["p%d" % k])
     cp(T.pf[:, 0:5], T.pi[:, 0:5], ["p", "p0", "p1", "p2", "p3"], ["pf"])
     col = lambda k: T.pf[:, k:k + 1]
+    fill(col(7), -0.5, "half")
+    fill(col(8), 0.5, "half2")
     ts(col(5), col(1), 16.0, col(2), ALU.mult, ALU.add, ["pf"], ["lq"])
     ts(col(6), col(3), 8.0, col(4), ALU.mult, ALU.add, ["pf"], ["ql"])
     ts(T.permt[:], T.im[:], col(6), None, ALU.is_equal, None, ["im", "ql"], ["permt"], 128)
     ts(T.permq[:], T.im[:], col(5), None, ALU.is_equal, None, ["im", "lq"], ["perm"], 128)
+    ts(T.permh[:], T.im[:], col(5), None, ALU.is_equal, None, ["im", "lq"], ["permh"], 128)
     ts(T.ident[:], T.im[:], col(0), None, ALU.is_equal, None, ["im", "pf"], ["id"], 128)
     ts(T.nident[:], T.im[:], col(0), -1.0, ALU.is_equal, ALU.mult, ["im", "pf"], ["nid"], 128)
+    ts(T.idf[:], T.im[:], col(0), None, ALU.is_equal, None, ["im", "pf"], ["idf"], 128)
     ts(T.bsel[:], T.im[:, 0:8], col(4), None, ALU.is_equal, None, ["im", "pf"], ["bsel"])
     ts(T.mq[:], T.im[:, 0:16], col(2), None, ALU.is_equal, None, ["im", "pf"], ["mq"])
     ts(T.boq[:], T.ig[:], col(1), None, ALU.is_equal, None, ["ig", "pf"], ["boq"], 128)
@@ -176,71 +195,84 @@ def rank_program(g, core, T, topo):
         for a, val in slots.items():
             consts.append("k%s%d" % (name, a))
             fill(T[name][:, a:a + 63 * REC[name] + 1:REC[name]], val, consts[-1])
-    cp(T.lnf[:, 0:64], T.lo_s[:], ["lo"], ["lof"])
-    cp(T.lnf[:, 64:128], T.n_s[:], ["n"], ["nf"])
-    mms([(T.pp[:, 0:128], T.permt[:], T.lnf[:], True, True)], 512, ["permt", "lof", "nf"], ["Pp"])
-    cp(T.loq[:], T.pp[:, 0:64], ["Pp"], ["loq"])
-    cp(T.nq[:], T.pp[:, 64:128], ["Pp"], ["nq"])
-    cp(T.nh[:], T.pp[:, 64:128], ["Pp"], ["nh"])
+    if min(WID) < 32:
+        for b in range(NPA):
+            fill(T["ab%d" % b][:], 0.0, "abz%d" % b, 512)
+    cp(T.nf[:], T.n_s[:], ["n"], ["nf"])
+    mms([(T.pp[:, 0:64], T.permt[:], T.nf[:], True, True)], 256, ["permt", "nf"], ["Pp"])
+    cp(T.nq[:], T.pp[:, 0:64], ["Pp"], ["nq"])
+    cp(T.nh[:], T.pp[:, 0:64], ["Pp"], ["nh"])
+
+    col0 = [sum(WID[:x]) for x in range(NP)]
 
     def rec(name, x, a, n=1):
         q = REC[name] // n
-        b = x * V * REC[name] + a
-        return T[name][:, b:b + (V * n - 1) * q + 1:q]
+        b = col0[x] * REC[name] + a
+        return T[name][:, b:b + (WID[x] * n - 1) * q + 1:q]
 
     def cols(name, x):
-        return T[name][:, x * V:(x + 1) * V]
+        return T[name][:, col0[x]:col0[x] + WID[x]]
 
     def tmp(name, k, x):
-        return T[name][:, k, x * V:(x + 1) * V]
+        return T[name][:, k, col0[x]:col0[x] + WID[x]]
 
-    def blk(name, x, a, b, base=0, wide=128):
-        return T[name][:, x * wide + base + a * V:x * wide + base + b * V]
+    def pair(name, x, a, b):
+        return T[name][:, col0[x]:col0[x] + WID[x], a:b]
+
+    def blk(name, x, a, b):
+        return T[name][:, x * 128 + a * WID[x]:x * 128 + b * WID[x]]
 
     def node(x, e):
+        v = WID[x]
         p0 = 0 if e == 0 else 1
         K = lambda n: "%s.%d" % (n, x)
         R = lambda name, a, n=1: rec(name, x, a, n)
-        W = lambda a: blk("wr", x, a, a + 1)
+        W = lambda a: blk("wt", x, a, a + 1)
         mb, h, sb, xb, m, d = R("mo", 1), R("mo", 3), R("mr", 4), R("mr", 14), R("do", 2), tmp("ti", 0, x)
-        d2 = lambda a, b: T.d2[:, x * V:(x + 1) * V, a:b]
-        sg = lambda a, q: T.pv[:, x * 256 + a:x * 256 + 2 * V:q]
+        tt(d, R("xo", 4), mb, ALU.mult, [K("sg"), K("mh")], [K("d")])
         tt(xb, mb, h, ALU.subtract, [K("mh")], [K("xb")])
         tt(tmp("tf", 0, x), sb, h, ALU.subtract, [K("mh"), K("sb")], [K("t2l")])
         tt(tmp("tf", 1, x), xb, h, ALU.subtract, [K("mh"), K("xb")], [K("t2w")])
-        tt(d, R("xo", 4), mb, ALU.mult, [K("sg"), K("mh")], [K("d")])
-        tt(sg(0, 2), R("xo", 3), tmp("tf", 0, x), ALU.min, [K("sg"), K("t2l")], [K("sgl"), K("acc")])
-        tt(sg(1, 2), R("xo", 4), tmp("tf", 1, x), ALU.min, [K("sg"), K("t2w")], [K("sgw"), K("acc2")])
-        tt(W(2), m, d, ALU.add, [K("m"), K("d")], [K("w")])
-        tt(d2(0, 2), sg(0, 1), R("mr", 4, 2), ALU.mult, [K("sgl"), K("sgw"), K("sb"), K("xb"), K("acc"), K("acc2")], [K("d2")])
-        tt(W(1), m, d2(0, 1), ALU.add, [K("m"), K("d2")], [K("wl")])
-        tt(W(3), W(2), d2(1, 2), ALU.add, [K("w"), K("d2")], [K("ww")])
-        n = (4 - p0) * V
-        kw = [K("w"), K("wl"), K("ww")] + ([] if e else [K("w0")])
-        mms([(T.pp[:, 0:n], T.permq[:], blk("wr", x, p0, 4), True, True)], 4 * n, kw + ["perm"], ["Pp"])
-        cp(T["off%d" % x][:, p0 * V:4 * V], T.pp[:, 0:n], ["Pp"], [K("off")], n)
-        tt(blk("wt", x, p0, 4), blk("wr", x, p0, 4), blk("pv", x, p0, 4, 128, 256), ALU.subtract, kw + [K("lo4")], [K("wt")], n)
-        tt(R("dr", 0), d2(1, 2), d2(0, 1), ALU.subtract, [K("d2")], [K("dd")])
-        cp(R("dr", 1), d2(0, 1), [K("d2")], [K("dl")])
-        if e < NE - 1:
-            tt(R("mr", 0), xb, sb, ALU.subtract, [K("xb"), K("sb")], [K("dm")])
-            ts(R("mr", 16), h, -0.5, None, ALU.add, None, [K("mh")], [K("hb")])
+        tt(pair("sg", x, 0, 1), R("xo", 3), tmp("tf", 0, x), ALU.min, [K("sg"), K("t2l")], [K("sgl")])
+        tt(pair("sg", x, 1, 2), R("xo", 4), tmp("tf", 1, x), ALU.min, [K("sg"), K("t2w")], [K("sgw")])
+        tt(W(1), m, d, ALU.add, [K("m"), K("d")], [K("w1")])
+        tt(pair("d2", x, 0, 2), pair("sg", x, 0, 2), R("mr", 4, 2), ALU.mult, [K("sgl"), K("sgw"), K("sb"), K("xb")], [K("d2")], 4 * v)
+        tt(W(2), W(1), pair("d2", x, 1, 2), ALU.add, [K("w1"), K("d2")], [K("w2")])
+        tt(W(3), m, pair("d2", x, 0, 1), ALU.add, [K("m"), K("d2")], [K("w3")])
+        for a, b in ([(1, 2), (2, 4)] if e and EARLY else [(p0, 4)]):
+            n = (b - a) * v
+            to, kb = (T.pp[:, 0:n], "Pp") if b == 4 else (T.ps[:, 128:128 + n], "Ps")
+            mms([(to, T.idf[:], blk("lo4", x, a, b), True, False)], 4 * max(64, n), [K("lo4"), "idf"], [kb])
+            mms([(to, T.permh[:], blk("wt", x, a, b), False, True)], max(64, n), [K("w%d" % p) for p in range(a, b)] + ["permh"], [kb])
+            cp(T["off%d" % x][:, a * v:b * v], to, [kb], [K("off%d" % p) for p in range(a, b)], n)
 
-    nbank = [0]
-
-    def bank():
-        k = nbank[0] % NPA
-        nbank[0] += 1
-        return k
-
-    def start(x):
+    def rest(x, e):
         K = lambda n: "%s.%d" % (n, x)
         R = lambda name, a, n=1: rec(name, x, a, n)
-        n, lo = cols("nq", x), cols("loq", x)
+        if e:
+            tt(tmp("tf", 4, x), R("so", 2), R("gr", 3), ALU.max, [K("so"), K("gm1")], [K("gm")])
+        tt(R("dr", 0), pair("d2", x, 1, 2), pair("d2", x, 0, 1), ALU.subtract, [K("d2")], [K("dd")])
+        cp(R("dr", 1), pair("d2", x, 0, 1), [K("d2")], [K("dl")])
+        if e < NE - 1:
+            tt(R("mr", 0), R("mr", 14), R("mr", 4), ALU.subtract, [K("xb"), K("sb")], [K("dm")])
+            less_half("hb", R("mr", 16), R("mo", 3), [K("mh")], [K("hb")])
+
+    turn = {"pa": 0, "pt": 0}
+
+    def bank(kind):
+        k = turn[kind] % (NPA if kind == "pa" else NPT)
+        turn[kind] += 1
+        return T["%s%d" % (kind, k)], "P%s%d" % (kind[1], k), k
+
+    def start(x):
+        v = WID[x]
+        K = lambda n: "%s.%d" % (n, x)
+        R = lambda name, a, n=1: rec(name, x, a, n)
+        n = cols("nq", x)
         I = lambda k: tmp("ti", k, x)
-        tt(tmp("tf", 3, x), cols("n_s", x), cols("lo_s", x), ALU.add, ["n", "lo"], [K("f3")])
-        cp(T["eo%d" % x][:, 0:V], cols("lo_s", x), ["lo"], [K("e0")])
-        cp(T["eo%d" % x][:, V:2 * V], tmp("tf", 3, x), [K("f3")], [K("en")])
+        tt(tmp("tf", 3, x), cols("n_s", x), cols("lo_s", x), ALU.add, ["n", "lo"], [K("nv")])
+        cp(T["eo%d" % x][:, 0:v], cols("lo_s", x), ["lo"], [K("e0")])
+        cp(T["eo%d" % x][:, 32:32 + v], tmp("tf", 3, x), [K("nv")], [K("en")])
         ts(I(1), n, 1, None, ALU.arith_shift_right, None, ["nq"], [K("i1")])
         tt(I(2), n, I(1), ALU.subtract, ["nq", K("i1")], [K("i2")])
         ts(I(3), I(2), 1, None, ALU.arith_shift_right, None, [K("i2")], [K("i3")])
@@ -250,111 +282,146 @@ def rank_program(g, core, T, topo):
         tt(tmp("tf", 2, x), I(2), I(1), ALU.subtract, [K("i1"), K("i2")], [K("ud")])
         ts(R("xo", 3), tmp("tf", 2, x), -1.0, 0.5, ALU.mult, ALU.add, [K("ud")], [K("a2")])
         ts(R("xo", 4), tmp("tf", 2, x), -0.5, None, ALU.add, None, [K("ud"), K("a2")], [K("sg")])
-        tt(R("do", 2), I(1), lo, ALU.add, [K("i1"), "loq"], [K("m")])
-        cp(blk("wr", x, 0, 1), R("do", 2), [K("m")], [K("w0")])
+        cp(R("do", 2), I(1), [K("i1")], [K("m")])
+        cp(blk("wt", x, 0, 1), I(1), [K("i1")], [K("w0")])
         for p in range(4):
-            cp(blk("pv", x, p, p + 1, 128, 256), lo, ["loq"] + ([K("lo4")] if p else []), [K("lo4")])
-        k = bank()
-        mms([(T["pa%d" % k][:, :, a], fx(a), cols("nh", x), True, True) for a in range(16)], 64,
-            ["f%d" % a for a in range(16)] + ["nh"], ["Pa%d" % k])
-        act(T["nw%d" % x][:], T["pa%d" % k][:], ACT.Copy, ["Pa%d" % k], [K("nw")], 512)
+            cp(blk("lo4", x, p, p + 1), cols("lo_s", x), ["lo"] + ([K("lo4")] if p else []), [K("lo4")])
+        pa, kb, _b = bank("pa")
+        mms([(pa[:, a // 4:4 * v:4, a % 4], fx(a), cols("nh", x), True, True) for a in range(16)], 16 * 64,
+            ["f%d" % a for a in range(16)] + ["nh"], [kb])
+        act(T["nw%d" % x][:, 0:16 * v], pa[:, 0:4 * v, :], ACT.Copy, [kb], [K("nw")], 16 * v)
         node(x, 0)
 
     def advance(x, e):
+        v = WID[x]
         K = lambda n: "%s.%d" % (n, x)
         R = lambda name, a, n=1: rec(name, x, a, n)
         i = NP * e + x
         p0 = 0 if e == 0 else 1
-        n = (4 - p0) * V
-        slot = lambda k, a, b: T.land[:, (3 * i + k) * 128 + a * V:(3 * i + k) * 128 + b * V]
-        acc = lambda a, b: blk("pv", x, a, b, 0, 256)
-        gm, g1, g3 = tmp("tf", 4, x), blk("gt", x, 0, 1, 0, 64), blk("gt", x, 1, 2, 0, 64)
-        tt(acc(p0, 4), T.sendb[:, i * 128 + p0 * V:(i + 1) * 128], slot(0, p0, 4), ALU.add, ["snd%d" % i, "arr%d.0" % i], [K("acc"), K("acc2")], 2 * n)
-        tt(acc(p0, 4), acc(p0, 4), slot(1, p0, 4), ALU.add, [K("acc"), "arr%d.1" % i], [K("acc")], n)
+        slot = lambda k, a, n: T.land[:, (3 * i + k) * 128 + a * 32:(3 * i + k) * 128 + a * 32 + n]
+        acc = lambda a, n: T.pp[:, 128 + a * 32:128 + a * 32 + n]
+        gt = lambda a, n: T.gt[:, x * 64 + a:x * 64 + a + n]
+        gm, g1, g3 = tmp("tf", 4, x), gt(0, v), gt(32, v)
+        n = 128 - 32 * p0
+        mms([(acc(p0, n), T.idf[:], T.sendb[:, i * 128 + p0 * 32:(i + 1) * 128], True, False)], 4 * n, ["snd%d" % i, "idf"], ["Pp"])
+        mms([(acc(p0, n), T.idf[:], slot(0, p0, n), False, False)], 4 * n, ["arr%d.0" % i], ["Pp"])
+        mms([(acc(p0, n), T.idf[:], slot(1, p0, n), False, True)], 4 * n, ["arr%d.1" % i], ["Pp"])
         if e == 0:
-            tt(gm, acc(0, 1), slot(2, 0, 1), ALU.add, [K("acc"), "arr%d.2" % i], [K("gm")])
-        tt(blk("gt", x, 0, 2, 0, 64), acc(2, 4), slot(2, 2, 4), ALU.add, [K("acc"), "arr%d.2" % i], [K("G")])
-        tt(R("gr", 1), acc(1, 2), slot(2, 1, 2), ALU.add, [K("acc"), "arr%d.2" % i], [K("G2")])
+            tt(gm, acc(0, v), slot(2, 0, v), ALU.add, ["Pp", "arr%d.2" % i], [K("gm")])
+        tt(gt(0, 64), acc(1, 64), slot(2, 1, 64), ALU.add, ["Pp", "arr%d.2" % i], [K("G")])
+        tt(R("gr", 1), acc(3, v), slot(2, 3, v), ALU.add, ["Pp", "arr%d.2" % i], [K("G2")])
         u1, u2, ud = R("ur", 20), R("ur", 40), tmp("tf", 2, x)
         tt(u1, g1, gm, ALU.is_gt, [K("G"), K("gm")], [K("u1")])
-        tt(R("gr", 3), g1, gm, ALU.max, [K("G"), K("gm")], [K("gm1")])
         tt(R("gr", 0), g3, R("gr", 1), ALU.subtract, [K("G"), K("G2")], [K("dg")])
-        scan(R("so", 0, 4), R("ur", 5, 4), R("gr", 0, 4), ALU.subtract, [K("u1"), K("gm1"), K("dg"), K("G2")] + consts, [K("so")], 4 * V)
+        tt(R("gr", 3), g1, gm, ALU.max, [K("G"), K("gm")], [K("gm1")])
+        scan(R("so", 0, 4), R("ur", 5, 4), R("gr", 0, 4), ALU.subtract, [K("u1"), K("gm1"), K("dg"), K("G2")] + consts, [K("so")], 4 * v)
+        ts(u2, R("so", 3), 0.0, None, ALU.is_gt, None, [K("so")], [K("u2")])
+        if e < NE - 1:
+            scan(R("ao", 0, 5), R("ur", 8, 5), R("mr", 0, 5), ALU.add, [K("u1"), K("dm"), K("sb"), K("hb")] + consts, [K("a1")], 5 * v)
+            tt(R("mr", 11), R("ao", 1), R("ao", 4), ALU.subtract, [K("a1")], [K("y")])
+            scan(R("mo", 0, 4), R("ur", 25, 4), R("mr", 11, 4), ALU.add, [K("u2"), K("y"), K("hb")] + consts, [K("mh")], 4 * v)
         tt(ud, u1, tmp("ti", 0, x), ALU.mult, [K("u1"), K("d")], [K("ud")])
         tt(R("dr", 2), R("do", 2), ud, ALU.add, [K("m"), K("ud")], [K("m1")])
-        ts(u2, R("so", 3), 0.0, None, ALU.is_gt, None, [K("so")], [K("u2")])
         scan(R("do", 0, 3), R("ur", 0, 3), R("dr", 0, 3), ALU.add,
-             [K("u1"), K("u2"), K("dd"), K("dl"), K("m1")] + consts, [K("m"), K("d1")], 3 * V)
+             [K("u1"), K("u2"), K("dd"), K("dl"), K("m1")] + consts, [K("m"), K("d1")], 3 * v)
         if e == NE - 1:
-            tt(blk("oq", x, 0, 1, 0, 64), R("so", 2), R("gr", 3), ALU.max, [K("so"), K("gm1")], [K("og")])
-            tt(blk("oq", x, 1, 2, 0, 64), R("do", 2), cols("loq", x), ALU.subtract, [K("m"), "loq"], [K("om")])
-            mms([(T.pp[:, 0:64], T.permq[:], blk("oq", x, 0, 2, 0, 64), True, True)], 256, [K("og"), K("om"), "perm"], ["Pp"])
-            cp(blk("ol", x, 0, 2, 0, 64), T.pp[:, 0:64], ["Pp"], [K("ol")])
+            tt(gm, R("so", 2), R("gr", 3), ALU.max, [K("so"), K("gm1")], [K("gm")])
+            mms([(T.pp[:, 0:v], T.permq[:], gm, True, True), (T.pp[:, v:2 * v], T.permq[:], R("do", 2), True, True)], 512,
+                [K("gm"), K("m"), "perm"], ["Pp"])
+            cp(T.ol[:, x * 64:x * 64 + 2 * v], T.pp[:, 0:2 * v], ["Pp"], [K("ol")])
             return
-        tt(gm, R("so", 2), R("gr", 3), ALU.max, [K("so"), K("gm1")], [K("gm")])
-        scan(R("ao", 0, 5), R("ur", 8, 5), R("mr", 0, 5), ALU.add, [K("u1"), K("dm"), K("sb"), K("hb")] + consts, [K("a1")], 5 * V)
-        ts(tmp("tf", 3, x), R("so", 3), 0.0, 0.5, ALU.is_le, ALU.subtract, [K("so")], [K("nv")])
-        tt(R("mr", 11), R("ao", 1), R("ao", 4), ALU.subtract, [K("a1")], [K("y")])
-        ts(R("mr", 4), R("ao", 3), -0.5, None, ALU.add, None, [K("a1")], [K("sb")])
-        scan(R("mo", 0, 4), R("ur", 25, 4), R("mr", 11, 4), ALU.add, [K("u2"), K("y"), K("hb")] + consts, [K("mh")], 4 * V)
+        if "nv" in ASIDE:
+            add("a", [lambda: g.scalar.activation(tmp("tf", 3, x), R("so", 3), ACT.Sign, T.pf[:, 8:9], -1.0)], 64 * CYC, [K("so"), "half2"], [K("nv")])
+        else:
+            ts(tmp("tf", 3, x), R("so", 3), 0.0, 0.5, ALU.is_le, ALU.subtract, [K("so")], [K("nv")])
+        less_half("sb", R("mr", 4), R("ao", 3), [K("a1")], [K("sb")])
         tt(R("xb", 1), R("ao", 3), R("mo", 1), ALU.subtract, [K("a1"), K("mh")], [K("nt")])
         tt(R("xa", 1), R("do", 1), tmp("tf", 3, x), ALU.mult, [K("d1"), K("nv")], [K("q")])
-        scan(R("xo", 0, 5), R("xa", 0, 5), R("xb", 0, 5), ALU.max, [K("q"), K("nt")] + consts, [K("sg")], 5 * V)
+        scan(R("xo", 0, 5), R("xa", 0, 5), R("xb", 0, 5), ALU.max, [K("q"), K("nt")] + consts, [K("sg")], 5 * v)
         node(x, e + 1)
 
     def gather(off):
         return T.win[:, 0:WC].indirect(off)
 
-    GC = 512 * GAM + 64
-
     def rise(x):
-        s0, ri, eo = T["s0_%d" % x], T["ri%d" % x], T["eo%d" % x]
-        act(s0[:], gather(eo[:, 0:V]), ACT.Copy, ["win", "e0.%d" % x], ["s0.%d" % x], GC)
-        tt(ri[:], gather(eo[:, V:2 * V]), s0[:], ALU.subtract, ["win", "en.%d" % x, "s0.%d" % x], ["ri.%d" % x], GC)
+        v = WID[x]
+        s0, ri, eo = T["s0_%d" % x][:, 0:16 * v], T["ri%d" % x][:, 0:16 * v], T["eo%d" % x]
+        act(s0, gather(eo[:, 0:v]), ACT.Copy, ["win", "e0.%d" % x], ["s0.%d" % x], 16 * v * GAM + 64)
+        tt(ri, gather(eo[:, 32:32 + v]), s0, ALU.subtract, ["win", "en.%d" % x, "s0.%d" % x], ["ri.%d" % x], 16 * v * GAM + 64)
 
     def gains(x, e):
+        v = WID[x]
+        w = 16 * v
         p0 = 0 if e == 0 else 1
-        n = (4 - p0) * V
         i = NP * e + x
         K = lambda nm: "%s.%d" % (nm, x)
         st, off, qb = T["st%d" % x], T["off%d" % x], T["qb%d" % x]
         for p in range(p0, 4):
+            args = (st[:, w * p:w * p + w], gather(off[:, p * v:p * v + v]))
             if (x, e, p) in VGATHER:
-                cp(st[:, 512 * p:512 * p + 512], gather(off[:, p * V:p * V + V]), ["win", K("off")], [K("st%d" % p)], GC)
+                cp(args[0], args[1], ["win", K("off%d" % p)], [K("st%d" % p)], w * GAM + 64)
             else:
-                act(st[:, 512 * p:512 * p + 512], gather(off[:, p * V:p * V + V]), ACT.Copy, ["win", K("off")], [K("st%d" % p)], GC)
+                act(args[0], args[1], ACT.Copy, ["win", K("off%d" % p)], [K("st%d" % p)], w * GAM + 64)
         for k in range(4):
-            pt, kt = T["pt%d" % (k % 2)], "Pt%d" % (k % 2)
-            mms([(pt[:, p0 * V:4 * V, c], fx(4 * c + k), blk("wt", x, p0, 4), True, True) for c in range(4)], n,
-                [K("wt")] + ["f%d" % (4 * c + k) for c in range(4)], [kt])
+            pt, kt, _b = bank("pt")
+            mms([(pt[:, p0 * v:4 * v, c], fx(4 * c + k), blk("wt", x, p0, 4), True, True) for c in range(4)], 4 * max(64, (4 - p0) * v),
+                [K("w%d" % p) for p in range(p0, 4)] + ["f%d" % (4 * c + k) for c in range(4)], [kt])
             for p in range(p0, 4):
-                tt(qb[:, 512 * p + k:512 * p + 512:4], pt[:, p * V:p * V + V, :], T["ri%d" % x][:, k:512:4], ALU.mult,
-                   [kt, K("ri")], [K("q%d.%d" % (p, k))], 128)
-        for p in range(p0, 4):
-            b = bank()
-            pa, kb, ab = T["pa%d" % b], "Pa%d" % b, T["ab%d" % b]
-            mms([(pa[:], T.nident[:], T["s0_%d" % x][:], True, False)], 512, [K("s0"), "nid"], [kb])
-            mms([(pa[:], T.ident[:], st[:, 512 * p:512 * p + 512], False, True)], 512, [K("st%d" % p), "id"], [kb])
-            tt(pa[:], pa[:], T["nw%d" % x][:], ALU.mult, [kb, K("nw")], [kb], 512)
-            tt(pa[:], pa[:], qb[:, 512 * p:512 * p + 512], ALU.subtract, [kb] + [K("q%d.%d" % (p, k)) for k in range(4)], [kb], 512)
+                tt(qb[:, w * p + k:w * p + w:4], pt[:, p * v:p * v + v, :], T["ri%d" % x][:, k:w:4], ALU.mult,
+                   [kt, K("ri")], [K("q%d.%d" % (p, k))], 4 * v)
+        parts = [(p, 0, v) for p in range(p0, 4)]
+        if SPLIT:
+            parts[-1:] = [(3, 0, v // 2), (3, v // 2, v)]
+        held = {}
+
+        def times_n(p, c0, c1):
+            pb, kb, b = bank("pa" if c0 == 0 else "pt")
+            held[p, c0] = (pb, kb)
+            held.setdefault(p, b)
+            wide = pb[:, 0:4 * (c1 - c0), :]
+            mms([(wide, T.nident[:], T["s0_%d" % x][:, 16 * c0:16 * c1], True, False)], 16 * (c1 - c0), [K("s0"), "nid"], [kb])
+            mms([(wide, T.ident[:], st[:, w * p + 16 * c0:w * p + 16 * c1], False, True)], 16 * (c1 - c0), [K("st%d" % p), "id"], [kb])
+            for a in range(c0, c1, WG):
+                z = min(c1, a + WG)
+                cut = pb[:, 4 * (a - c0):4 * (z - c0), :]
+                tt(cut, cut, T["nw%d" % x][:, 16 * a:16 * z], ALU.mult, [kb, K("nw")], [K("nu%d.%d" % (p, a))], 16 * (z - a))
+
+        def sizes(p, c0, c1):
+            (pb, kb), b, u = held[p, c0], held[p], c1 - c0
+            ab = T["ab%d" % b]
+            for a in range(c0, c1, WG):
+                z = min(c1, a + WG)
+                cut = pb[:, 4 * (a - c0):4 * (z - c0), :]
+                tt(cut, cut, qb[:, w * p + 16 * a:w * p + 16 * z], ALU.subtract,
+                   [kb, K("nu%d.%d" % (p, a))] + [K("q%d.%d" % (p, k)) for k in range(4)], [K("df%d.%d" % (p, a))], 16 * (z - a))
             for c in range(4):
-                act(ab[:, 128 * c:128 * c + 128], pa[:, :, 4 * c:4 * c + 4], ACT.Abs, [kb], ["ab%d.%d" % (b, c)], 128)
-            mms([(T.ps[:, 32 * p + 8 * k:32 * p + 8 * k + 8], ab[:, k:512:4], T.bsel[:], True, True) for k in range(4)], 256,
-                ["ab%d.%d" % (b, c) for c in range(4)] + ["bsel"], ["Ps"])
-        src = T.sendb[:, i * 128 + p0 * V:(i + 1) * 128]
-        add("v", [lambda: g.vector.transpose(src, T.ps[:, p0 * V:128])], n * CYC, ["Ps"], ["snd%d" % i])
+                act(ab[:, 128 * c + 4 * c0:128 * c + 4 * c1], pb[:, c:4 * u:4, :], ACT.Abs,
+                    [kb, "abz%d" % b] + [K("df%d.%d" % (p, a)) for a in range(c0, c1, WG)],
+                    ["ab%d.%d.%d" % (b, c, h) for h in range(2) if (c1 == v if h else c0 == 0)], 4 * u)
+            if c1 == v:
+                mms([(T.ps[:, 32 * p + 8 * k:32 * p + 8 * k + 8], ab[:, k:512:4], T.bsel[:], True, True) for k in range(4)], 1024,
+                    ["ab%d.%d.%d" % (b, c, h) for c in range(4) for h in range(2)] + ["bsel"], ["Ps"])
+
+        for k, part in enumerate(parts):
+            times_n(*part)
+            if k:
+                sizes(*parts[k - 1])
+        sizes(*parts[-1])
+        src = T.sendb[:, i * 128 + p0 * 32:(i + 1) * 128]
+        add("v", [lambda: g.vector.transpose(src, T.ps[:, p0 * 32:128])], (128 - p0 * 32) * CYC, ["Ps"], ["snd%d" % i])
         ids, dsts = [], []
         for q in peers:
             rid, pid, _se = topo.addr(cores[q])
             k = (q - rank - 1) % nr
             ids.append(DstId(rid=rid, pnc=pid))
-            dsts.append(T.land[:, (3 * i + k) * 128 + p0 * V:(3 * i + k + 1) * 128])
+            dsts.append(T.land[:, (3 * i + k) * 128 + p0 * 32:(3 * i + k + 1) * 128])
         add("g", [lambda: g.remote_dma_fused(
             [RemoteDMATransfer(dst_ids=ids, dma_engine_mask=emask, remote_sem=T.sem["arr%d_%d" % (i, rank)], src=src, dsts=dsts)],
-            local_sem=T.sem.sent)], 0.5, ["snd%d" % i], ["out%d" % i], 0.0, ("sent", 0))
+            local_sem=T.sem.sent)], 0.3, ["snd%d" % i], ["out%d" % i], 0.0, ("sent", 0))
         for k in range(nr - 1):
-            add("x", [lambda: None], 0.0, ["out%d" % i], ["arr%d.%d" % (i, k)], LINK * (k + 4) / 6,
+            add("x", [lambda: None], 0.0, ["out%d" % i], ["arr%d.%d" % (i, k)], LINK + STEP * (k - 2),
                 ("arr%d_%d" % (i, (rank - k - 1) % nr), neng))
+        rest(x, e)
 
     for x in range(NP):
         start(x)
@@ -365,14 +432,15 @@ def rank_program(g, core, T, topo):
         gains(x, 0)
     for e in range(1, NE):
         for x in range(NP):
-            phase[0] = NP * e + x
+            phase[0] = NP * e + x - AHEAD
             advance(x, e - 1)
+            phase[0] = NP * e + x
             gains(x, e)
     for x in range(NP):
         phase[0] = NP * NE + x
         advance(x, NE - 1)
-        dma("a", g.scalar, cols("yg", x), blk("ol", x, 0, 1, 0, 64), "st_a", 16 * NP, 2.0, ["ol.%d" % x], [])
-        dma("s", g.sync, cols("ym", x), blk("ol", x, 1, 2, 0, 64), "st_s", 16 * NP, 2.0, ["ol.%d" % x], [])
+        dma("a", g.scalar, cols("yg", x), T.ol[:, x * 64:x * 64 + WID[x]], "st_a", 16 * NP, 2.0, ["ol.%d" % x], [])
+        dma("s", g.sync, cols("ym", x), T.ol[:, x * 64 + WID[x]:x * 64 + 2 * WID[x]], "st_s", 16 * NP, 2.0, ["ol.%d" % x], [])
 
     ns = len(steps)
     succ = [[] for _ in range(ns)]
@@ -382,7 +450,7 @@ def rank_program(g, core, T, topo):
 
     def waits(j, i):
         raw = steps[i]["deps"][j]
-        return not (raw is None or (steps[j]["e"] == steps[i]["e"] and steps[i]["e"] in "t" and not raw))
+        return not (raw is None or (steps[j]["e"] == steps[i]["e"] and steps[i]["e"] in "tva" and not raw))
 
     def gap(j, i):
         if not waits(j, i):
@@ -438,7 +506,18 @@ def rank_program(g, core, T, topo):
         way = [0.0] * ns
         for i in range(ns - 1, -1, -1):
             way[i] = cost[i] + max([steps[i]["lat"]] + [d + way[j] for j, d in outof[i]])
-        at = greedy(way)
+        left = [len(s["deps"]) for s in steps]
+        ready = [i for i in range(ns) if left[i] == 0]
+        seq = []
+        while ready:
+            i = min(ready, key=lambda j: (steps[j]["w"], j))
+            ready.remove(i)
+            seq.append(i)
+            for j in succ[i]:
+                left[j] -= 1
+                if left[j] == 0:
+                    ready.append(j)
+        at = greedy(way) if GREEDY else place(seq, False)
         best = None
         for _ in range(ROUNDS + 1):
             end = max(at[i] + cost[i] + steps[i]["lat"] for i in range(ns))

@@ -2,63 +2,67 @@ from concourse.bass import DstId, RemoteDMATransfer
 from concourse.mybir import AluOpType as ALU, ActivationFunctionType as ACT
 
 WC = 12288
-WID = [32, 32]
-NP = len(WID)
+V = 32
+W = 16 * V
 NE = 4
 NPA = 3
 NPT = 3
 SPLIT = True
 EARLY = True
+FIRST = True
+TSUB = {0: [0], 1: [0]}
+CUT = 2
+LAG = 1
 VGATHER = [(0, 0, 0)]
-ASIDE = ["hb", "sb", "nv"]
 CYC = 0.00083
 PEC = 0.00042
-GAM = 1.56
-LINK = 5.0
-STEP = 1.16
-HOP = 0.18
-SAME = 0.18
-SLACK = 0.05
-LOAD = 12.5
-ROUNDS = 3
-GREEDY = False
-AHEAD = 0
-WG = 32
+GAM = 1.7
+FIX = 0.012
+LINK = 3.8
+STEP = 0.5
+HOP = 0.19
+SAME = 0.2
+LOAD = 5.5
+ROUNDS = 3000
+SHAKE = [0.25, 0.6, 1.4]
+CASES = [({}, -0.8, 0.0, 1.0), ({}, 1.6, 0.0, 0.7), ({"t": 1.4}, -0.8, 0.08, 0.7), ({"v": 1.3, "a": 1.4}, -0.8, 0.0, 0.5)]
 ORDER = []
-MG = 12582912.0
+MG = 12582912
 REC = {"ur": 60, "gr": 4, "mr": 20, "so": 4, "ao": 5, "mo": 4, "dr": 3, "do": 3, "xa": 5, "xb": 5, "xo": 5}
+FIXED = {"ur": {0: 0, 5: 0, 35: -1, 50: 1, 8: 0, 32: 0.5, 44: 1, 56: 1, 25: 0, 55: 0.5, 70: 1}, "gr": {2: 0},
+         "mr": {8: MG, 12: -MG, 21: MG, 26: -MG}, "xa": {0: 0, 2: -1, 3: -1, 4: -1}, "xb": {0: 1, 2: -0.5, 3: -0.5, 4: -0.5}}
 
 SCRATCH = {
     "win": ("sbuf", [128, WC], "bfloat16"),
     "lo_s": ("sbuf", [128, 64], "int32"),
     "n_s": ("sbuf", [128, 64], "int32"),
     "nf": ("sbuf", [128, 64], "float32"),
-    "lo4": ("sbuf", [128, NP * 128], "float32"),
-    "nq": ("sbuf", [128, 64], "int32"),
     "nh": ("sbuf", [128, 64], "float16"),
-    "im": ("sbuf", [128, 128], "int32"),
-    "ig": ("sbuf", [128, 128], "int32"),
-    "pi": ("sbuf", [128, 8], "int32"),
-    "pf": ("sbuf", [128, 16], "float32"),
+    "lo2": ("sbuf", [128, 2, 64], "int32"),
+    "lob": ("sbuf", [128, 2, 64], "bfloat16"),
+    "eo": ("sbuf", [128, 128], "uint16"),
+    "ones": ("sbuf", [128, 128], "bfloat16"),
+    "half": ("sbuf", [128, 2], "float32"),
     "ident": ("sbuf", [128, 128], "bfloat16"),
     "nident": ("sbuf", [128, 128], "bfloat16"),
-    "permq": ("sbuf", [128, 128], "float32"),
-    "permh": ("sbuf", [128, 128], "float16"),
-    "permt": ("sbuf", [128, 128], "float32"),
+    "id64": ("sbuf", [128, 128], "bfloat16"),
     "idf": ("sbuf", [128, 128], "float32"),
+    "nidf": ("sbuf", [128, 128], "float32"),
+    "permq": ("sbuf", [128, 128], "float32"),
+    "permh": ("sbuf", [128, 128], "bfloat16"),
+    "permt": ("sbuf", [128, 128], "float32"),
+    "bsel1": ("sbuf", [128, 8], "float32"),
     "bsel": ("sbuf", [128, 8], "float32"),
-    "boq": ("sbuf", [128, 128], "float16"),
-    "mq": ("sbuf", [128, 16], "float32"),
-    "fexp": ("sbuf", [128, 2048], "float16"),
-    "land": ("sbuf", [128, NP * NE * 3 * 128], "float32"),
-    "sendb": ("sbuf", [128, NP * NE * 128], "float32"),
-    "ol": ("sbuf", [128, NP * 64], "float32"),
-    "wt": ("sbuf", [128, NP * 128], "float16"),
-    "gt": ("sbuf", [128, NP * 64], "float32"),
+    "fexp": ("sbuf", [128, 2048], "bfloat16"),
+    "land": ("sbuf", [128, 2 * NE * 3 * 128], "float32"),
+    "sendb": ("sbuf", [128, 2 * NE * 128], "float32"),
+    "ol": ("sbuf", [128, 128], "float32"),
+    "wt": ("sbuf", [128, 4, 64], "float16"),
+    "gt": ("sbuf", [128, 128], "float32"),
     "d2": ("sbuf", [128, 64, 2], "int32"),
     "sg": ("sbuf", [128, 64, 2], "float32"),
-    "ti": ("sbuf", [128, 4, 64], "int32"),
-    "tf": ("sbuf", [128, 6, 64], "float32"),
+    "ti": ("sbuf", [128, 3, 64], "int32"),
+    "tf": ("sbuf", [128, 5, 64], "float32"),
     "ps": ("psum", [128, 512], "float32"),
     "pp": ("psum", [128, 512], "float32"),
 }
@@ -68,18 +72,17 @@ for _k in range(NPT):
     SCRATCH["pt%d" % _k] = ("psum", [128, 128, 4], "float32")
 for _k in range(NPA):
     SCRATCH["pa%d" % _k] = ("psum", [128, 128, 4], "float32")
-    SCRATCH["ab%d" % _k] = ("sbuf", [128, 512], "float32")
-for _x in range(NP):
-    SCRATCH["nw%d" % _x] = ("sbuf", [128, 512], "float32")
-    SCRATCH["qb%d" % _x] = ("sbuf", [128, 2048], "float32")
-    SCRATCH["st%d" % _x] = ("sbuf", [128, 2048], "bfloat16")
-    SCRATCH["s0_%d" % _x] = ("sbuf", [128, 512], "bfloat16")
-    SCRATCH["ri%d" % _x] = ("sbuf", [128, 512], "bfloat16")
-    SCRATCH["eo%d" % _x] = ("sbuf", [128, 64], "uint16")
+    SCRATCH["ab%d" % _k] = ("sbuf", [128, W], "float32")
+for _x in range(2):
+    SCRATCH["nw%d" % _x] = ("sbuf", [128, W], "float32")
+    SCRATCH["qb%d" % _x] = ("sbuf", [128, 4 * W], "float32")
+    SCRATCH["st%d" % _x] = ("sbuf", [128, 4 * W], "bfloat16")
+    SCRATCH["s0_%d" % _x] = ("sbuf", [128, W], "bfloat16")
+    SCRATCH["ri%d" % _x] = ("sbuf", [128, 3 * W], "bfloat16")
     SCRATCH["off%d" % _x] = ("sbuf", [128, 128], "uint16")
 
 SEMAPHORES = ["cv", "ca", "ct", "cg", "ld_lo", "ld_n", "ld_w", "sent", "st_s", "st_a"] + \
-    ["arr%d_%d" % (_k, _r) for _k in range(NP * NE) for _r in range(4)]
+    ["arr%d_%d" % (_k, _r) for _k in range(2 * NE) for _r in range(4)]
 
 
 def rank_program(g, core, T, topo):
@@ -99,7 +102,11 @@ def rank_program(g, core, T, topo):
     readers = {}
     phase = [-1]
 
+    def flat(keys):
+        return [k for ks in keys for k in (ks if isinstance(ks, list) else [ks])]
+
     def add(e, fns, cost, reads, writes, lat=0.0, event=None, after=None):
+        reads, writes = flat(reads), flat(writes)
         deps = {}
         for k in reads:
             if k in lastw:
@@ -139,17 +146,11 @@ def rank_program(g, core, T, topo):
     def scan(out, d0, d1, o1, reads, writes, n):
         add("v", [lambda: g.vector.tensor_tensor_scan(out, d0, d1, 0.0, ALU.mult, o1)], max(64, n) * CYC, reads, writes)
 
-    def fill(ap, val, key, n=64):
-        add("v", [lambda: g.vector.memset(ap, val)], max(64, n) * CYC, [], [key])
+    def fill(ap, val, key):
+        add("v", [lambda: g.vector.memset(ap, val)], 64 * CYC, [], [key])
 
-    def act(out, a, f, reads, writes, n, after=None):
-        return add("a", [lambda: g.scalar.activation(out, a, f)], max(64, n) * CYC, reads, writes, after=after)
-
-    def less_half(name, out, a, reads, writes):
-        if name in ASIDE:
-            add("a", [lambda: g.scalar.activation(out, a, ACT.Identity, T.pf[:, 7:8])], 64 * CYC, reads + ["half"], writes)
-        else:
-            ts(out, a, -0.5, None, ALU.add, None, reads, writes)
+    def act(out, a, f, reads, writes, n=64, bias=0.0, scale=1.0):
+        add("a", [lambda: g.scalar.activation(out, a, f, bias, scale)], max(64, n) * CYC, reads, writes)
 
     def mms(calls, cyc, reads, writes):
         fns = [(lambda c=c: g.tensor.matmul(c[0], c[1], c[2], c[3], c[4])) for c in calls]
@@ -158,104 +159,56 @@ def rank_program(g, core, T, topo):
     def dma(e, q, out, src, sem, val, lat, reads, writes, after=None):
         add(e, [lambda: q.dma_start(out, src).then_inc(T.sem[sem], 16)], 0.1, reads, writes, lat, (sem, val), after)
 
-    def pool(fn, reads, writes):
-        add("g", [fn], 0.4, reads, writes)
+    def select(out, src, pattern, alu, base, step, reads, writes, n):
+        add("g", [lambda: g.affine_select(out, src, pattern, alu, 0.0, base, step)], 0.17 + 2 * n * CYC, reads, writes)
+
+    span = lambda x: (0, 64) if x is None else (x * V, x * V + V)
+
+    def rec(name, x, a, n=1):
+        c0, c1 = span(x)
+        q = REC[name] // n
+        b = c0 * REC[name] + a
+        return T[name][:, b:b + ((c1 - c0) * n - 1) * q + 1:q]
+
+    cols = lambda name, x: T[name][:, span(x)[0]:span(x)[1]]
+    tmp = lambda name, k, x: T[name][:, k, span(x)[0]:span(x)[1]]
+    pair = lambda name, x, a, b: T[name][:, span(x)[0]:span(x)[1], a:b]
+    places = lambda x, a, b: T.wt[:, a:b, span(x)[0]:span(x)[1]]
+    keys = lambda x: (lambda n: ["%s.%d" % (n, y) for y in range(2) if x in (None, y)])
+    fx = lambda a: T.fexp[:, a * 128:(a + 1) * 128]
+    gather = lambda off: T.win[:, 0:WC].indirect(off)
+    GC = W * GAM + 64
 
     dma("a", g.scalar, T.n_s[:], T.span[:], "ld_n", 16, 2.0, [], ["n"])
     dma("s", g.sync, T.lo_s[:], T.lo[:], "ld_lo", 16, 2.0, [], ["lo"])
     dma("s", g.sync, T.win[:], T.walk[:], "ld_w", 16, LOAD, [], ["win"], len(steps) - 1)
 
-    pool(lambda: g.iota(T.pi[:, 0:1], [[1, 1]], 0, 1), [], ["p"])
-    pool(lambda: g.iota(T.im[:], [[1, 128]], 0, 0), [], ["im"])
-    pool(lambda: g.iota(T.ig[:], [[1, 8], [0, 16]], 0, 0), [], ["ig"])
-    for k, (val, alu) in enumerate([(7, ALU.bitwise_and), (3, ALU.arith_shift_right), (15, ALU.bitwise_and), (4, ALU.arith_shift_right)]):
-        ts(T.pi[:, k + 1:k + 2], T.pi[:, 0:1], val, None, alu, None, ["p"], ["p%d" % k])
-    cp(T.pf[:, 0:5], T.pi[:, 0:5], ["p", "p0", "p1", "p2", "p3"], ["pf"])
-    col = lambda k: T.pf[:, k:k + 1]
-    fill(col(7), -0.5, "half")
-    fill(col(8), 0.5, "half2")
-    ts(col(5), col(1), 16.0, col(2), ALU.mult, ALU.add, ["pf"], ["lq"])
-    ts(col(6), col(3), 8.0, col(4), ALU.mult, ALU.add, ["pf"], ["ql"])
-    ts(T.permt[:], T.im[:], col(6), None, ALU.is_equal, None, ["im", "ql"], ["permt"], 128)
-    ts(T.permq[:], T.im[:], col(5), None, ALU.is_equal, None, ["im", "lq"], ["perm"], 128)
-    ts(T.permh[:], T.im[:], col(5), None, ALU.is_equal, None, ["im", "lq"], ["permh"], 128)
-    ts(T.ident[:], T.im[:], col(0), None, ALU.is_equal, None, ["im", "pf"], ["id"], 128)
-    ts(T.nident[:], T.im[:], col(0), -1.0, ALU.is_equal, ALU.mult, ["im", "pf"], ["nid"], 128)
-    ts(T.idf[:], T.im[:], col(0), None, ALU.is_equal, None, ["im", "pf"], ["idf"], 128)
-    ts(T.bsel[:], T.im[:, 0:8], col(4), None, ALU.is_equal, None, ["im", "pf"], ["bsel"])
-    ts(T.mq[:], T.im[:, 0:16], col(2), None, ALU.is_equal, None, ["im", "pf"], ["mq"])
-    ts(T.boq[:], T.ig[:], col(1), None, ALU.is_equal, None, ["ig", "pf"], ["boq"], 128)
-    for a in range(16):
-        ts(T.fexp[:, a * 128:(a + 1) * 128], T.boq[:], T.mq[:, a:a + 1], None, ALU.mult, None, ["boq", "mq"], ["f%d" % a])
-    fx = lambda a: T.fexp[:, a * 128:(a + 1) * 128]
+    fill(T.ones[:], 1.0, "ones")
+    fill(T.half[:, 0:1], -0.5, "half")
+    fill(T.half[:, 1:2], 0.5, "half2")
+    select(T.ident[:], T.ones[:], [[-1, 128]], ALU.is_equal, 0, 1, ["ones"], ["id"], 128)
+    select(T.permt[:], T.ones[:], [[-1, 16], [-16, 8]], ALU.is_equal, 0, 1, ["ones"], ["permt"], 128)
+    select(T.permh[:], T.ones[:], [[-1, 8], [-8, 16]], ALU.is_equal, 0, 1, ["ones"], ["permh"], 128)
+    select(T.bsel1[:], T.ones[:, 0:8], [[-16, 8]], ALU.is_ge, 0, 1, ["ones"], ["bsel1"], 8)
+    select(T.bsel[:], T.bsel1[:], [[16, 8]], ALU.is_ge, 15, -1, ["bsel1"], ["bsel"], 8)
+    act(T.id64[:], T.ident[:], ACT.Copy, ["id"], ["id64"], 128, scale=64.0)
+    act(T.nident[:], T.ident[:], ACT.Copy, ["id"], ["nid"], 128, scale=-1.0)
+    for r in range(16):
+        act(T.fexp[:, r:2048:16], T.ident[:], ACT.Copy, ["id"], ["f%d" % r], 128)
+    kf = ["f%d" % r for r in range(16)]
+    act(T.nidf[:], T.ident[:], ACT.Copy, ["id"], ["nidf"], 128, scale=-1.0)
+    act(T.idf[:], T.ident[:], ACT.Copy, ["id"], ["idf"], 128)
+    act(T.permq[:], T.permh[:], ACT.Copy, ["permh"], ["perm"], 128)
     consts = []
-    for name, slots in [("ur", {0: 0.0, 5: 0.0, 35: -1.0, 50: 1.0, 8: 0.0, 32: 0.5, 44: 1.0, 56: 1.0, 25: 0.0, 55: 0.5, 70: 1.0}),
-                        ("gr", {2: 0.0}), ("mr", {8: MG, 12: -MG, 21: MG, 26: -MG}),
-                        ("xa", {0: 0.0, 2: -1.0, 3: -1.0, 4: -1.0}), ("xb", {0: 1.0, 2: -0.5, 3: -0.5, 4: -0.5})]:
-        for a, val in slots.items():
+    for name in FIXED:
+        for a, val in FIXED[name].items():
+            ap = T[name][:, a:a + 63 * REC[name] + 1:REC[name]]
             consts.append("k%s%d" % (name, a))
-            fill(T[name][:, a:a + 63 * REC[name] + 1:REC[name]], val, consts[-1])
-    if min(WID) < 32:
-        for b in range(NPA):
-            fill(T["ab%d" % b][:], 0.0, "abz%d" % b, 512)
-    cp(T.nf[:], T.n_s[:], ["n"], ["nf"])
-    mms([(T.pp[:, 0:64], T.permt[:], T.nf[:], True, True)], 256, ["permt", "nf"], ["Pp"])
-    cp(T.nq[:], T.pp[:, 0:64], ["Pp"], ["nq"])
-    cp(T.nh[:], T.pp[:, 0:64], ["Pp"], ["nh"])
-
-    col0 = [sum(WID[:x]) for x in range(NP)]
-
-    def rec(name, x, a, n=1):
-        q = REC[name] // n
-        b = col0[x] * REC[name] + a
-        return T[name][:, b:b + (WID[x] * n - 1) * q + 1:q]
-
-    def cols(name, x):
-        return T[name][:, col0[x]:col0[x] + WID[x]]
-
-    def tmp(name, k, x):
-        return T[name][:, k, col0[x]:col0[x] + WID[x]]
-
-    def pair(name, x, a, b):
-        return T[name][:, col0[x]:col0[x] + WID[x], a:b]
-
-    def blk(name, x, a, b):
-        return T[name][:, x * 128 + a * WID[x]:x * 128 + b * WID[x]]
-
-    def node(x, e):
-        v = WID[x]
-        p0 = 0 if e == 0 else 1
-        K = lambda n: "%s.%d" % (n, x)
-        R = lambda name, a, n=1: rec(name, x, a, n)
-        W = lambda a: blk("wt", x, a, a + 1)
-        mb, h, sb, xb, m, d = R("mo", 1), R("mo", 3), R("mr", 4), R("mr", 14), R("do", 2), tmp("ti", 0, x)
-        tt(d, R("xo", 4), mb, ALU.mult, [K("sg"), K("mh")], [K("d")])
-        tt(xb, mb, h, ALU.subtract, [K("mh")], [K("xb")])
-        tt(tmp("tf", 0, x), sb, h, ALU.subtract, [K("mh"), K("sb")], [K("t2l")])
-        tt(tmp("tf", 1, x), xb, h, ALU.subtract, [K("mh"), K("xb")], [K("t2w")])
-        tt(pair("sg", x, 0, 1), R("xo", 3), tmp("tf", 0, x), ALU.min, [K("sg"), K("t2l")], [K("sgl")])
-        tt(pair("sg", x, 1, 2), R("xo", 4), tmp("tf", 1, x), ALU.min, [K("sg"), K("t2w")], [K("sgw")])
-        tt(W(1), m, d, ALU.add, [K("m"), K("d")], [K("w1")])
-        tt(pair("d2", x, 0, 2), pair("sg", x, 0, 2), R("mr", 4, 2), ALU.mult, [K("sgl"), K("sgw"), K("sb"), K("xb")], [K("d2")], 4 * v)
-        tt(W(2), W(1), pair("d2", x, 1, 2), ALU.add, [K("w1"), K("d2")], [K("w2")])
-        tt(W(3), m, pair("d2", x, 0, 1), ALU.add, [K("m"), K("d2")], [K("w3")])
-        for a, b in ([(1, 2), (2, 4)] if e and EARLY else [(p0, 4)]):
-            n = (b - a) * v
-            to, kb = (T.pp[:, 0:n], "Pp") if b == 4 else (T.ps[:, 128:128 + n], "Ps")
-            mms([(to, T.idf[:], blk("lo4", x, a, b), True, False)], 4 * max(64, n), [K("lo4"), "idf"], [kb])
-            mms([(to, T.permh[:], blk("wt", x, a, b), False, True)], max(64, n), [K("w%d" % p) for p in range(a, b)] + ["permh"], [kb])
-            cp(T["off%d" % x][:, a * v:b * v], to, [kb], [K("off%d" % p) for p in range(a, b)], n)
-
-    def rest(x, e):
-        K = lambda n: "%s.%d" % (n, x)
-        R = lambda name, a, n=1: rec(name, x, a, n)
-        if e:
-            tt(tmp("tf", 4, x), R("so", 2), R("gr", 3), ALU.max, [K("so"), K("gm1")], [K("gm")])
-        tt(R("dr", 0), pair("d2", x, 1, 2), pair("d2", x, 0, 1), ALU.subtract, [K("d2")], [K("dd")])
-        cp(R("dr", 1), pair("d2", x, 0, 1), [K("d2")], [K("dl")])
-        if e < NE - 1:
-            tt(R("mr", 0), R("mr", 14), R("mr", 4), ALU.subtract, [K("xb"), K("sb")], [K("dm")])
-            less_half("hb", R("mr", 16), R("mo", 3), [K("mh")], [K("hb")])
+            if val == int(val):
+                add("g", [lambda ap=ap, val=val: g.iota(ap, [[0, 64]], val, 0, allow_small_or_imprecise_dtypes=True)],
+                    0.13 + 128 * CYC, [], [consts[-1]])
+            else:
+                act(ap, T.ones[:, 0:64], ACT.Copy, ["ones"], [consts[-1]], scale=val)
 
     turn = {"pa": 0, "pt": 0}
 
@@ -264,183 +217,230 @@ def rank_program(g, core, T, topo):
         turn[kind] += 1
         return T["%s%d" % (kind, k)], "P%s%d" % (kind[1], k), k
 
-    def start(x):
-        v = WID[x]
-        K = lambda n: "%s.%d" % (n, x)
+    def node(x):
+        K = keys(x)
         R = lambda name, a, n=1: rec(name, x, a, n)
-        n = cols("nq", x)
-        I = lambda k: tmp("ti", k, x)
-        tt(tmp("tf", 3, x), cols("n_s", x), cols("lo_s", x), ALU.add, ["n", "lo"], [K("nv")])
-        cp(T["eo%d" % x][:, 0:v], cols("lo_s", x), ["lo"], [K("e0")])
-        cp(T["eo%d" % x][:, 32:32 + v], tmp("tf", 3, x), [K("nv")], [K("en")])
-        ts(I(1), n, 1, None, ALU.arith_shift_right, None, ["nq"], [K("i1")])
-        tt(I(2), n, I(1), ALU.subtract, ["nq", K("i1")], [K("i2")])
-        ts(I(3), I(2), 1, None, ALU.arith_shift_right, None, [K("i2")], [K("i3")])
-        ts(R("mr", 4), I(1), -0.5, None, ALU.add, None, [K("i1")], [K("sb")])
-        ts(R("mo", 1), I(2), -0.5, None, ALU.add, None, [K("i2")], [K("a0")])
-        cp(R("mo", 3), I(3), [K("i3"), K("a0")], [K("mh")])
-        tt(tmp("tf", 2, x), I(2), I(1), ALU.subtract, [K("i1"), K("i2")], [K("ud")])
-        ts(R("xo", 3), tmp("tf", 2, x), -1.0, 0.5, ALU.mult, ALU.add, [K("ud")], [K("a2")])
-        ts(R("xo", 4), tmp("tf", 2, x), -0.5, None, ALU.add, None, [K("ud"), K("a2")], [K("sg")])
-        cp(R("do", 2), I(1), [K("i1")], [K("m")])
-        cp(blk("wt", x, 0, 1), I(1), [K("i1")], [K("w0")])
-        for p in range(4):
-            cp(blk("lo4", x, p, p + 1), cols("lo_s", x), ["lo"] + ([K("lo4")] if p else []), [K("lo4")])
-        pa, kb, _b = bank("pa")
-        mms([(pa[:, a // 4:4 * v:4, a % 4], fx(a), cols("nh", x), True, True) for a in range(16)], 16 * 64,
-            ["f%d" % a for a in range(16)] + ["nh"], [kb])
-        act(T["nw%d" % x][:, 0:16 * v], pa[:, 0:4 * v, :], ACT.Copy, [kb], [K("nw")], 16 * v)
-        node(x, 0)
+        c = 64 if x is not None else 128
+        mb, h, sb, xb, m, d = R("mo", 1), R("mo", 3), R("mr", 4), R("mr", 14), R("do", 2), tmp("ti", 0, x)
+        tt(d, R("xo", 4), mb, ALU.mult, [K("sg"), K("mh")], [K("d")], c)
+        tt(xb, mb, h, ALU.subtract, [K("mh")], [K("xb")], c)
+        tt(tmp("tf", 0, x), sb, h, ALU.subtract, [K("mh"), K("sb")], [K("t2l")], c)
+        tt(tmp("tf", 1, x), xb, h, ALU.subtract, [K("mh"), K("xb")], [K("t2w")], c)
+        tt(pair("sg", x, 0, 1), R("xo", 3), tmp("tf", 0, x), ALU.min, [K("sg"), K("t2l")], [K("sgl")], c)
+        tt(pair("sg", x, 1, 2), R("xo", 4), tmp("tf", 1, x), ALU.min, [K("sg"), K("t2w")], [K("sgw")], c)
+        tt(tmp("wt", 1, x), m, d, ALU.add, [K("m"), K("d")], [K("w1")], c)
+        tt(pair("d2", x, 0, 2), pair("sg", x, 0, 2), R("mr", 4, 2), ALU.mult, [K("sgl"), K("sgw"), K("sb"), K("xb")], [K("d2")], 2 * c)
+        tt(tmp("wt", 2, x), tmp("wt", 1, x), pair("d2", x, 1, 2), ALU.add, [K("w1"), K("d2")], [K("w2")], c)
+        tt(tmp("wt", 3, x), m, pair("d2", x, 0, 1), ALU.add, [K("m"), K("d2")], [K("w3")], c)
+
+    def columns(x, e):
+        K = keys(x)
+        for a, b in ([(0, 4)] if e == 0 else [(1, 2), (2, 4)] if EARLY else [(1, 4)]):
+            n = (b - a) * V
+            to, kb, c0 = (T.pp, "Pp", 0) if b == 4 else (T.ps, "Ps", 128)
+            mms([(to[:, c0 + p * V:c0 + p * V + V], (T.id64, T.ident)[k][:], tmp("lob", k, x), p + k == 0, False)
+                 for p in range(b - a) for k in range(2)], 128 * (b - a), ["lob0", "lob1", "id", "id64"], [kb])
+            mms([(to[:, c0:c0 + n], T.permh[:], places(x, a, b), False, True)], max(64, n), [K("w%d" % p) for p in range(a, b)] + ["permh"], [kb])
+            cp(T["off%d" % x][:, a * V:b * V], to[:, c0:c0 + n], [kb], [K("off%d" % p) for p in range(a, b)], n)
+
+    def rest(x, e):
+        K = keys(x)
+        R = lambda name, a, n=1: rec(name, x, a, n)
+        c = 64 if x is not None else 128
+        if e:
+            tt(tmp("tf", 4, x), R("so", 2), R("gr", 3), ALU.max, [K("so"), K("gm1")], [K("gm")])
+        tt(R("dr", 0), pair("d2", x, 1, 2), pair("d2", x, 0, 1), ALU.subtract, [K("d2")], [K("dd")], c)
+        cp(R("dr", 1), pair("d2", x, 0, 1), [K("d2")], [K("dl")])
+        if e < NE - 1:
+            tt(R("mr", 0), R("mr", 14), R("mr", 4), ALU.subtract, [K("xb"), K("sb")], [K("dm")], c)
+            act(R("mr", 16), R("mo", 3), ACT.Identity, [K("mh"), "half"], [K("hb")], bias=T.half[:, 0:1])
+
+    def start():
+        K = keys(None)
+        R = lambda name, a, n=1: rec(name, None, a, n)
+        n, s, h = T.pp[:, 0:64], T.ti[:, 1, :], T.ti[:, 2, :]
+        cp(T.nf[:], T.n_s[:], ["n"], ["nf"])
+        mms([(n, T.permt[:], T.nf[:], True, True)], 256, ["permt", "nf"], ["Pp"])
+        ts(s, n, 0.5, -0.25, ALU.mult, ALU.add, ["Pp"], ["s"])
+        ts(h, n, 0.25, -0.125, ALU.mult, ALU.add, ["Pp"], ["h"])
+        ts(T.tf[:, 2, :], s, 0.5, None, ALU.add, None, ["s"], [K("ud")])
+        tt(R("mo", 1), n, T.tf[:, 2, :], ALU.subtract, ["Pp", K("ud")], ["mb"])
+        cp(T.nh[:], n, ["Pp"], ["nh"])
+        cp(R("mo", 3), h, ["h", "mb"], [K("mh")])
+        tt(R("xo", 4), R("mo", 1), s, ALU.subtract, ["mb", "s"], ["sg4"], 128)
+        tt(R("xo", 3), s, R("mo", 1), ALU.subtract, ["mb", "s", "sg4"], [K("sg")], 128)
+        ts(R("mr", 4), s, -0.5, None, ALU.add, None, ["s"], [K("sb")])
+        cp(R("do", 2), s, ["s"], [K("m")])
+        cp(T.wt[:, 0, :], s, ["s"], [K("w0")])
+        ts(T.lo2[:, 0, :], T.lo_s[:], 6, None, ALU.arith_shift_right, None, ["lo"], ["lo2a"])
+        ts(T.lo2[:, 1, :], T.lo_s[:], 63, None, ALU.bitwise_and, None, ["lo"], ["lo2b"])
+        cp(T.lob[:], T.lo2[:], ["lo2a", "lo2b"], ["lob0", "lob1"], 128)
+        cp(T.eo[:, 0:64], T.lo_s[:], ["lo"], ["e0"])
+        tt(T.tf[:, 3, :], T.n_s[:], T.lo_s[:], ALU.add, ["n", "lo"], [K("nv")], 128)
+        cp(T.eo[:, 64:128], T.tf[:, 3, :], [K("nv")], ["en"])
+        node(None)
+        for x in range(2):
+            columns(x, 0)
+        for x in range(2):
+            pa, kb, _b = bank("pa")
+            mms([(pa[:, a // 4:128:4, a % 4], fx(a), cols("nh", x), True, True) for a in range(16)], 16 * 64, [kf, "nh"], [kb])
+            act(T["nw%d" % x][:], pa[:], ACT.Copy, [kb], ["nw.%d" % x], W)
+        rest(None, 0)
 
     def advance(x, e):
-        v = WID[x]
-        K = lambda n: "%s.%d" % (n, x)
+        K = keys(x)
         R = lambda name, a, n=1: rec(name, x, a, n)
-        i = NP * e + x
+        i = 2 * e + x
         p0 = 0 if e == 0 else 1
-        slot = lambda k, a, n: T.land[:, (3 * i + k) * 128 + a * 32:(3 * i + k) * 128 + a * 32 + n]
-        acc = lambda a, n: T.pp[:, 128 + a * 32:128 + a * 32 + n]
+        slot = lambda k, a, n: T.land[:, (3 * i + k) * 128 + a * V:(3 * i + k) * 128 + a * V + n]
+        acc = lambda a, n: T.pp[:, 128 + a * V:128 + a * V + n]
         gt = lambda a, n: T.gt[:, x * 64 + a:x * 64 + a + n]
-        gm, g1, g3 = tmp("tf", 4, x), gt(0, v), gt(32, v)
-        n = 128 - 32 * p0
-        mms([(acc(p0, n), T.idf[:], T.sendb[:, i * 128 + p0 * 32:(i + 1) * 128], True, False)], 4 * n, ["snd%d" % i, "idf"], ["Pp"])
+        gm, g1, g3 = tmp("tf", 4, x), gt(0, V), gt(V, V)
+        n = 128 - V * p0
+        mms([(acc(p0, n), T.idf[:], T.sendb[:, i * 128 + p0 * V:(i + 1) * 128], True, False)], 4 * n, ["snd%d" % i, "idf"], ["Pp"])
         mms([(acc(p0, n), T.idf[:], slot(0, p0, n), False, False)], 4 * n, ["arr%d.0" % i], ["Pp"])
         mms([(acc(p0, n), T.idf[:], slot(1, p0, n), False, True)], 4 * n, ["arr%d.1" % i], ["Pp"])
         if e == 0:
-            tt(gm, acc(0, v), slot(2, 0, v), ALU.add, ["Pp", "arr%d.2" % i], [K("gm")])
+            tt(gm, acc(0, V), slot(2, 0, V), ALU.add, ["Pp", "arr%d.2" % i], [K("gm")])
         tt(gt(0, 64), acc(1, 64), slot(2, 1, 64), ALU.add, ["Pp", "arr%d.2" % i], [K("G")])
-        tt(R("gr", 1), acc(3, v), slot(2, 3, v), ALU.add, ["Pp", "arr%d.2" % i], [K("G2")])
+        tt(R("gr", 1), acc(3, V), slot(2, 3, V), ALU.add, ["Pp", "arr%d.2" % i], [K("G2")])
         u1, u2, ud = R("ur", 20), R("ur", 40), tmp("tf", 2, x)
         tt(u1, g1, gm, ALU.is_gt, [K("G"), K("gm")], [K("u1")])
         tt(R("gr", 0), g3, R("gr", 1), ALU.subtract, [K("G"), K("G2")], [K("dg")])
         tt(R("gr", 3), g1, gm, ALU.max, [K("G"), K("gm")], [K("gm1")])
-        scan(R("so", 0, 4), R("ur", 5, 4), R("gr", 0, 4), ALU.subtract, [K("u1"), K("gm1"), K("dg"), K("G2")] + consts, [K("so")], 4 * v)
+        scan(R("so", 0, 4), R("ur", 5, 4), R("gr", 0, 4), ALU.subtract, [K("u1"), K("gm1"), K("dg"), K("G2"), consts], [K("so")], 4 * V)
         ts(u2, R("so", 3), 0.0, None, ALU.is_gt, None, [K("so")], [K("u2")])
         if e < NE - 1:
-            scan(R("ao", 0, 5), R("ur", 8, 5), R("mr", 0, 5), ALU.add, [K("u1"), K("dm"), K("sb"), K("hb")] + consts, [K("a1")], 5 * v)
+            scan(R("ao", 0, 5), R("ur", 8, 5), R("mr", 0, 5), ALU.add, [K("u1"), K("dm"), K("sb"), K("hb"), consts], [K("a1")], 5 * V)
             tt(R("mr", 11), R("ao", 1), R("ao", 4), ALU.subtract, [K("a1")], [K("y")])
-            scan(R("mo", 0, 4), R("ur", 25, 4), R("mr", 11, 4), ALU.add, [K("u2"), K("y"), K("hb")] + consts, [K("mh")], 4 * v)
+            scan(R("mo", 0, 4), R("ur", 25, 4), R("mr", 11, 4), ALU.add, [K("u2"), K("y"), K("hb"), consts], [K("mh")], 4 * V)
         tt(ud, u1, tmp("ti", 0, x), ALU.mult, [K("u1"), K("d")], [K("ud")])
         tt(R("dr", 2), R("do", 2), ud, ALU.add, [K("m"), K("ud")], [K("m1")])
         scan(R("do", 0, 3), R("ur", 0, 3), R("dr", 0, 3), ALU.add,
-             [K("u1"), K("u2"), K("dd"), K("dl"), K("m1")] + consts, [K("m"), K("d1")], 3 * v)
+             [K("u1"), K("u2"), K("dd"), K("dl"), K("m1"), consts], [K("m"), K("d1")], 3 * V)
         if e == NE - 1:
             tt(gm, R("so", 2), R("gr", 3), ALU.max, [K("so"), K("gm1")], [K("gm")])
-            mms([(T.pp[:, 0:v], T.permq[:], gm, True, True), (T.pp[:, v:2 * v], T.permq[:], R("do", 2), True, True)], 512,
+            mms([(T.pp[:, 0:V], T.permq[:], gm, True, True), (T.pp[:, V:2 * V], T.permq[:], R("do", 2), True, True)], 512,
                 [K("gm"), K("m"), "perm"], ["Pp"])
-            cp(T.ol[:, x * 64:x * 64 + 2 * v], T.pp[:, 0:2 * v], ["Pp"], [K("ol")])
+            cp(T.ol[:, x * 64:x * 64 + 64], T.pp[:, 0:64], ["Pp"], [K("ol")])
             return
-        if "nv" in ASIDE:
-            add("a", [lambda: g.scalar.activation(tmp("tf", 3, x), R("so", 3), ACT.Sign, T.pf[:, 8:9], -1.0)], 64 * CYC, [K("so"), "half2"], [K("nv")])
-        else:
-            ts(tmp("tf", 3, x), R("so", 3), 0.0, 0.5, ALU.is_le, ALU.subtract, [K("so")], [K("nv")])
-        less_half("sb", R("mr", 4), R("ao", 3), [K("a1")], [K("sb")])
+        act(tmp("tf", 3, x), R("so", 3), ACT.Sign, [K("so"), "half2"], [K("nv")], bias=T.half[:, 1:2], scale=-1.0)
+        act(R("mr", 4), R("ao", 3), ACT.Identity, [K("a1"), "half"], [K("sb")], bias=T.half[:, 0:1])
         tt(R("xb", 1), R("ao", 3), R("mo", 1), ALU.subtract, [K("a1"), K("mh")], [K("nt")])
         tt(R("xa", 1), R("do", 1), tmp("tf", 3, x), ALU.mult, [K("d1"), K("nv")], [K("q")])
-        scan(R("xo", 0, 5), R("xa", 0, 5), R("xb", 0, 5), ALU.max, [K("q"), K("nt")] + consts, [K("sg")], 5 * v)
-        node(x, e + 1)
-
-    def gather(off):
-        return T.win[:, 0:WC].indirect(off)
+        scan(R("xo", 0, 5), R("xa", 0, 5), R("xb", 0, 5), ALU.max, [K("q"), K("nt"), consts], [K("sg")], 5 * V)
+        node(x)
+        columns(x, e + 1)
 
     def rise(x):
-        v = WID[x]
-        s0, ri, eo = T["s0_%d" % x][:, 0:16 * v], T["ri%d" % x][:, 0:16 * v], T["eo%d" % x]
-        act(s0, gather(eo[:, 0:v]), ACT.Copy, ["win", "e0.%d" % x], ["s0.%d" % x], 16 * v * GAM + 64)
-        tt(ri, gather(eo[:, 32:32 + v]), s0, ALU.subtract, ["win", "en.%d" % x, "s0.%d" % x], ["ri.%d" % x], 16 * v * GAM + 64)
+        s0 = T["s0_%d" % x][:]
+        act(s0, gather(cols("eo", x)), ACT.Copy, ["win", "e0"], ["s0.%d" % x], GC)
+        tt(T["ri%d" % x][:, 0:W], gather(T.eo[:, 64 + x * V:64 + x * V + V]), s0, ALU.subtract, ["win", "en", "s0.%d" % x], ["ri.%d" % x], GC)
 
     def gains(x, e):
-        v = WID[x]
-        w = 16 * v
         p0 = 0 if e == 0 else 1
-        i = NP * e + x
-        K = lambda nm: "%s.%d" % (nm, x)
-        st, off, qb = T["st%d" % x], T["off%d" % x], T["qb%d" % x]
+        i = 2 * e + x
+        K = keys(x)
+        st, off, qb, ri, s0, nw = [T[n % x] for n in ("st%d", "off%d", "qb%d", "ri%d", "s0_%d", "nw%d")]
         for p in range(p0, 4):
-            args = (st[:, w * p:w * p + w], gather(off[:, p * v:p * v + v]))
+            to, src = st[:, W * p:W * p + W], gather(off[:, p * V:p * V + V])
             if (x, e, p) in VGATHER:
-                cp(args[0], args[1], ["win", K("off%d" % p)], [K("st%d" % p)], w * GAM + 64)
+                cp(to, src, ["win", K("off%d" % p)], [K("st%d" % p)], GC)
             else:
-                act(args[0], args[1], ACT.Copy, ["win", K("off%d" % p)], [K("st%d" % p)], w * GAM + 64)
-        for k in range(4):
-            pt, kt, _b = bank("pt")
-            mms([(pt[:, p0 * v:4 * v, c], fx(4 * c + k), blk("wt", x, p0, 4), True, True) for c in range(4)], 4 * max(64, (4 - p0) * v),
-                [K("w%d" % p) for p in range(p0, 4)] + ["f%d" % (4 * c + k) for c in range(4)], [kt])
-            for p in range(p0, 4):
-                tt(qb[:, w * p + k:w * p + w:4], pt[:, p * v:p * v + v, :], T["ri%d" % x][:, k:w:4], ALU.mult,
-                   [kt, K("ri")], [K("q%d.%d" % (p, k))], 4 * v)
-        parts = [(p, 0, v) for p in range(p0, 4)]
-        if SPLIT:
-            parts[-1:] = [(3, 0, v // 2), (3, v // 2, v)]
+                act(to, src, ACT.Copy, ["win", K("off%d" % p)], [K("st%d" % p)], GC)
+        for a, b in ([(1, 2), (2, 4)] if FIRST and e else [(p0, 4)]):
+            for k in range(4):
+                pt, kt, _b = bank("pt")
+                mms([(pt[:, a * V:b * V, c], fx(4 * c + k), places(x, a, b), True, True) for c in range(4)], 4 * max(64, (b - a) * V),
+                    [K("w%d" % p) for p in range(a, b)] + [kf], [kt])
+                for p, z in ([(a, b)] if e else [(p, p + 1) for p in range(a, b)]):
+                    tt(qb[:, W * p + k:W * z:4], pt[:, p * V:z * V, :], ri[:, k:W * (z - p):4], ALU.mult,
+                       [kt, K("ri")] + [K("ri%d" % r) for r in range(1, z - p)], [K("q%d.%d" % (r, k)) for r in range(p, z)], 4 * V * (z - p))
+        tsub = TSUB.get(i, [])
+        parts = [(p, 0, V) for p in range(p0, 4)]
+        if SPLIT and 3 not in tsub:
+            parts[-1:] = [(3, 0, V // 2), (3, V // 2, V)]
         held = {}
 
         def times_n(p, c0, c1):
             pb, kb, b = bank("pa" if c0 == 0 else "pt")
             held[p, c0] = (pb, kb)
             held.setdefault(p, b)
-            wide = pb[:, 0:4 * (c1 - c0), :]
-            mms([(wide, T.nident[:], T["s0_%d" % x][:, 16 * c0:16 * c1], True, False)], 16 * (c1 - c0), [K("s0"), "nid"], [kb])
-            mms([(wide, T.ident[:], st[:, w * p + 16 * c0:w * p + 16 * c1], False, True)], 16 * (c1 - c0), [K("st%d" % p), "id"], [kb])
-            for a in range(c0, c1, WG):
-                z = min(c1, a + WG)
-                cut = pb[:, 4 * (a - c0):4 * (z - c0), :]
-                tt(cut, cut, T["nw%d" % x][:, 16 * a:16 * z], ALU.mult, [kb, K("nw")], [K("nu%d.%d" % (p, a))], 16 * (z - a))
+            n = 16 * (c1 - c0)
+            wide = pb[:, 0:n // 4, :]
+            mms([(wide, T.nident[:], s0[:, 16 * c0:16 * c1], True, False)], n, [K("s0"), "nid"], [kb])
+            mms([(wide, T.ident[:], st[:, W * p + 16 * c0:W * p + 16 * c1], False, True)], n, [K("st%d" % p), "id"], [kb])
+            if p not in tsub:
+                tt(wide, wide, nw[:, 16 * c0:16 * c1], ALU.mult, [kb, K("nw")], [kb], n)
+                return
+            pd, kd, b = bank("pt")
+            held[p, c0] = (pd, kd)
+            mms([(pd[:], T.nident[:], s0[:], True, False)], W, [K("s0"), "nid"], [kd])
+            tt(pd[:], wide, nw[:], ALU.mult, [kb, kd, K("nw")], [kd], W)
 
         def sizes(p, c0, c1):
             (pb, kb), b, u = held[p, c0], held[p], c1 - c0
             ab = T["ab%d" % b]
-            for a in range(c0, c1, WG):
-                z = min(c1, a + WG)
-                cut = pb[:, 4 * (a - c0):4 * (z - c0), :]
-                tt(cut, cut, qb[:, w * p + 16 * a:w * p + 16 * z], ALU.subtract,
-                   [kb, K("nu%d.%d" % (p, a))] + [K("q%d.%d" % (p, k)) for k in range(4)], [K("df%d.%d" % (p, a))], 16 * (z - a))
+            if p in tsub:
+                for a in range(CUT):
+                    n = W // CUT
+                    mms([(pb[:, n // 4 * a:n // 4 * (a + 1), :], T.nidf[:], qb[:, W * p + n * a:W * p + n * (a + 1)], False, a == CUT - 1)], 4 * n,
+                        [K("q%d.%d" % (p, k)) for k in range(4)] + ["nidf", kb], [kb])
+            else:
+                wide = pb[:, 0:4 * u, :]
+                tt(wide, wide, qb[:, W * p + 16 * c0:W * p + 16 * c1], ALU.subtract, [kb] + [K("q%d.%d" % (p, k)) for k in range(4)], [kb], 16 * u)
             for c in range(4):
-                act(ab[:, 128 * c + 4 * c0:128 * c + 4 * c1], pb[:, c:4 * u:4, :], ACT.Abs,
-                    [kb, "abz%d" % b] + [K("df%d.%d" % (p, a)) for a in range(c0, c1, WG)],
-                    ["ab%d.%d.%d" % (b, c, h) for h in range(2) if (c1 == v if h else c0 == 0)], 4 * u)
-            if c1 == v:
-                mms([(T.ps[:, 32 * p + 8 * k:32 * p + 8 * k + 8], ab[:, k:512:4], T.bsel[:], True, True) for k in range(4)], 1024,
+                act(ab[:, 128 * c + 4 * c0:128 * c + 4 * c1], pb[:, c:4 * u:4, :], ACT.Abs, [kb],
+                    ["ab%d.%d.%d" % (b, c, h) for h in range(2) if (c1 == V if h else c0 == 0)], 4 * u)
+            if c1 == V:
+                mms([(T.ps[:, 32 * p + 8 * k:32 * p + 8 * k + 8], ab[:, k:W:4], T.bsel[:], True, True) for k in range(4)], 1024,
                     ["ab%d.%d.%d" % (b, c, h) for c in range(4) for h in range(2)] + ["bsel"], ["Ps"])
 
-        for k, part in enumerate(parts):
+        todo = []
+        for part in parts:
             times_n(*part)
-            if k:
-                sizes(*parts[k - 1])
-        sizes(*parts[-1])
-        src = T.sendb[:, i * 128 + p0 * 32:(i + 1) * 128]
-        add("v", [lambda: g.vector.transpose(src, T.ps[:, p0 * 32:128])], (128 - p0 * 32) * CYC, ["Ps"], ["snd%d" % i])
+            for old in [o for o in todo if o[0] not in tsub or parts.index(part) - parts.index(o) >= LAG][::-1]:
+                sizes(*old)
+                todo.remove(old)
+            todo.append(part)
+        for old in todo:
+            sizes(*old)
+        src = T.sendb[:, i * 128 + p0 * V:(i + 1) * 128]
+        add("v", [lambda: g.vector.transpose(src, T.ps[:, p0 * V:128])], (128 - p0 * V) * CYC, ["Ps"], ["snd%d" % i])
         ids, dsts = [], []
         for q in peers:
             rid, pid, _se = topo.addr(cores[q])
             k = (q - rank - 1) % nr
             ids.append(DstId(rid=rid, pnc=pid))
-            dsts.append(T.land[:, (3 * i + k) * 128 + p0 * 32:(3 * i + k + 1) * 128])
+            dsts.append(T.land[:, (3 * i + k) * 128 + p0 * V:(3 * i + k + 1) * 128])
         add("g", [lambda: g.remote_dma_fused(
             [RemoteDMATransfer(dst_ids=ids, dma_engine_mask=emask, remote_sem=T.sem["arr%d_%d" % (i, rank)], src=src, dsts=dsts)],
             local_sem=T.sem.sent)], 0.3, ["snd%d" % i], ["out%d" % i], 0.0, ("sent", 0))
         for k in range(nr - 1):
             add("x", [lambda: None], 0.0, ["out%d" % i], ["arr%d.%d" % (i, k)], LINK + STEP * (k - 2),
                 ("arr%d_%d" % (i, (rank - k - 1) % nr), neng))
-        rest(x, e)
+        if e:
+            rest(x, e)
+        else:
+            for r in range(1, 2 if FIRST else 3):
+                act(ri[:, r * W:r * W + W], ri[:, 0:W], ACT.Copy, [K("ri")], [K("ri%d" % r)], W)
 
-    for x in range(NP):
-        start(x)
-    for x in range(NP):
+    start()
+    for x in range(2):
         phase[0] = x - 0.5
         rise(x)
         phase[0] = x
         gains(x, 0)
     for e in range(1, NE):
-        for x in range(NP):
-            phase[0] = NP * e + x - AHEAD
+        for x in range(2):
+            phase[0] = 2 * e + x
             advance(x, e - 1)
-            phase[0] = NP * e + x
             gains(x, e)
-    for x in range(NP):
-        phase[0] = NP * NE + x
+    for x in range(2):
+        phase[0] = 2 * NE + x
         advance(x, NE - 1)
-        dma("a", g.scalar, cols("yg", x), T.ol[:, x * 64:x * 64 + WID[x]], "st_a", 16 * NP, 2.0, ["ol.%d" % x], [])
-        dma("s", g.sync, cols("ym", x), T.ol[:, x * 64 + WID[x]:x * 64 + 2 * WID[x]], "st_s", 16 * NP, 2.0, ["ol.%d" % x], [])
+        dma("a", g.scalar, cols("yg", x), T.ol[:, x * 64:x * 64 + V], "st_a", 32, 2.0, ["ol.%d" % x], [])
+        dma("s", g.sync, cols("ym", x), T.ol[:, x * 64 + V:x * 64 + 64], "st_s", 32, 2.0, ["ol.%d" % x], [])
 
     ns = len(steps)
     succ = [[] for _ in range(ns)]
@@ -457,7 +457,7 @@ def rank_program(g, core, T, topo):
             return 0.0
         return steps[j]["lat"] + (SAME if steps[j]["e"] == steps[i]["e"] else HOP)
 
-    cost = [s["cost"] for s in steps]
+    cost = [s["cost"] + (FIX * len(s["fns"]) if s["event"] is None else 0.0) for s in steps]
     into = [[(j, gap(j, i)) for j in steps[i]["deps"]] for i in range(ns)]
     outof = [[(j, gap(i, j)) for j in succ[i]] for i in range(ns)]
 
@@ -480,85 +480,95 @@ def rank_program(g, core, T, topo):
             at[i] = t
         return at
 
-    def greedy(way):
-        left = [len(s["deps"]) for s in steps]
-        can = [0.0] * ns
-        at = [0.0] * ns
-        ready = {e: [] for e in "vatgsx"}
-        free = {e: 0.0 for e in "vatgsx"}
-        for i in range(ns):
-            if left[i] == 0:
-                ready[steps[i]["e"]].append(i)
-        for _ in range(ns):
-            t0, e = min((max(free[e], min(can[i] for i in ready[e])), e) for e in ready if ready[e])
-            i = max([j for j in ready[e] if can[j] <= t0 + SLACK], key=lambda j: (-steps[j]["w"], way[j], -j))
-            ready[e].remove(i)
-            at[i] = max(t0, can[i])
-            free[e] = at[i] + cost[i]
-            for j, d in outof[i]:
-                can[j] = max(can[j], free[e] + d)
-                left[j] -= 1
-                if left[j] == 0:
-                    ready[steps[j]["e"]].append(j)
-        return at
-
     if not ORDER:
-        way = [0.0] * ns
-        for i in range(ns - 1, -1, -1):
-            way[i] = cost[i] + max([steps[i]["lat"]] + [d + way[j] for j, d in outof[i]])
-        left = [len(s["deps"]) for s in steps]
-        ready = [i for i in range(ns) if left[i] == 0]
-        seq = []
-        while ready:
-            i = min(ready, key=lambda j: (steps[j]["w"], j))
-            ready.remove(i)
-            seq.append(i)
-            for j in succ[i]:
-                left[j] -= 1
-                if left[j] == 0:
-                    ready.append(j)
-        at = greedy(way) if GREEDY else place(seq, False)
-        best = None
-        for _ in range(ROUNDS + 1):
-            end = max(at[i] + cost[i] + steps[i]["lat"] for i in range(ns))
-            if best is None or end < best[0]:
-                best = (end, at)
+        cases = []
+        for slow, late, wake, weight in CASES:
+            cases.append(([c * slow.get(s["e"], 1.0) if s["event"] is None else c for c, s in zip(cost, steps)],
+                          [[(j, d + (late if steps[j]["e"] == "x" else wake if d else 0.0)) for j, d in into[i]] for i in range(ns)], weight))
+        eng = [s["e"] for s in steps]
+
+        def worth(at):
+            seq = sorted(range(ns), key=lambda i: (at[i], i))
+            total = 0.0
+            for c, pre, weight in cases:
+                end = [0.0] * ns
+                free = {e: 0.0 for e in "vatgsx"}
+                for i in seq:
+                    t = free[eng[i]] if eng[i] != "x" else 0.0
+                    for j, d in pre[i]:
+                        if end[j] + d > t:
+                            t = end[j] + d
+                    end[i] = free[eng[i]] = t + c[i]
+                total += weight * max(end)
+            return total
+
+        def tighten(at):
             back = place(sorted(range(ns), key=lambda i: (-(at[i] + cost[i]), -i)), True)
-            at = place(sorted(range(ns), key=lambda i: (-(back[i] + cost[i]), i)), False)
-        ORDER.extend(sorted(range(ns), key=lambda i: (best[1][i], i)))
+            return place(sorted(range(ns), key=lambda i: (-(back[i] + cost[i]), i)), False)
+
+        seed = [1]
+
+        def draw():
+            seed[0] = seed[0] * 48271 % 2147483647
+            return seed[0] / 2147483647
+
+        at = tighten(place(sorted(range(ns), key=lambda i: (steps[i]["w"], i)), False))
+        best = worth(at)
+        for k in range(ROUNDS):
+            mid, wide, amp = max(at) * draw(), 1 + 5 * draw(), SHAKE[k % len(SHAKE)]
+            key = [a + amp * (draw() + draw() - 1) if abs(a - mid) < wide else a for a in at]
+            for i in range(ns):
+                for j, d in into[i]:
+                    key[i] = max(key[i], key[j] + 1e-6)
+            new = place(sorted(range(ns), key=lambda i: (key[i], i)), False)
+            if k % 2:
+                new = tighten(new)
+            val = worth(new)
+            if val <= best:
+                best, at = val, new
+        ORDER.extend(sorted(range(ns), key=lambda i: (at[i], i)))
     order = ORDER
 
     queue = {"v": g.vector, "a": g.scalar, "t": g.tensor, "g": g, "s": g.sync}
     semof = {"v": "cv", "a": "ca", "t": "ct", "g": "cg"}
+    mark = {}
+    seen = {e: {} for e in queue}
+    knows = {}
+    needs = {}
+    for n, i in enumerate(order):
+        e = steps[i]["e"]
+        mark[i] = steps[i]["event"] or (semof[e], n + 1)
+        if e == "x":
+            knows[i] = {}
+            continue
+        needs[i] = []
+        for j in sorted([j for j in steps[i]["deps"] if waits(j, i)], key=lambda j: -mark[j][1]):
+            if mark[j][1] > seen[e].get(mark[j][0], 0):
+                needs[i].append(j)
+                seen[e][mark[j][0]] = mark[j][1]
+                for sem, val in knows[j].items():
+                    seen[e][sem] = max(seen[e].get(sem, 0), val)
+        knows[i] = dict(seen[e])
+    awaited = set(j for i in needs for j in needs[i])
     count = {"v": 0, "a": 0, "t": 0, "g": 0}
-    known = {}
     done = {}
     for i in order:
         s = steps[i]
         e = s["e"]
-        if e == "x":
-            done[i] = s["event"]
-            continue
-        want = {}
-        for j in s["deps"]:
-            if waits(j, i):
-                sem, val = done[j]
-                want[sem] = max(want.get(sem, 0), val)
-        for sem, val in want.items():
-            if val > known.get((e, sem), 0):
-                queue[e].wait_ge(T.sem[sem], val)
-                known[(e, sem)] = val
+        for j in needs.get(i, []):
+            queue[e].wait_ge(T.sem[done[j][0]], done[j][1])
         if s["event"] is not None:
             s["fns"][0]()
             done[i] = s["event"]
-        else:
-            for fn in s["fns"]:
-                count[e] += 1
-                fn().then_inc(T.sem[semof[e]], 1)
+            continue
+        calls = [fn() for fn in s["fns"]]
+        if i in awaited:
+            count[e] += 1
+            calls[-1].then_inc(T.sem[semof[e]], 1)
             done[i] = (semof[e], count[e])
 
     for e in "vatg":
         g.wait_ge(T.sem[semof[e]], count[e])
-    g.wait_ge(T.sem.sent, neng * NP * NE)
-    g.wait_ge(T.sem.st_a, 16 * NP)
-    g.wait_ge(T.sem.st_s, 16 * NP)
+    g.wait_ge(T.sem.sent, neng * 2 * NE)
+    g.wait_ge(T.sem.st_a, 32)
+    g.wait_ge(T.sem.st_s, 32)

from concourse.bass import DstId, RemoteDMATransfer
from concourse.mybir import AluOpType as ALU, ActivationFunctionType as ACT

WC = 12288
V = 32
W = 16 * V
NE = 4
NPA = 3
NPT = 3
SPLIT = True
EARLY = True
FIRST = True
TSUB = {0: [0], 1: [0]}
CUT = 2
LAG = 1
VGATHER = [(0, 0, 0)]
CYC = 0.00083
PEC = 0.00042
GAM = 1.7
FIX = 0.012
LINK = 3.8
STEP = 0.5
HOP = 0.19
SAME = 0.2
LOAD = 5.5
ROUNDS = 3000
SHAKE = [0.25, 0.6, 1.4]
CASES = [({}, -0.8, 0.0, 1.0), ({}, 1.6, 0.0, 0.7), ({"t": 1.4}, -0.8, 0.08, 0.7), ({"v": 1.3, "a": 1.4}, -0.8, 0.0, 0.5)]
ORDER = []
MG = 12582912
REC = {"ur": 60, "gr": 4, "mr": 20, "so": 4, "ao": 5, "mo": 4, "dr": 3, "do": 3, "xa": 5, "xb": 5, "xo": 5}
FIXED = {"ur": {0: 0, 5: 0, 35: -1, 50: 1, 8: 0, 32: 0.5, 44: 1, 56: 1, 25: 0, 55: 0.5, 70: 1}, "gr": {2: 0},
         "mr": {8: MG, 12: -MG, 21: MG, 26: -MG}, "xa": {0: 0, 2: -1, 3: -1, 4: -1}, "xb": {0: 1, 2: -0.5, 3: -0.5, 4: -0.5}}

SCRATCH = {
    "win": ("sbuf", [128, WC], "bfloat16"),
    "lo_s": ("sbuf", [128, 64], "int32"),
    "n_s": ("sbuf", [128, 64], "int32"),
    "nf": ("sbuf", [128, 64], "float32"),
    "nh": ("sbuf", [128, 64], "float16"),
    "lo2": ("sbuf", [128, 2, 64], "int32"),
    "lob": ("sbuf", [128, 2, 64], "bfloat16"),
    "eo": ("sbuf", [128, 128], "uint16"),
    "ones": ("sbuf", [128, 128], "bfloat16"),
    "half": ("sbuf", [128, 2], "float32"),
    "ident": ("sbuf", [128, 128], "bfloat16"),
    "nident": ("sbuf", [128, 128], "bfloat16"),
    "id64": ("sbuf", [128, 128], "bfloat16"),
    "idf": ("sbuf", [128, 128], "float32"),
    "nidf": ("sbuf", [128, 128], "float32"),
    "permq": ("sbuf", [128, 128], "float32"),
    "permh": ("sbuf", [128, 128], "bfloat16"),
    "permt": ("sbuf", [128, 128], "float32"),
    "bsel1": ("sbuf", [128, 8], "float32"),
    "bsel": ("sbuf", [128, 8], "float32"),
    "fexp": ("sbuf", [128, 2048], "bfloat16"),
    "land": ("sbuf", [128, 2 * NE * 3 * 128], "float32"),
    "sendb": ("sbuf", [128, 2 * NE * 128], "float32"),
    "ol": ("sbuf", [128, 128], "float32"),
    "wt": ("sbuf", [128, 4, 64], "float16"),
    "gt": ("sbuf", [128, 128], "float32"),
    "d2": ("sbuf", [128, 64, 2], "int32"),
    "sg": ("sbuf", [128, 64, 2], "float32"),
    "ti": ("sbuf", [128, 3, 64], "int32"),
    "tf": ("sbuf", [128, 5, 64], "float32"),
    "ps": ("psum", [128, 512], "float32"),
    "pp": ("psum", [128, 512], "float32"),
}
for _n in REC:
    SCRATCH[_n] = ("sbuf", [128, 65 * REC[_n]], "float32")
for _k in range(NPT):
    SCRATCH["pt%d" % _k] = ("psum", [128, 128, 4], "float32")
for _k in range(NPA):
    SCRATCH["pa%d" % _k] = ("psum", [128, 128, 4], "float32")
    SCRATCH["ab%d" % _k] = ("sbuf", [128, W], "float32")
for _x in range(2):
    SCRATCH["nw%d" % _x] = ("sbuf", [128, W], "float32")
    SCRATCH["qb%d" % _x] = ("sbuf", [128, 4 * W], "float32")
    SCRATCH["st%d" % _x] = ("sbuf", [128, 4 * W], "bfloat16")
    SCRATCH["s0_%d" % _x] = ("sbuf", [128, W], "bfloat16")
    SCRATCH["ri%d" % _x] = ("sbuf", [128, 3 * W], "bfloat16")
    SCRATCH["off%d" % _x] = ("sbuf", [128, 128], "uint16")

SEMAPHORES = ["cv", "ca", "ct", "cg", "ld_lo", "ld_n", "ld_w", "sent", "st_s", "st_a"] + \
    ["arr%d_%d" % (_k, _r) for _k in range(2 * NE) for _r in range(4)]


def rank_program(g, core, T, topo):
    rank = T.rank_of(core)
    if rank is None:
        return
    cores = list(T.cores)
    nr = len(cores)
    peers = [(rank + k) % nr for k in range(1, nr)]
    emask = topo.mask(core, cores[peers[0]])
    for q in peers[1:]:
        emask = emask & topo.mask(core, cores[q])
    neng = bin(emask).count("1")

    steps = []
    lastw = {}
    readers = {}
    phase = [-1]

    def flat(keys):
        return [k for ks in keys for k in (ks if isinstance(ks, list) else [ks])]

    def add(e, fns, cost, reads, writes, lat=0.0, event=None, after=None):
        reads, writes = flat(reads), flat(writes)
        deps = {}
        for k in reads:
            if k in lastw:
                deps[lastw[k]] = True
            if k.startswith("P"):
                for j in readers.get(k, []):
                    if steps[j]["e"] != e:
                        deps.setdefault(j, False)
        for k in writes:
            if k in lastw:
                deps.setdefault(lastw[k], False)
            for j in readers.get(k, []):
                deps.setdefault(j, False)
        if after is not None:
            deps.setdefault(after, None)
        i = len(steps)
        steps.append({"e": e, "fns": fns, "cost": cost, "lat": lat, "event": event, "deps": deps, "w": phase[0]})
        for k in reads:
            readers.setdefault(k, []).append(i)
        for k in writes:
            lastw[k] = i
            readers[k] = []
        return i

    def tt(out, a, b, alu, reads, writes, n=64):
        add("v", [lambda: g.vector.tensor_tensor(out, a, b, alu)], max(64, n) * CYC, reads, writes)

    def ts(out, a, s1, s2, o0, o1, reads, writes, n=64):
        if o1 is None:
            add("v", [lambda: g.vector.tensor_scalar(out, a, s1, None, o0)], max(64, n) * CYC, reads, writes)
        else:
            add("v", [lambda: g.vector.tensor_scalar(out, a, s1, s2, o0, o1)], max(64, n) * CYC, reads, writes)

    def cp(out, a, reads, writes, n=64):
        add("v", [lambda: g.vector.tensor_copy(out, a)], max(64, n) * CYC, reads, writes)

    def scan(out, d0, d1, o1, reads, writes, n):
        add("v", [lambda: g.vector.tensor_tensor_scan(out, d0, d1, 0.0, ALU.mult, o1)], max(64, n) * CYC, reads, writes)

    def fill(ap, val, key):
        add("v", [lambda: g.vector.memset(ap, val)], 64 * CYC, [], [key])

    def act(out, a, f, reads, writes, n=64, bias=0.0, scale=1.0):
        add("a", [lambda: g.scalar.activation(out, a, f, bias, scale)], max(64, n) * CYC, reads, writes)

    def mms(calls, cyc, reads, writes):
        fns = [(lambda c=c: g.tensor.matmul(c[0], c[1], c[2], c[3], c[4])) for c in calls]
        add("t", fns, cyc * PEC, reads, writes)

    def dma(e, q, out, src, sem, val, lat, reads, writes, after=None):
        add(e, [lambda: q.dma_start(out, src).then_inc(T.sem[sem], 16)], 0.1, reads, writes, lat, (sem, val), after)

    def select(out, src, pattern, alu, base, step, reads, writes, n):
        add("g", [lambda: g.affine_select(out, src, pattern, alu, 0.0, base, step)], 0.17 + 2 * n * CYC, reads, writes)

    span = lambda x: (0, 64) if x is None else (x * V, x * V + V)

    def rec(name, x, a, n=1):
        c0, c1 = span(x)
        q = REC[name] // n
        b = c0 * REC[name] + a
        return T[name][:, b:b + ((c1 - c0) * n - 1) * q + 1:q]

    cols = lambda name, x: T[name][:, span(x)[0]:span(x)[1]]
    tmp = lambda name, k, x: T[name][:, k, span(x)[0]:span(x)[1]]
    pair = lambda name, x, a, b: T[name][:, span(x)[0]:span(x)[1], a:b]
    places = lambda x, a, b: T.wt[:, a:b, span(x)[0]:span(x)[1]]
    keys = lambda x: (lambda n: ["%s.%d" % (n, y) for y in range(2) if x in (None, y)])
    fx = lambda a: T.fexp[:, a * 128:(a + 1) * 128]
    gather = lambda off: T.win[:, 0:WC].indirect(off)
    GC = W * GAM + 64

    dma("a", g.scalar, T.n_s[:], T.span[:], "ld_n", 16, 2.0, [], ["n"])
    dma("s", g.sync, T.lo_s[:], T.lo[:], "ld_lo", 16, 2.0, [], ["lo"])
    dma("s", g.sync, T.win[:], T.walk[:], "ld_w", 16, LOAD, [], ["win"], len(steps) - 1)

    fill(T.ones[:], 1.0, "ones")
    fill(T.half[:, 0:1], -0.5, "half")
    fill(T.half[:, 1:2], 0.5, "half2")
    select(T.ident[:], T.ones[:], [[-1, 128]], ALU.is_equal, 0, 1, ["ones"], ["id"], 128)
    select(T.permt[:], T.ones[:], [[-1, 16], [-16, 8]], ALU.is_equal, 0, 1, ["ones"], ["permt"], 128)
    select(T.permh[:], T.ones[:], [[-1, 8], [-8, 16]], ALU.is_equal, 0, 1, ["ones"], ["permh"], 128)
    select(T.bsel1[:], T.ones[:, 0:8], [[-16, 8]], ALU.is_ge, 0, 1, ["ones"], ["bsel1"], 8)
    select(T.bsel[:], T.bsel1[:], [[16, 8]], ALU.is_ge, 15, -1, ["bsel1"], ["bsel"], 8)
    act(T.id64[:], T.ident[:], ACT.Copy, ["id"], ["id64"], 128, scale=64.0)
    act(T.nident[:], T.ident[:], ACT.Copy, ["id"], ["nid"], 128, scale=-1.0)
    for r in range(16):
        act(T.fexp[:, r:2048:16], T.ident[:], ACT.Copy, ["id"], ["f%d" % r], 128)
    kf = ["f%d" % r for r in range(16)]
    act(T.nidf[:], T.ident[:], ACT.Copy, ["id"], ["nidf"], 128, scale=-1.0)
    act(T.idf[:], T.ident[:], ACT.Copy, ["id"], ["idf"], 128)
    act(T.permq[:], T.permh[:], ACT.Copy, ["permh"], ["perm"], 128)
    consts = []
    for name in FIXED:
        for a, val in FIXED[name].items():
            ap = T[name][:, a:a + 63 * REC[name] + 1:REC[name]]
            consts.append("k%s%d" % (name, a))
            if val == int(val):
                add("g", [lambda ap=ap, val=val: g.iota(ap, [[0, 64]], val, 0, allow_small_or_imprecise_dtypes=True)],
                    0.13 + 128 * CYC, [], [consts[-1]])
            else:
                act(ap, T.ones[:, 0:64], ACT.Copy, ["ones"], [consts[-1]], scale=val)

    turn = {"pa": 0, "pt": 0}

    def bank(kind):
        k = turn[kind] % (NPA if kind == "pa" else NPT)
        turn[kind] += 1
        return T["%s%d" % (kind, k)], "P%s%d" % (kind[1], k), k

    def node(x):
        K = keys(x)
        R = lambda name, a, n=1: rec(name, x, a, n)
        c = 64 if x is not None else 128
        mb, h, sb, xb, m, d = R("mo", 1), R("mo", 3), R("mr", 4), R("mr", 14), R("do", 2), tmp("ti", 0, x)
        tt(d, R("xo", 4), mb, ALU.mult, [K("sg"), K("mh")], [K("d")], c)
        tt(xb, mb, h, ALU.subtract, [K("mh")], [K("xb")], c)
        tt(tmp("tf", 0, x), sb, h, ALU.subtract, [K("mh"), K("sb")], [K("t2l")], c)
        tt(tmp("tf", 1, x), xb, h, ALU.subtract, [K("mh"), K("xb")], [K("t2w")], c)
        tt(pair("sg", x, 0, 1), R("xo", 3), tmp("tf", 0, x), ALU.min, [K("sg"), K("t2l")], [K("sgl")], c)
        tt(pair("sg", x, 1, 2), R("xo", 4), tmp("tf", 1, x), ALU.min, [K("sg"), K("t2w")], [K("sgw")], c)
        tt(tmp("wt", 1, x), m, d, ALU.add, [K("m"), K("d")], [K("w1")], c)
        tt(pair("d2", x, 0, 2), pair("sg", x, 0, 2), R("mr", 4, 2), ALU.mult, [K("sgl"), K("sgw"), K("sb"), K("xb")], [K("d2")], 2 * c)
        tt(tmp("wt", 2, x), tmp("wt", 1, x), pair("d2", x, 1, 2), ALU.add, [K("w1"), K("d2")], [K("w2")], c)
        tt(tmp("wt", 3, x), m, pair("d2", x, 0, 1), ALU.add, [K("m"), K("d2")], [K("w3")], c)

    def columns(x, e):
        K = keys(x)
        for a, b in ([(0, 4)] if e == 0 else [(1, 2), (2, 4)] if EARLY else [(1, 4)]):
            n = (b - a) * V
            to, kb, c0 = (T.pp, "Pp", 0) if b == 4 else (T.ps, "Ps", 128)
            mms([(to[:, c0 + p * V:c0 + p * V + V], (T.id64, T.ident)[k][:], tmp("lob", k, x), p + k == 0, False)
                 for p in range(b - a) for k in range(2)], 128 * (b - a), ["lob0", "lob1", "id", "id64"], [kb])
            mms([(to[:, c0:c0 + n], T.permh[:], places(x, a, b), False, True)], max(64, n), [K("w%d" % p) for p in range(a, b)] + ["permh"], [kb])
            cp(T["off%d" % x][:, a * V:b * V], to[:, c0:c0 + n], [kb], [K("off%d" % p) for p in range(a, b)], n)

    def rest(x, e):
        K = keys(x)
        R = lambda name, a, n=1: rec(name, x, a, n)
        c = 64 if x is not None else 128
        if e:
            tt(tmp("tf", 4, x), R("so", 2), R("gr", 3), ALU.max, [K("so"), K("gm1")], [K("gm")])
        tt(R("dr", 0), pair("d2", x, 1, 2), pair("d2", x, 0, 1), ALU.subtract, [K("d2")], [K("dd")], c)
        cp(R("dr", 1), pair("d2", x, 0, 1), [K("d2")], [K("dl")])
        if e < NE - 1:
            tt(R("mr", 0), R("mr", 14), R("mr", 4), ALU.subtract, [K("xb"), K("sb")], [K("dm")], c)
            act(R("mr", 16), R("mo", 3), ACT.Identity, [K("mh"), "half"], [K("hb")], bias=T.half[:, 0:1])

    def start():
        K = keys(None)
        R = lambda name, a, n=1: rec(name, None, a, n)
        n, s, h = T.pp[:, 0:64], T.ti[:, 1, :], T.ti[:, 2, :]
        cp(T.nf[:], T.n_s[:], ["n"], ["nf"])
        mms([(n, T.permt[:], T.nf[:], True, True)], 256, ["permt", "nf"], ["Pp"])
        ts(s, n, 0.5, -0.25, ALU.mult, ALU.add, ["Pp"], ["s"])
        ts(h, n, 0.25, -0.125, ALU.mult, ALU.add, ["Pp"], ["h"])
        ts(T.tf[:, 2, :], s, 0.5, None, ALU.add, None, ["s"], [K("ud")])
        tt(R("mo", 1), n, T.tf[:, 2, :], ALU.subtract, ["Pp", K("ud")], ["mb"])
        cp(T.nh[:], n, ["Pp"], ["nh"])
        cp(R("mo", 3), h, ["h", "mb"], [K("mh")])
        tt(R("xo", 4), R("mo", 1), s, ALU.subtract, ["mb", "s"], ["sg4"], 128)
        tt(R("xo", 3), s, R("mo", 1), ALU.subtract, ["mb", "s", "sg4"], [K("sg")], 128)
        ts(R("mr", 4), s, -0.5, None, ALU.add, None, ["s"], [K("sb")])
        cp(R("do", 2), s, ["s"], [K("m")])
        cp(T.wt[:, 0, :], s, ["s"], [K("w0")])
        ts(T.lo2[:, 0, :], T.lo_s[:], 6, None, ALU.arith_shift_right, None, ["lo"], ["lo2a"])
        ts(T.lo2[:, 1, :], T.lo_s[:], 63, None, ALU.bitwise_and, None, ["lo"], ["lo2b"])
        cp(T.lob[:], T.lo2[:], ["lo2a", "lo2b"], ["lob0", "lob1"], 128)
        cp(T.eo[:, 0:64], T.lo_s[:], ["lo"], ["e0"])
        tt(T.tf[:, 3, :], T.n_s[:], T.lo_s[:], ALU.add, ["n", "lo"], [K("nv")], 128)
        cp(T.eo[:, 64:128], T.tf[:, 3, :], [K("nv")], ["en"])
        node(None)
        for x in range(2):
            columns(x, 0)
        for x in range(2):
            pa, kb, _b = bank("pa")
            mms([(pa[:, a // 4:128:4, a % 4], fx(a), cols("nh", x), True, True) for a in range(16)], 16 * 64, [kf, "nh"], [kb])
            act(T["nw%d" % x][:], pa[:], ACT.Copy, [kb], ["nw.%d" % x], W)
        rest(None, 0)

    def advance(x, e):
        K = keys(x)
        R = lambda name, a, n=1: rec(name, x, a, n)
        i = 2 * e + x
        p0 = 0 if e == 0 else 1
        slot = lambda k, a, n: T.land[:, (3 * i + k) * 128 + a * V:(3 * i + k) * 128 + a * V + n]
        acc = lambda a, n: T.pp[:, 128 + a * V:128 + a * V + n]
        gt = lambda a, n: T.gt[:, x * 64 + a:x * 64 + a + n]
        gm, g1, g3 = tmp("tf", 4, x), gt(0, V), gt(V, V)
        n = 128 - V * p0
        mms([(acc(p0, n), T.idf[:], T.sendb[:, i * 128 + p0 * V:(i + 1) * 128], True, False)], 4 * n, ["snd%d" % i, "idf"], ["Pp"])
        mms([(acc(p0, n), T.idf[:], slot(0, p0, n), False, False)], 4 * n, ["arr%d.0" % i], ["Pp"])
        mms([(acc(p0, n), T.idf[:], slot(1, p0, n), False, True)], 4 * n, ["arr%d.1" % i], ["Pp"])
        if e == 0:
            tt(gm, acc(0, V), slot(2, 0, V), ALU.add, ["Pp", "arr%d.2" % i], [K("gm")])
        tt(gt(0, 64), acc(1, 64), slot(2, 1, 64), ALU.add, ["Pp", "arr%d.2" % i], [K("G")])
        tt(R("gr", 1), acc(3, V), slot(2, 3, V), ALU.add, ["Pp", "arr%d.2" % i], [K("G2")])
        u1, u2, ud = R("ur", 20), R("ur", 40), tmp("tf", 2, x)
        tt(u1, g1, gm, ALU.is_gt, [K("G"), K("gm")], [K("u1")])
        tt(R("gr", 0), g3, R("gr", 1), ALU.subtract, [K("G"), K("G2")], [K("dg")])
        tt(R("gr", 3), g1, gm, ALU.max, [K("G"), K("gm")], [K("gm1")])
        scan(R("so", 0, 4), R("ur", 5, 4), R("gr", 0, 4), ALU.subtract, [K("u1"), K("gm1"), K("dg"), K("G2"), consts], [K("so")], 4 * V)
        ts(u2, R("so", 3), 0.0, None, ALU.is_gt, None, [K("so")], [K("u2")])
        if e < NE - 1:
            scan(R("ao", 0, 5), R("ur", 8, 5), R("mr", 0, 5), ALU.add, [K("u1"), K("dm"), K("sb"), K("hb"), consts], [K("a1")], 5 * V)
            tt(R("mr", 11), R("ao", 1), R("ao", 4), ALU.subtract, [K("a1")], [K("y")])
            scan(R("mo", 0, 4), R("ur", 25, 4), R("mr", 11, 4), ALU.add, [K("u2"), K("y"), K("hb"), consts], [K("mh")], 4 * V)
        tt(ud, u1, tmp("ti", 0, x), ALU.mult, [K("u1"), K("d")], [K("ud")])
        tt(R("dr", 2), R("do", 2), ud, ALU.add, [K("m"), K("ud")], [K("m1")])
        scan(R("do", 0, 3), R("ur", 0, 3), R("dr", 0, 3), ALU.add,
             [K("u1"), K("u2"), K("dd"), K("dl"), K("m1"), consts], [K("m"), K("d1")], 3 * V)
        if e == NE - 1:
            tt(gm, R("so", 2), R("gr", 3), ALU.max, [K("so"), K("gm1")], [K("gm")])
            mms([(T.pp[:, 0:V], T.permq[:], gm, True, True), (T.pp[:, V:2 * V], T.permq[:], R("do", 2), True, True)], 512,
                [K("gm"), K("m"), "perm"], ["Pp"])
            cp(T.ol[:, x * 64:x * 64 + 64], T.pp[:, 0:64], ["Pp"], [K("ol")])
            return
        act(tmp("tf", 3, x), R("so", 3), ACT.Sign, [K("so"), "half2"], [K("nv")], bias=T.half[:, 1:2], scale=-1.0)
        act(R("mr", 4), R("ao", 3), ACT.Identity, [K("a1"), "half"], [K("sb")], bias=T.half[:, 0:1])
        tt(R("xb", 1), R("ao", 3), R("mo", 1), ALU.subtract, [K("a1"), K("mh")], [K("nt")])
        tt(R("xa", 1), R("do", 1), tmp("tf", 3, x), ALU.mult, [K("d1"), K("nv")], [K("q")])
        scan(R("xo", 0, 5), R("xa", 0, 5), R("xb", 0, 5), ALU.max, [K("q"), K("nt"), consts], [K("sg")], 5 * V)
        node(x)
        columns(x, e + 1)

    def rise(x):
        s0 = T["s0_%d" % x][:]
        act(s0, gather(cols("eo", x)), ACT.Copy, ["win", "e0"], ["s0.%d" % x], GC)
        tt(T["ri%d" % x][:, 0:W], gather(T.eo[:, 64 + x * V:64 + x * V + V]), s0, ALU.subtract, ["win", "en", "s0.%d" % x], ["ri.%d" % x], GC)

    def gains(x, e):
        p0 = 0 if e == 0 else 1
        i = 2 * e + x
        K = keys(x)
        st, off, qb, ri, s0, nw = [T[n % x] for n in ("st%d", "off%d", "qb%d", "ri%d", "s0_%d", "nw%d")]
        for p in range(p0, 4):
            to, src = st[:, W * p:W * p + W], gather(off[:, p * V:p * V + V])
            if (x, e, p) in VGATHER:
                cp(to, src, ["win", K("off%d" % p)], [K("st%d" % p)], GC)
            else:
                act(to, src, ACT.Copy, ["win", K("off%d" % p)], [K("st%d" % p)], GC)
        for a, b in ([(1, 2), (2, 4)] if FIRST and e else [(p0, 4)]):
            for k in range(4):
                pt, kt, _b = bank("pt")
                mms([(pt[:, a * V:b * V, c], fx(4 * c + k), places(x, a, b), True, True) for c in range(4)], 4 * max(64, (b - a) * V),
                    [K("w%d" % p) for p in range(a, b)] + [kf], [kt])
                for p, z in ([(a, b)] if e else [(p, p + 1) for p in range(a, b)]):
                    tt(qb[:, W * p + k:W * z:4], pt[:, p * V:z * V, :], ri[:, k:W * (z - p):4], ALU.mult,
                       [kt, K("ri")] + [K("ri%d" % r) for r in range(1, z - p)], [K("q%d.%d" % (r, k)) for r in range(p, z)], 4 * V * (z - p))
        tsub = TSUB.get(i, [])
        parts = [(p, 0, V) for p in range(p0, 4)]
        if SPLIT and 3 not in tsub:
            parts[-1:] = [(3, 0, V // 2), (3, V // 2, V)]
        held = {}

        def times_n(p, c0, c1):
            pb, kb, b = bank("pa" if c0 == 0 else "pt")
            held[p, c0] = (pb, kb)
            held.setdefault(p, b)
            n = 16 * (c1 - c0)
            wide = pb[:, 0:n // 4, :]
            mms([(wide, T.nident[:], s0[:, 16 * c0:16 * c1], True, False)], n, [K("s0"), "nid"], [kb])
            mms([(wide, T.ident[:], st[:, W * p + 16 * c0:W * p + 16 * c1], False, True)], n, [K("st%d" % p), "id"], [kb])
            if p not in tsub:
                tt(wide, wide, nw[:, 16 * c0:16 * c1], ALU.mult, [kb, K("nw")], [kb], n)
                return
            pd, kd, b = bank("pt")
            held[p, c0] = (pd, kd)
            mms([(pd[:], T.nident[:], s0[:], True, False)], W, [K("s0"), "nid"], [kd])
            tt(pd[:], wide, nw[:], ALU.mult, [kb, kd, K("nw")], [kd], W)

        def sizes(p, c0, c1):
            (pb, kb), b, u = held[p, c0], held[p], c1 - c0
            ab = T["ab%d" % b]
            if p in tsub:
                for a in range(CUT):
                    n = W // CUT
                    mms([(pb[:, n // 4 * a:n // 4 * (a + 1), :], T.nidf[:], qb[:, W * p + n * a:W * p + n * (a + 1)], False, a == CUT - 1)], 4 * n,
                        [K("q%d.%d" % (p, k)) for k in range(4)] + ["nidf", kb], [kb])
            else:
                wide = pb[:, 0:4 * u, :]
                tt(wide, wide, qb[:, W * p + 16 * c0:W * p + 16 * c1], ALU.subtract, [kb] + [K("q%d.%d" % (p, k)) for k in range(4)], [kb], 16 * u)
            for c in range(4):
                act(ab[:, 128 * c + 4 * c0:128 * c + 4 * c1], pb[:, c:4 * u:4, :], ACT.Abs, [kb],
                    ["ab%d.%d.%d" % (b, c, h) for h in range(2) if (c1 == V if h else c0 == 0)], 4 * u)
            if c1 == V:
                mms([(T.ps[:, 32 * p + 8 * k:32 * p + 8 * k + 8], ab[:, k:W:4], T.bsel[:], True, True) for k in range(4)], 1024,
                    ["ab%d.%d.%d" % (b, c, h) for c in range(4) for h in range(2)] + ["bsel"], ["Ps"])

        todo = []
        for part in parts:
            times_n(*part)
            for old in [o for o in todo if o[0] not in tsub or parts.index(part) - parts.index(o) >= LAG][::-1]:
                sizes(*old)
                todo.remove(old)
            todo.append(part)
        for old in todo:
            sizes(*old)
        src = T.sendb[:, i * 128 + p0 * V:(i + 1) * 128]
        add("v", [lambda: g.vector.transpose(src, T.ps[:, p0 * V:128])], (128 - p0 * V) * CYC, ["Ps"], ["snd%d" % i])
        ids, dsts = [], []
        for q in peers:
            rid, pid, _se = topo.addr(cores[q])
            k = (q - rank - 1) % nr
            ids.append(DstId(rid=rid, pnc=pid))
            dsts.append(T.land[:, (3 * i + k) * 128 + p0 * V:(3 * i + k + 1) * 128])
        add("g", [lambda: g.remote_dma_fused(
            [RemoteDMATransfer(dst_ids=ids, dma_engine_mask=emask, remote_sem=T.sem["arr%d_%d" % (i, rank)], src=src, dsts=dsts)],
            local_sem=T.sem.sent)], 0.3, ["snd%d" % i], ["out%d" % i], 0.0, ("sent", 0))
        for k in range(nr - 1):
            add("x", [lambda: None], 0.0, ["out%d" % i], ["arr%d.%d" % (i, k)], LINK + STEP * (k - 2),
                ("arr%d_%d" % (i, (rank - k - 1) % nr), neng))
        if e:
            rest(x, e)
        else:
            for r in range(1, 2 if FIRST else 3):
                act(ri[:, r * W:r * W + W], ri[:, 0:W], ACT.Copy, [K("ri")], [K("ri%d" % r)], W)

    start()
    for x in range(2):
        phase[0] = x - 0.5
        rise(x)
        phase[0] = x
        gains(x, 0)
    for e in range(1, NE):
        for x in range(2):
            phase[0] = 2 * e + x
            advance(x, e - 1)
            gains(x, e)
    for x in range(2):
        phase[0] = 2 * NE + x
        advance(x, NE - 1)
        dma("a", g.scalar, cols("yg", x), T.ol[:, x * 64:x * 64 + V], "st_a", 32, 2.0, ["ol.%d" % x], [])
        dma("s", g.sync, cols("ym", x), T.ol[:, x * 64 + V:x * 64 + 64], "st_s", 32, 2.0, ["ol.%d" % x], [])

    ns = len(steps)
    succ = [[] for _ in range(ns)]
    for i, s in enumerate(steps):
        for j in s["deps"]:
            succ[j].append(i)

    def waits(j, i):
        raw = steps[i]["deps"][j]
        return not (raw is None or (steps[j]["e"] == steps[i]["e"] and steps[i]["e"] in "tva" and not raw))

    def gap(j, i):
        if not waits(j, i):
            return 0.0
        return steps[j]["lat"] + (SAME if steps[j]["e"] == steps[i]["e"] else HOP)

    cost = [s["cost"] + (FIX * len(s["fns"]) if s["event"] is None else 0.0) for s in steps]
    into = [[(j, gap(j, i)) for j in steps[i]["deps"]] for i in range(ns)]
    outof = [[(j, gap(i, j)) for j in succ[i]] for i in range(ns)]

    def place(seq, back):
        busy = {e: [] for e in "vatgsx"}
        at = [0.0] * ns
        for i in seq:
            c = cost[i]
            t = steps[i]["lat"] if back else 0.0
            for j, d in (outof[i] if back else into[i]):
                t = max(t, at[j] + cost[j] + d)
            line = busy[steps[i]["e"]]
            k = len(line)
            while k > 0 and line[k - 1][1] > t:
                k -= 1
            while k < len(line) and line[k][0] < t + c - 1e-9:
                t = max(t, line[k][1])
                k += 1
            line.insert(k, (t, t + c))
            at[i] = t
        return at

    if not ORDER:
        cases = []
        for slow, late, wake, weight in CASES:
            cases.append(([c * slow.get(s["e"], 1.0) if s["event"] is None else c for c, s in zip(cost, steps)],
                          [[(j, d + (late if steps[j]["e"] == "x" else wake if d else 0.0)) for j, d in into[i]] for i in range(ns)], weight))
        eng = [s["e"] for s in steps]

        def worth(at):
            seq = sorted(range(ns), key=lambda i: (at[i], i))
            total = 0.0
            for c, pre, weight in cases:
                end = [0.0] * ns
                free = {e: 0.0 for e in "vatgsx"}
                for i in seq:
                    t = free[eng[i]] if eng[i] != "x" else 0.0
                    for j, d in pre[i]:
                        if end[j] + d > t:
                            t = end[j] + d
                    end[i] = free[eng[i]] = t + c[i]
                total += weight * max(end)
            return total

        def tighten(at):
            back = place(sorted(range(ns), key=lambda i: (-(at[i] + cost[i]), -i)), True)
            return place(sorted(range(ns), key=lambda i: (-(back[i] + cost[i]), i)), False)

        seed = [1]

        def draw():
            seed[0] = seed[0] * 48271 % 2147483647
            return seed[0] / 2147483647

        at = tighten(place(sorted(range(ns), key=lambda i: (steps[i]["w"], i)), False))
        best = worth(at)
        for k in range(ROUNDS):
            mid, wide, amp = max(at) * draw(), 1 + 5 * draw(), SHAKE[k % len(SHAKE)]
            key = [a + amp * (draw() + draw() - 1) if abs(a - mid) < wide else a for a in at]
            for i in range(ns):
                for j, d in into[i]:
                    key[i] = max(key[i], key[j] + 1e-6)
            new = place(sorted(range(ns), key=lambda i: (key[i], i)), False)
            if k % 2:
                new = tighten(new)
            val = worth(new)
            if val <= best:
                best, at = val, new
        ORDER.extend(sorted(range(ns), key=lambda i: (at[i], i)))
    order = ORDER

    queue = {"v": g.vector, "a": g.scalar, "t": g.tensor, "g": g, "s": g.sync}
    semof = {"v": "cv", "a": "ca", "t": "ct", "g": "cg"}
    mark = {}
    seen = {e: {} for e in queue}
    knows = {}
    needs = {}
    for n, i in enumerate(order):
        e = steps[i]["e"]
        mark[i] = steps[i]["event"] or (semof[e], n + 1)
        if e == "x":
            knows[i] = {}
            continue
        needs[i] = []
        for j in sorted([j for j in steps[i]["deps"] if waits(j, i)], key=lambda j: -mark[j][1]):
            if mark[j][1] > seen[e].get(mark[j][0], 0):
                needs[i].append(j)
                seen[e][mark[j][0]] = mark[j][1]
                for sem, val in knows[j].items():
                    seen[e][sem] = max(seen[e].get(sem, 0), val)
        knows[i] = dict(seen[e])
    awaited = set(j for i in needs for j in needs[i])
    count = {"v": 0, "a": 0, "t": 0, "g": 0}
    done = {}
    for i in order:
        s = steps[i]
        e = s["e"]
        for j in needs.get(i, []):
            queue[e].wait_ge(T.sem[done[j][0]], done[j][1])
        if s["event"] is not None:
            s["fns"][0]()
            done[i] = s["event"]
            continue
        calls = [fn() for fn in s["fns"]]
        if i in awaited:
            count[e] += 1
            calls[-1].then_inc(T.sem[semof[e]], 1)
            done[i] = (semof[e], count[e])

    for e in "vatg":
        g.wait_ge(T.sem[semof[e]], count[e])
    g.wait_ge(T.sem.sent, neng * 2 * NE)
    g.wait_ge(T.sem.st_a, 32)
    g.wait_ge(T.sem.st_s, 32)
